import numpy as np, ml_dtypes
CORES = [25,29,65,69,153,157,193,197]
N = 8
BF = ml_dtypes.bfloat16
M, L, CAP, VI, ST = 2304, 208, 160, 3, 5
W = M + (VI - 1) * L
def weights(rng):
    w = rng.integers(0, 64, (N, 8, 16)); o = np.argsort(rng.random((N, 8, 16)), axis=-1)
    a = o[..., :1] == np.arange(16); b = o[..., 1:2] == np.arange(16)
    return np.where(a, 1, np.where(b, 16, w)), a[:, :, None], b[:, :, None]
def aim(v, w, a, b, t):
    v = np.where(a | b, 0, v); need = (t - np.sum(v * w[:, :, None], axis=-1)) & 63
    return v + a * (need & 15)[..., None] + b * (need >> 4)[..., None]
def shake(rng, v, k, top):
    return np.clip(v + np.floor((2 * k + 1) * rng.random(v.shape)).astype(np.int64) - k, 0, top)
def homes(rng, e):
    t = (64 * rng.random((N, 8, M)) ** e).astype(np.int64)
    t = (t * (2 * rng.integers(0, 32, (N, 8, 1)) + 1) + rng.integers(0, 64, (N, 8, 1))) & 63
    t[:, :, 1:65] = np.arange(64); return t
def points(rng, w, a, b, top):
    tree = homes(rng, rng.choice(np.array([1.0, 1.5, 2.0, 3.0]), (N, 8, 1)))
    mid = rng.integers(0, top + 1, (N, 8, 64, 16)); k = rng.integers(0, 9, (N, 8, M, 1)); k[:, :, 1:65] = 0
    v = shake(rng, np.take_along_axis(mid, tree[..., None], 2), k, top)
    far = rng.random((N, 8, M, 1)) < 0.3; far[:, :, 1:65] = False
    return tree, aim(np.where(far, rng.integers(0, top + 1, v.shape), v), w, a, b, tree)
def grow(v, tree):
    x = v.astype(np.int32); c = np.zeros(N * 8 * M * 16, np.int64)
    R, g, n = np.nonzero(np.broadcast_to(np.arange(M) > 64, (N, 8, M))); at = tree[R, g, n] + 1
    for _ in range(24):
        if len(n) == 0: break
        band = np.add.reduce(np.abs(x[R, g, n] - x[R, g, at]), axis=-1) >> 4
        key = ((R * 8 + g) * M + at) * 16 + band
        u, i = np.unique(key, return_index=True); c[u] = n[i]
        more = np.ones(len(n), bool); more[i] = False
        R, g, n, at = R[more], g[more], n[more], c[key[more]]
    return c.reshape(N, 8, M, 16)
def queries(rng, v, tree, w, a, b):
    o = rng.integers(1, M, (N, 8, VI * L)); k = rng.integers(0, 7, (N, 8, VI * L, 1))
    s = shake(rng, np.take_along_axis(v, o[..., None], 2), k, 15)
    s = np.where(rng.random((N, 8, VI * L, 1)) < 0.25, rng.integers(0, 16, s.shape), s)
    return aim(s, w, a, b, np.take_along_axis(tree, o, 2))
def radii(rng):
    z = (N, 8, VI * L)
    return np.where(rng.random(z) < 0.7, rng.integers(100, 256, z), rng.integers(0, 100, z))
def full(v):
    return np.ascontiguousarray(v.transpose(0, 1, 3, 2)).reshape(N, 128, -1)
def pack(v, c, s, w, r0, th):
    return {"pt": full(v).astype(np.float32).astype(BF), "ch": full(c).astype(np.int32), "q": full(s).astype(np.float32).astype(BF),
            "w": np.ascontiguousarray(w.reshape(N, 128, 1)).astype(np.int32), "r0": r0.astype(np.int32), "th": np.repeat(th, 16, axis=1)[..., None].astype(np.int32)}
def setup_inputs(rng):
    w, a, b = weights(rng); tree, v = points(rng, w, a, b, 15)
    return pack(v, grow(v, tree), queries(rng, v, tree, w, a, b), w, radii(rng), rng.integers(20, 60, (N, 8)))
def setup_inputs_room(rng):
    w, a, b = weights(rng); tree, v = points(rng, w, a, b, 10); z = (N, 8, VI * L)
    n = rng.choice(np.array([0, 1, CAP - 1, CAP, CAP + 1, L]), (N, 8)); n[0] = (CAP, CAP + 1, L, CAP - 1, 1, 0, CAP, CAP + 1); n[:, 2] = L
    n = np.concatenate([n[:, :, None], np.full((N, 8, VI - 1), L // 2)], axis=2)
    hot = (np.argsort(rng.random((N, 8, VI, L)), axis=-1) < n[..., None]).reshape(z)
    s = np.where(hot[..., None], rng.integers(12, 16, z + (16,)), queries(rng, v, tree, w, a, b))
    r0 = np.where(hot, rng.choice(np.array([20, 21, 255, 255, 255]), z), rng.integers(0, 20, z))
    return pack(v, grow(v, tree), s, w, r0, np.full((N, 8), 20))
def setup_inputs_knots(rng):
    w, a, b = weights(rng); v = rng.integers(0, 16, (N, 8, M, 16)); v[:, 1::2] = v[:, 1::2][:, :, rng.integers(0, 37, M)]
    dens = rng.choice(np.array([1.0, 0.6, 0.2]), (N, 8, 1, 1)); dens[:, 0] = 1.0; dens[:, 1] = 0.2; dens[:, 2] = 0.3
    c = np.where(rng.random((N, 8, M, 16)) < dens, rng.integers(1, M, (N, 8, M, 16)), 0)
    c[:, 3] = rng.choice(np.array([0, 1, 64, 65, M - 1]), (N, M, 16))
    c[:, 5] = np.where(rng.random((N, M, 16)) < 0.5, np.arange(M)[:, None], c[:, 5])
    x = rng.integers(1, M, (N, M, 2)); e = np.arange(16) - rng.integers(1, 6, (N, M, 1)); j = rng.choice(np.array([-1, 3, 4]), (N, M, 1))
    some = rng.random((N, M, 1)) < 0.4; some[:, 1:65] = True
    c[:, 6] = some * np.where((e >= 0) & (e < 3), x[:, :, :1], np.where(e == j, x[:, :, 1:], 0)); c[:, :, 0] = 0
    return pack(v, c, queries(rng, v, rng.integers(0, 64, (N, 8, M)), w, a, b), w, radii(rng), rng.integers(20, 80, (N, 8)))
def setup_inputs_ties(rng):
    w = rng.integers(0, 64, (N, 8, 16)); v = 4 * rng.integers(0, 4, (N, 8, M, 16)); tree = homes(rng, 1.0); z = (N, 8, VI * L)
    s = np.take_along_axis(v, rng.integers(1, M, z)[..., None], 2); s = np.where(rng.random(s.shape) < 0.3, 4 * rng.integers(0, 4, s.shape), s)
    s = np.where(rng.random(s.shape) < 0.01, 15, s); s[:, ::2, 1::2] = s[:, ::2, ::2]
    r0 = np.where(rng.random(z) < 0.4, 16 * rng.integers(3, 9, z) + rng.choice(np.array([-1, 1]), z), 4 * rng.integers(10, 40, z))
    return pack(v, grow(v, tree), s, w, r0, 4 * rng.integers(8, 15, (N, 8)))
def setup_inputs_ends(rng):
    w, a, b = weights(rng); tree, v = points(rng, w, a, b, 15); n = np.arange(L)
    v[:, 4, 65:65 + L] = rng.integers(0, 16, (N, L, 16)); tree[:, 4, 65:65 + L] = n & 63; v = aim(v, w, a, b, tree)
    s = queries(rng, v, tree, w, a, b); s[:, 4, :L] = v[:, 4, 65:65 + L]
    w[:, 1] = 0; w[:, 2] = 63; v[:, :, 1] = 0; v[:, :, 64] = 15; v[:, :, M - 1] = 15; v[:, 3, 1:65] = 0
    c = grow(v, tree); c[:, :, 1, 15] = M - 1; c[:, 3] = 0; c[:, 4, 65:] = 0; c[:, 4, 1 + (n & 63), 4 * (n >> 6) + 2] = 65 + n
    R = np.arange(N); z = 1 + ((15 * np.sum(w[:, 7], axis=-1)) & 63)
    v[R, 7, z] = 0; v[:, 7, 65] = 0; v[:, 7, 66] = 15
    c[R, 7, z] = 0; c[R, 7, z, 9] = 65; c[:, 7, 65] = 0; c[:, 7, 65, 4] = 66
    s[:, 1, ::3] = 15; s[:, 3, ::2] = 15; s[:, 3, 1::4] = rng.integers(14, 16, s[:, 3, 1::4].shape); s[:, 7, ::4] = 15
    s[:, :, 0] = 15; s[:, :, L - 1] = 0
    r0 = rng.choice(np.array([0, 1, 15, 16, 17, 120, 254, 255]), (N, 8, VI * L)); high = np.array([240, 241, 255])
    r0[:, 3, ::2] = rng.choice(high, r0[:, 3, ::2].shape); r0[:, 3, 1::4] = rng.choice(np.array([191, 192, 239, 240, 241, 255]), r0[:, 3, 1::4].shape)
    r0[:, 4, :L] = 255; r0[:, 7, ::4] = rng.choice(high, r0[:, 7, ::4].shape); r0[:, :, 0] = 255; r0[:, :, L - 1] = 255
    th = rng.choice(np.array([0, 1, 16, 30, 240]), (N, 8)); th[:, 0] = 0; th[:, 3] = np.array([0, 240, 241, 255])[R & 3]; th[:, 4] = 0; th[:, 5] = 255; th[:, 6] = 240
    return pack(v, c, s, w, r0, th)
def setup_inputs_spread(rng):
    w = rng.integers(0, 64, (N, 8, 16)); e = rng.choice(np.array([0.25, 0.5, 1.0, 2.0, 4.0]), (N, 8, 1, 16))
    v = (16 * rng.random((N, 8, M, 16)) ** e).astype(np.int64); s = (16 * rng.random((N, 8, VI * L, 16)) ** e).astype(np.int64)
    c = grow(v, homes(rng, 4.0)); c = np.where(rng.random(c.shape) < 0.1, rng.integers(0, M, c.shape), c); c[:, :, 0] = 0
    th = np.exp2(7 * rng.random((N, 8))).astype(np.int64); th[:, 0] = 8
    return pack(np.clip(v, 0, 15), c, np.clip(s, 0, 15), w, rng.integers(0, 256, (N, 8, VI * L)), th)
def check_inputs(d):
    bad = []
    for k in ("pt", "q"):
        x = np.asarray(d[k]).astype(np.float32)
        if not (np.all(x >= 0) and np.all(x <= 15) and np.all(x == np.floor(x))): bad.append("whole numbers from 0 to 15 in " + k)
    for k, hi in (("ch", M - 1), ("w", 63), ("r0", 255), ("th", 255)):
        if np.min(d[k]) < 0 or np.max(d[k]) > hi: bad.append("range of " + k)
    if np.any(np.asarray(d["ch"])[:, :, 0] != 0): bad.append("column 0 of ch")
    x = np.asarray(d["th"]).reshape(-1, 16)
    if np.any(x != x[:, :1]): bad.append("one threshold a group")
    return bad
def dist(u, v):
    return np.add.reduce(np.abs(u - v), axis=-1)
def inside(D, rho):
    i = np.arange(16); return (16 * i <= (D + rho)[..., None]) & (16 * i + 15 >= (D - rho)[..., None])
def at(k, i):
    return np.take_along_axis(k, i[..., None], -1)[..., 0]
def reference(pt, ch, q, w, r0, th):
    X = np.zeros((N, 8, W, 16), np.int32); X[:, :, :M] = pt.astype(np.float32).astype(np.int32).reshape(N, 8, 16, M).transpose(0, 1, 3, 2)
    C = np.zeros((N, 8, W, 16), np.int32); C[:, :, :M] = ch.reshape(N, 8, 16, M).transpose(0, 1, 3, 2)
    Q = np.ascontiguousarray(q.astype(np.float32).astype(np.int32).reshape(N, 8, 16, VI * L).transpose(0, 1, 3, 2))
    wt = w.astype(np.int32).reshape(N, 8, 1, 16); lim = th.reshape(N, 8, 16)[:, :, :1]
    a, b, ln = np.ogrid[0:N, 0:8, 0:L]; far_off = 1000
    yr, yb, yp, held = [], [], [], None
    for t in range(VI):
        v = np.array(Q[:, :, t * L:(t + 1) * L]); rho = np.array(r0[:, :, t * L:(t + 1) * L]).astype(np.int32); best = np.zeros((N, 8, L), np.int32)
        if held is not None:
            hv, hr, hb, sent, place = held; h = np.nonzero(sent); to = ((h[0] + 1) % N, h[1], place[h])
            v[to] = hv[h]; rho[to] = hr[h]; best[to] = hb[h]
        kid = np.zeros((N, 8, ST + 1, L, 16), np.int32); far = np.zeros((N, 8, ST + 1, L, 16), np.int32); own = np.zeros((N, 8, ST + 1, L), np.int32)
        lev = np.zeros((N, 8, L), np.int64); push = np.ones((N, 8, L), bool)
        m = 1 + (np.add.reduce(wt * v, axis=-1) & 63); D = dist(X[a, b, m], v)
        for s in range(ST + 1):
            if s > 0:
                k = kid[a, b, lev, ln]; f = far[a, b, lev, ln]; ok = (k > 0) & inside(own[a, b, lev, ln], rho)
                i = np.argmin(np.where(ok, f, far_off), axis=-1); push = np.any(ok, axis=-1)
                m = np.where(push, at(k, i), 0); D = np.where(push, at(f, i), far_off)
                h = np.nonzero(push); kid[h[0], h[1], lev[h], h[2], i[h]] = 0
                lev = np.where(push, lev + 1, np.maximum(lev - 1, 0))
            P = np.where(inside(D, rho) & push[..., None], C[a, b, m], 0)
            F = dist(X[a[..., None], b[..., None], P], v[:, :, :, None])
            h = np.nonzero(push); e = (h[0], h[1], lev[h], h[2])
            kid[e] = P[h]; far[e] = F[h]; own[e] = D[h]
            key = np.concatenate([D[..., None], np.where(P > 0, F, far_off)], axis=-1); node = np.concatenate([m[..., None], P], axis=-1)
            i = np.argmin(key, axis=-1); least = at(key, i); better = least < rho
            best = np.where(better, 4096 * a + at(node, i), best); rho = np.where(better, least, rho)
        yr.append(rho); yb.append(best)
        if t == VI - 1: break
        goes = rho >= lim; here = (best > 0) & (best >> 12 == a); node = np.where(here, best & 4095, 0); row = rho >> 4
        can = goes & here & (C[a, b, node, row] == 0)
        earlier = np.arange(L)[None, :] < np.arange(L)[:, None]
        win = can & ~np.any((node[:, :, :, None] == node[:, :, None, :]) & can[:, :, None, :] & earlier, axis=-1)
        X[:, :, M + t * L:M + (t + 1) * L] = v; h = np.nonzero(win); C[h[0], h[1], node[h], row[h]] = M + t * L + h[2]
        yp.append(np.where(win, node, 0))
        place = np.add.accumulate(goes.astype(np.int64), axis=2) - 1
        held = (v, rho, best, goes & (place < CAP), place)
    return {"yr": np.concatenate(yr, axis=2).astype(np.float32), "yb": np.concatenate(yb, axis=2).astype(np.float32), "yp": np.concatenate(yp, axis=2).astype(np.float32)}

@@ -1,0 +1,733 @@
+from concourse.mybir import AluOpType as OP, AxisListType, ActivationFunctionType as AF
+
+M, L, CAP, VI, ST = 2304, 208, 160, 3, 5
+W = M + (VI - 1) * L
+CW = W + L
+NL, K0 = (112, 96), (0, 112)
+TOP = 16777216
+CYC = 0.00095
+VS = {0: ((0, 36), (36, 72)), 1: ((0, 30), (30, 62))}
+SS = {0: ((72, 92), (92, 112)), 1: ((62, 78), (78, 96))}
+TRIES = [(0.2 * b, 0.3 * (s > 1), 1e-9, s) for b in range(20) for s in range(1, 30)]
+
+SCRATCH = {"PT": ("sbuf", [128, W], "bfloat16"), "QA": ("sbuf", [128, VI * L], "bfloat16"), "CH": ("sbuf", [128, CW], "float32"),
+           "CHI": ("sbuf", [128, CW], "int32"), "WI": ("sbuf", [128, 1], "int32"), "THI": ("sbuf", [128, 1], "int32"),
+           "Q16": ("sbuf", [128, 16 * L], "bfloat16"), "R0I": ("sbuf", [8, VI * L], "int32"),
+           "R0F": ("sbuf", [8, VI * L], "float32"), "YO": ("sbuf", [16, VI * L], "float32"), "YPO": ("sbuf", [8, 2 * L], "float32")}
+for _h in ("0", "1"):
+    SCRATCH["SEND" + _h] = ("sbuf", [128, 736], "bfloat16")
+    SCRATCH["LAND" + _h] = ("sbuf", [128, 2 * CAP], "bfloat16")
+    for _n in ("KEY", "ZB", "FB", "SP"):
+        SCRATCH[_n + _h] = ("psum", [128, 512], "float32")
+PSUMS = {n for n in SCRATCH if SCRATCH[n][0] == "psum"}
+SIZES = {n: (SCRATCH[n][1], SCRATCH[n][2]) for n in SCRATCH}
+POOL = {}
+
+
+def _pool(dtype, halves, **bufs):
+    big, at = "ALL" + dtype[0], 0
+    for two, group in ((False, bufs), (True, halves)):
+        for k in group:
+            for name in ([k + "_0", k + "_1"] if two else [k]):
+                POOL[name] = (big, at)
+                SIZES[name] = ([128, group[k]], dtype)
+                at += (group[k] + 15) // 16 * 16
+    SCRATCH[big] = ("sbuf", [128, at], dtype)
+
+
+_pool("bfloat16", dict(DT=1792, A0=112, ST=16, ST0=112, ST1=112, ST2=112, ST3=112, U=256, UF=256, UG=256, EA=128, EB=128, EC=128,
+                       ED=128, OL=128), THB=128, ONB=128, IB=128, I25=128, IN=128, R8=8, W8=8, ZC=896, TRI=128, TRP=112, MW=24,
+      LG=8 * L, FAR=16, ML=256, ML2=256, ML3=256, MG=L, MGN=L, EE=L, FM=CAP, QF1=L, QF2=L, XG0=512, XG1=512, QC1=L, QC2=L)
+_pool("float32", dict(PF=112, SC1=128, SC2=128, FS=128, FS2=128, NR=8, X=128, Y=128, LB=128, FC=8, FV=8, FX=8, R0S=24, KM0=128,
+                      KM1=128, KM2=128, KM3=128, PA=8, PB=8, PC=8), WF=1, THF=1, ONF=128, IF=128, ICOL=1, C4K=1, C4K1=1,
+      LMASK=128, CMASK=8, SEGR=128, KC=16, KC2=16, KJ=16, KN=L, TH=8, LD0=128, LF=128, LS=128, NB=16, S0=16, DA=16, DB=16,
+      DST=16, NOD=16, Z1=16, N1=16, B1=16, GMF=8, FARS=16, BST=16, OUTL=32, GG=L, BN=L, BX=L, LOF=16, HIF=16, GD=16, CAN=16,
+      DMIN=16, YPL=16, NF=16)
+_pool("int32", dict(SEL=8, ND=8, RBC=8, ROOT=8, BI=8), PI=2, RI=128, BCI=16, H=128, LW=128, LWL=16, SI=32, BEST=16, MI=256,
+      MCJ=256, NCI=16)
+_pool("uint16", dict(P16=112, LT=8), BCL=8, BCS=8, DL=14, NLT=14, DL2=14)
+SEMAPHORES = ["cv", "cs", "ct", "cg", "aq0", "aq1", "am0", "am1", "lq0", "lq1", "lm0", "lm1"] + ["d%d" % i for i in range(16)]
+PLAN = {}
+
+
+def hop_of(src, dst, cores, topo):
+    if topo.may_write(src, dst):
+        return dst
+    fit = [c for c in topo.cores_of(src) if c not in cores and topo.may_write(c, dst)]
+    return ([c for c in fit if topo.die(c) == topo.die(src)] or fit)[0]
+
+
+def some(engines):
+    return sum(1 << e for e in engines[:8])
+
+
+def rank_program(g, core, T, topo):
+    rank = T.rank_of(core)
+    cores = list(T.cores)
+    n = len(cores)
+    if rank is None:
+        for r in range(n):
+            src, dst = cores[r], cores[(r + 1) % n]
+            if hop_of(src, dst, cores, topo) == core:
+                rid, pid = topo.addr(dst, core)
+                for t in ("q0", "m0", "q1", "m1"):
+                    a = T["LAND" + t[1]][:, 0:CAP] if t[0] == "q" else T["LAND" + t[1]][:, CAP:2 * CAP]
+                    g.wait_ge(T.sem["a" + t], 8)
+                    g.remote_dma(a, a, T.sem["a" + t], T.sem["l" + t], pid, rid, some(topo.engines(core, dst)))
+                for t in ("q0", "m0", "q1", "m1"):
+                    g.wait_ge(T.sem["l" + t], 8)
+        return
+
+    ops, half, ndma, turn = [], [0], [0], [0]
+    QUE = {"v": g.vector, "s": g.scalar, "t": g.tensor, "g": g, "y": g.sync}
+    SEM = {"v": T.sem.cv, "s": T.sem.cs, "t": T.sem.ct, "g": T.sem.cg}
+
+    def A(name, c0=0, c1=None, st=1, p=(0, None)):
+        shp, (b, o) = SIZES[name][0], POOL.get(name, (name, 0))
+        c1 = shp[1] if c1 is None else c1
+        p1 = shp[0] if p[1] is None else p[1]
+        x = T[b][p[0]:p1, o + c0:o + c1:st] if st > 1 else T[b][p[0]:p1, o + c0:o + c1]
+        return (x, name, p[0], p1, c0, c1, st)
+
+    def ind(win, off):
+        return ("I", win, off)
+
+    def is_ind(x):
+        return isinstance(x[0], str)
+
+    def ap(x):
+        return x[1][0].indirect(x[2][0]) if is_ind(x) else x[0]
+
+    def size(x):
+        return 16 * (x[2][5] - x[2][4]) if is_ind(x) else (x[5] - x[4] + x[6] - 1) // x[6]
+
+    def cost(q, what, out, ins):
+        m = size(out)
+        if q == "v":
+            if is_ind(out):
+                return 0.05 + m * 3.5 * CYC
+            if any(is_ind(x) for x in ins):
+                return 0.05 + m * 1.5 * CYC
+            if what == "tt":
+                m *= 1 if any(x[1] in PSUMS for x in ins) else 2
+            elif what == "red":
+                m = size(ins[0])
+            elif what != "scan" and all(SIZES[x[1]][1] in ("bfloat16", "uint16") for x in [out] + list(ins)):
+                m *= 0.5
+            return max(64, m) * CYC
+        if q == "s":
+            return 0.065 + m * (1.5 if is_ind(ins[0]) else 1) * CYC
+        if q == "t":
+            return max(min(64, size(ins[0])), m) * 0.0007 * (4 if SIZES[ins[0][1]][1] == "float32" else 1)
+        return 0.15 + 2 * m * CYC
+
+    def op(q, fn, rd, wr, kind="c", sem=None, val=1, c=0.1):
+        R, Wr = [], []
+        for x in rd:
+            R += [x[1], x[2]] if is_ind(x) else [x]
+        for x in wr:
+            Wr.append(x[1] if is_ind(x) else x)
+            if is_ind(x):
+                R.append(x[2])
+        ops.append((q, fn, R, Wr, kind, sem, val, c, half[0]))
+
+    def call(q, what, fn, out, *ins):
+        op(q, fn, ins, [out], c=cost(q, what, out, ins))
+
+    def dma(q, out, in_, rd, wr):
+        s = T.sem["d%d" % ndma[0]]
+        ndma[0] += 1
+        op(q, lambda: QUE[q].dma_start(out, in_), rd, wr, "d", s, 16)
+
+    def load(q, name, src, a=0, b=None):
+        dma(q, A(name, a, b)[0], src, [], [A(name, a, b)])
+
+    def tt(out, a, b, o):
+        call("v", "tt", lambda: g.vector.tensor_tensor(ap(out), ap(a), ap(b), o), out, a, b)
+
+    def ts(out, a, s1, o0, s2=None, o1=None):
+        rd = [a] + [x for x in (s1, s2) if isinstance(x, tuple)]
+        v1, v2 = (ap(x) if isinstance(x, tuple) else x for x in (s1, s2))
+        more = () if o1 is None else (o1,)
+        op("v", lambda: g.vector.tensor_scalar(ap(out), ap(a), v1, v2, o0, *more), rd, [out], c=cost("v", "ts", out, [a]))
+
+    def cp(out, a):
+        call("v", "cp", lambda: g.vector.tensor_copy(ap(out), ap(a)), out, a)
+
+    def fill(out, c):
+        call("v", "fill", lambda: g.vector.memset(ap(out), c), out)
+
+    def scan(out, d0, d1, o0, o1):
+        call("v", "scan", lambda: g.vector.tensor_tensor_scan(ap(out), ap(d0), ap(d1), 0.0, o0, o1), out, d0, d1)
+
+    def least(out, a):
+        call("v", "red", lambda: g.vector.tensor_reduce(ap(out), ap(a), AxisListType.X, OP.min, apply_absolute_value=True), out, a)
+
+    def act(out, a, f, scale=1.0):
+        call("s", "", lambda: g.scalar.activation(ap(out), ap(a), f, scale=scale), out, a)
+
+    def mm(out, l, r, start=True, stop=True):
+        call("t", "", lambda: g.tensor.matmul(ap(out), ap(l), ap(r), start, stop), out, l, r)
+
+    def iota(out, pat, base, cm, small=False):
+        kw = {"allow_small_or_imprecise_dtypes": True} if small else {}
+        call("g", "", lambda: g.iota(ap(out), pat, base, cm, **kw), out)
+
+    def asel(out, a, pat, cmp, fillv, base, cm):
+        call("g", "", lambda: g.affine_select(ap(out), ap(a), pat, cmp, fillv, base, cm), out, a)
+
+    load("y", "WI", T.w[:])
+    load("y", "QA", T.q[:, 0:L], 0, L)
+    load("s", "R0I", T.r0[:])
+    load("s", "CHI", T.ch[:, 0:1152], 0, 1152)
+    load("y", "PT", T.pt[:], 0, M)
+    load("s", "CHI", T.ch[:, 1152:M], 1152, M)
+    load("y", "THI", T.th[:])
+    load("y", "QA", T.q[:, L:VI * L], L, VI * L)
+
+    fill(A("R8"), 65536.0)
+    fill(A("ONF"), 1.0)
+    fill(A("ONB"), 1.0)
+    fill(A("SEGR"), 0.0)
+    fill(A("ZC"), 0.0)
+    iota(A("PI", 0, 1), [[0, 1]], 0, 1)
+    iota(A("RI"), [[0, 8], [1, 16]], 0, 0)
+    asel(A("R8"), A("R8"), [[-16, 8]], OP.is_ge, 0.0, 0, 1)
+    asel(A("R8"), A("R8"), [[16, 8]], OP.is_ge, 0.0, 15, -1)
+    asel(A("CMASK"), A("ONF", 0, 8), [[-16, 8]], OP.is_ge, 0.0, 0, 1)
+    asel(A("CMASK"), A("CMASK"), [[16, 8]], OP.is_ge, 0.0, 15, -1)
+    iota(A("BCI", 0, 8), [[1, 8]], 0, 0)
+    iota(A("BCI", 8, 16), [[16, 8]], 15, 0)
+    asel(A("IF"), A("ONF"), [[-1, 128]], OP.is_equal, 0.0, 0, 1)
+    asel(A("IB"), A("ONB"), [[-1, 128]], OP.is_equal, 0.0, 0, 1)
+    Z = lambda b: A("ZC", b * 128, b * 128 + 128)
+    asel(Z(0), Z(0), [[-1, 8], [0, 16]], OP.not_equal, 1.0, 0, 1)
+    asel(Z(5), Z(5), [[-1, 8], [0, 16]], OP.not_equal, -1.0, -8, 1)
+    tt(Z(1), Z(5), Z(0), OP.subtract)
+    tt(Z(2), Z(5), Z(0), OP.add)
+    ts(Z(3), Z(0), -1.0, OP.mult)
+    cp(Z(4), Z(0))
+    cp(Z(6), Z(5))
+    for b, sgn, c in ((0, -16, -7.5), (1, 16, 0.0), (2, -16, -15.0)):
+        z = A("ZC", b * 128, b * 128 + 128, 1, (32, 34))
+        iota(z, [[0, 8], [sgn, 16]], 0, 0, True)
+        asel(z, z, [[0, 128]], OP.not_equal, c, -1, 1)
+    cp(A("ZC", 640, 896, 1, (32, 34)), A("ZC", 128, 384, 1, (32, 34)))
+    asel(A("SEGR"), A("SEGR"), [[0, 8], [1, 16]], OP.not_equal, float(TOP), 0, 0)
+    ts(A("PI", 1, 2), A("PI", 0, 1), 15, OP.bitwise_and)
+    cp(A("ICOL"), A("PI", 1, 2))
+    ts(A("C4K"), A("ICOL"), 4096.0, OP.mult)
+    ts(A("C4K1"), A("C4K"), 1.0, OP.add)
+    ts(A("LMASK"), A("RI"), A("ICOL"), OP.is_equal)
+    cp(A("BCL"), A("BCI", 0, 8))
+    cp(A("BCS"), A("BCI", 8, 16))
+    cp(A("WF"), A("WI"))
+    ts(A("W8"), A("R8"), 1.0 / 65536, OP.mult, A("WF"), OP.mult)
+    for h in ("_1", "_0"):
+        for nm in ("SC2", "NR", "Y", "FV", "KM0", "KM1", "KM2"):
+            fill(A(nm + h), 0.0)
+        fill(A("ND" + h), 0)
+        fill(A("BI" + h), 0)
+        for l in "0123":
+            fill(A("ST" + l + h), 0.0)
+            fill(A("ST" + l + h, 0, 112, 1, (32, 34)), 1.0)
+    fill(A("SI"), 0)
+    fill(A("H"), 0)
+    cp(A("H", 0, 128, 8), A("ONF", 0, 16))
+    for nm in ("NB", "DST", "S0", "DB", "FAR", "CAN", "DMIN"):
+        fill(A(nm), 0.0)
+    fill(A("PT", M, W), 0.0)
+    fill(A("CHI", M, CW), 0)
+    cp(A("R0F"), A("R0I"))
+    for h in (1, 0):
+        for t in range(VI):
+            a = t * L + K0[h]
+            mm(A("FB%d" % h, 8 * t, 8 * t + 8, 1, (0, NL[h])), A("R0F", a, a + NL[h]), A("IF", 0, 8, 1, (0, 8)))
+        ts(A("R0S_%d" % h, 0, 24, 1, (0, NL[h])), A("FB%d" % h, 0, 24, 1, (0, NL[h])), 65536.0, OP.mult)
+    ts(A("IN"), A("IB"), -1.0, OP.mult)
+    ts(A("I25"), A("IB"), 33554432.0, OP.mult)
+    fill(A("TRP"), 8192.0)
+    for nm in ("MW", "ML3"):
+        fill(A(nm), 0.0)
+    for nm in ("MI", "MCJ"):
+        fill(A(nm), 0)
+    cp(A("MI", 4, 256, 16), A("ONF", 0, 16))
+    for nm, j, v in (("ML3", 3, -1.0), ("ML3", 4, -64.0), ("MCJ", 1, 1.0), ("MCJ", 2, 64.0)):
+        ts(A(nm, j, 256, 16), A("ONF", 0, 16), v, OP.mult)
+    ts(A("GMF"), A("R8"), 1.0 / 65536, OP.mult)
+    for t in (0, 1):
+        fill(A("SEND%d" % t, 208, 368), -80.0)
+        fill(A("SEND%d" % t, 576, 736), 0.0)
+        ts(A("QF%d" % (t + 1)), A("QA", (t + 1) * L, (t + 2) * L), 64.0, OP.subtract)
+        cp(A("QC%d" % (t + 1), CAP, L), A("QA", (t + 1) * L + CAP, (t + 2) * L))
+    cp(A("THF"), A("THI"))
+    ts(A("THB"), A("ONB"), A("THF"), OP.mult)
+    asel(A("TRI"), A("ONB"), [[1, 128]], OP.is_ge, 0.0, -1, -1)
+    asel(A("TRI"), A("TRI"), [[1, 128]], OP.not_equal, -512.0, 0, -1)
+    asel(A("TRP"), A("TRP"), [[1, 112]], OP.is_ge, 0.0, 0, -1)
+    for c, j, v in ((0, 0, 65536.0), (8, 1, 1.0), (8, 2, 64.0), (8, 3, 4096.0), (16, 4, 1.0)):
+        asel(A("MW", c, c + 8), A("MW", c, c + 8), [[-16, 8]], OP.not_equal, v, -j, 1)
+    iota(A("KC"), [[112, 2], [0, 8]], 0, 1, True)
+    iota(A("KC2"), [[-112, 2], [0, 8]], 720, -1, True)
+    iota(A("KJ"), [[112, 2], [0, 8]], W, 1, True)
+    iota(A("KN"), [[1, L]], M, 0, True)
+    mm(A("FB1", 64, 72), A("THB"), A("R8"))
+    ts(A("TH"), A("FB1", 64, 72), 1.0 / 16, OP.mult)
+
+    def RW(nm, h, c0=0, c1=None, st=1):
+        return A(nm + str(h) if nm + str(h) in PSUMS else nm + "_" + str(h), c0, c1, st, (0, NL[h]))
+
+    HB = lambda nm, h, c0=0, c1=None, st=1: A(nm + "_" + str(h), c0, c1, st)
+    SI = lambda h, a, b: A("SI", 16 * h + a, 16 * h + b, 1, (0, NL[h]))
+    HI = lambda h, e: A("H", h * 64 + e, h * 64 + 64, 8, (0, NL[h]))
+    LAST = lambda nm, h: RW(nm, h, 15, 128, 16)
+    SEG = lambda h: A("SEGR", 0, 128, 1, (0, NL[h]))
+    EYE = lambda nm, k: A(nm, 0, k, 1, (0, k))
+    hc = lambda nm, h, r=None: A(nm, 8 * h, 8 * h + 8, 1, (0, NL[h] if r is None else r))
+
+    def to_list(win, h):
+        tt(HB("LB", h), ind(win, A("BCL")), A("LMASK"), OP.mult)
+        mm(A("KEY%d" % h, 128, 128 + NL[h] // 16), RW("LB", h), A("CMASK", 0, NL[h] // 16, 1, (0, NL[h])))
+
+    def list_copy(out, h, more=0.0):
+        ts(out, A("KEY%d" % h, 128, 128 + NL[h] // 16), more, OP.add)
+
+    def kids(h, more=0.0):
+        k = NL[h] // 16
+        list_copy(HB("LT", h, 0, k), h, more)
+        ts(HB("P16", h, 0, NL[h]), ind(A("CH"), HB("LT", h, 0, k)), A("C4K"), OP.subtract)
+        act(HB("PF", h, 0, NL[h]), ind(A("CH"), HB("LT", h, 0, k)), AF.Copy)
+
+    def masks(h, lev, want_y, fbs):
+        nl = NL[h]
+        stt = lambda l, k=34: A("ST%d_%d" % (min(l, 3), h), 0, nl, 1, (0, k))
+        mm(A("ZB%d" % h, 384, 384 + nl, 1, (0, 16)), RW("ST", h), EYE("IB", nl))
+        act(stt(lev, 16), A("ZB%d" % h, 384, 384 + nl, 1, (0, 16)), AF.Copy)
+        mm(RW("ZB", h, 0, 384), stt(lev), A("ZC", 0, 384, 1, (0, 34)))
+        act(RW("U", h), RW("ZB", h, 128, 384), AF.Relu, float(TOP))
+        if want_y:
+            act(RW("Y", h), RW("ZB", h, 0, 128), AF.Abs, 65536.0 * TOP)
+        for c, u, l, k, es in fbs:
+            mm(RW("FB", h, 128, 384), stt(l), A("ZC", 384, 640, 1, (0, 34)), True, False)
+            mm(RW("FB", h, 128, 384), stt(lev), A("ZC", 640, 896, 1, (0, 34)), False, True)
+            act(RW(u, h), RW("FB", h, 128, 384), AF.Relu, float(TOP))
+
+    def fallback(h, fbs):
+        for c, u, l, k, es in fbs:
+            o = RW("FB", h, c, c + 128)
+            mm(o, EYE("IF", NL[h]), RW(k, h), True, False)
+            for e in es:
+                mm(o, EYE("I25", NL[h]), RW(e, h), False, False)
+            mm(o, EYE("IB", NL[h]), RW(u, h, 0, 128), False, False)
+            mm(o, EYE("IB", NL[h]), RW(u, h, 128, 256), False, True)
+
+    def points_scalar(h, a, b):
+        z = turn[0] = 1 - turn[0]
+        w = 16 * (b - a)
+        x, o = A("XG%d" % z, 0, w), A("SP%d" % z, 0, w)
+        act(x, ind(A("PT"), HB("P16", h, a, b)), AF.Copy)
+        mm(o, A("IN"), A("Q16", 16 * (K0[h] + a), 16 * (K0[h] + b)), True, False)
+        mm(o, A("IB"), x, False, True)
+        act(HB("DT", h, 16 * a, 16 * b), o, AF.Abs)
+
+    def points_vector(h, a, b):
+        d = HB("DT", h, 16 * a, 16 * b)
+        tt(d, ind(A("PT"), HB("P16", h, a, b)), A("Q16", 16 * (K0[h] + a), 16 * (K0[h] + b)), OP.subtract)
+        act(d, d, AF.Abs)
+
+    def points(h):
+        for (a, b), (c, d) in zip(VS[h], SS[h]):
+            points_scalar(h, c, d)
+            points_vector(h, a, b)
+
+    def keys(h):
+        nl = NL[h]
+        o = RW("KEY", h, 0, 128)
+        mm(o, HB("PF", h, 0, nl), A("IF"), True, False)
+        mm(o, EYE("IB", nl), RW("U", h, 0, 128), False, False)
+        mm(o, EYE("IB", nl), RW("U", h, 128, 256), False, False)
+        for i in range(16):
+            mm(RW("KEY", h, i, 128, 16), HB("DT", h, i, 16 * nl, 16), A("R8"), False, i == 15)
+
+    FBS = {2: [(0, "UF", 0, "KM0", ("EA",))], 3: [(0, "UF", 1, "KM1", ("EB",))],
+           4: [(0, "UF", 2, "KM2", ("EC",)), (384, "UG", 0, "KM0", ("EA", "ED"))]}
+
+    def look(h, s):
+        scan(RW("SC1", h), SEG(h), RW("KEY", h, 0, 128), OP.max, OP.min)
+        t1, rho = HI(h, s + 1), SI(h, 8, 16)
+        tt(t1, LAST("SC1", h), RW("RBC", h) if s == 1 else rho, OP.min)
+        if s <= ST:
+            ts(RW("NR", h), t1, -float(TOP), OP.mult, -7.5 * 65536 * TOP, OP.add)
+        ts(rho, t1, 16711680, OP.bitwise_and)
+        if s == ST + 1:
+            return
+        tt(HB("X", h), ind(HB("NR", h), A("BCL")), HB("Y", h), OP.add)
+        km = "KM%d" % min(s - 1, 3)
+        tt(RW(km, h), RW("KEY", h, 0, 128), RW("X", h), OP.max)
+        scan(RW("SC2", h), SEG(h), RW(km, h), OP.max, OP.min)
+        if s >= 3:
+            scan(RW("FS", h), SEG(h), RW("FB", h, 0, 128), OP.max, OP.min)
+            fc = LAST("FS", h)
+            if s == 5:
+                scan(RW("FS2", h), SEG(h), RW("FB", h, 384, 512), OP.max, OP.min)
+                tt(RW("FX", h), RW("PA", h), RW("PB", h), OP.min)
+                tt(RW("FX", h), RW("FX", h), LAST("FS2", h), OP.max)
+                tt(RW("FC", h), RW("FX", h), fc, OP.min)
+                fc = RW("FC", h)
+            tt(RW("FV", h), fc, RW({3: "PA", 4: "PB", 5: "PC"}[s], h), OP.max)
+            tt(RW("SEL", h), LAST("SC2", h), RW("FV", h), OP.min)
+        else:
+            cp(RW("SEL", h), LAST("SC2", h))
+        ts(RW("ND", h), RW("SEL", h), 4095, OP.bitwise_and)
+        to_list(HB("ND", h), h)
+        ts(SI(h, 0, 8), RW("SEL", h), 33488896, OP.bitwise_and)
+        ts(RW("ST", h), SI(h, 0, 16), 1.0 / 65536, OP.mult)
+        masks(h, s, s < ST, FBS.get(s, []))
+        if s in (2, 3, 4):
+            ts(RW({2: "PA", 3: "PB", 4: "PC"}[s], h), RW("SEL", h), TOP, OP.is_lt, float(TOP), OP.mult)
+        if s <= 3:
+            tt(HB({1: "EA", 2: "EB", 3: "EC"}[s], h), ind(HB("SC2", h), A("BCS")), HB(km, h), OP.is_equal)
+        if s == 3:
+            tt(HB("ED", h), ind(HB("FV", h), A("BCL")), HB("KM0", h), OP.is_equal)
+
+    QN = ("QA", "QC1", "QC2")
+    nh = (112, CAP - 112)
+    for t in range(VI):
+        q = lambda a, b: A(QN[t], a, b)
+        if t:
+            ld, fq = "LAND%d" % (t - 1), "QF%d" % t
+            op("x", None, [], [A(ld, 0, CAP)], "x", T.sem["aq%d" % (t - 1)], 8)
+            op("x", None, [], [A(ld, CAP, 2 * CAP)], "x", T.sem["am%d" % (t - 1)], 8)
+            tt(A(fq, 0, CAP), A(fq, 0, CAP), A(ld, 0, CAP), OP.max)
+            ts(A("FM"), A(fq, 0, CAP), 0.0, OP.is_lt, 64.0, OP.mult)
+            tt(q(0, CAP), A("FM"), A(fq, 0, CAP), OP.add)
+        for h in (1, 0):
+            mm(RW("KEY", h, 136, 144), A(fq if t else "QA", K0[h], K0[h] + NL[h]), A("W8"))
+            if t:
+                mm(A("KEY%d" % h, 152, 176, 1, (0, nh[h])), A(ld, CAP + K0[h], CAP + K0[h] + nh[h]), A("MW"))
+        for h in (1, 0):
+            cp(RW("SEL", h), RW("KEY", h, 136, 144))
+            ts(RW("ND", h), RW("SEL", h), 63, OP.bitwise_and)
+            to_list(HB("ND", h), h)
+            ts(RW("ROOT", h), RW("ND", h), 1, OP.add)
+        for i in range(16):
+            if i < 10:
+                cp(A("Q16", i, 16 * L, 16), q(0, L))
+            else:
+                act(A("Q16", i, 16 * L, 16), q(0, L), AF.Copy)
+        for h in (1, 0):
+            cp(SI(h, 8, 16), RW("R0S", h, 8 * t, 8 * t + 8))
+            if t:
+                r = (0, nh[h])
+                k = lambda a: A("KEY%d" % h, a, a + 8, 1, r)
+                nf = hc("NF", h, nh[h])
+                ts(nf, k(168), 0.0, OP.is_equal)
+                tt(nf, nf, A("R0S_%d" % h, 8 * t, 8 * t + 8, 1, r), OP.mult)
+                tt(A("SI", 16 * h + 8, 16 * h + 16, 1, r), k(152), nf, OP.add)
+                ts(hc("NB", h, nh[h]), k(160), -1.0, OP.mult)
+        if t == 0:
+            for a, b in ((0, 1152), (1152, CW)):
+                ts(A("CH", a, b), A("CHI", a, b), A("C4K"), OP.add)
+            fill(A("PT", 0, 1), 256.0)
+        for h in (1, 0):
+            k = NL[h] // 16
+            kids(h, 1.0)
+            a0 = HB("A0", h, 0, NL[h])
+            tt(a0, ind(A("PT"), HB("LT", h, 0, k)), q(K0[h], K0[h] + NL[h]), OP.subtract)
+            act(a0, a0, AF.Abs)
+            mm(RW("KEY", h, 144, 152), a0, A("R8"))
+        for h in (1, 0):
+            cp(SI(h, 0, 8), RW("KEY", h, 144, 152))
+            ts(RW("ST", h), SI(h, 0, 16), 1.0 / 65536, OP.mult)
+            masks(h, 0, True, [])
+            tt(RW("SEL", h), SI(h, 0, 8), SI(h, 8, 16), OP.is_lt)
+            tt(RW("RBC", h), SI(h, 0, 8), SI(h, 8, 16), OP.min)
+            tt(HI(h, 1), RW("SEL", h), RW("ROOT", h), OP.mult)
+        for h in (1, 0):
+            points(h)
+            keys(h)
+        for s in range(1, ST + 2):
+            for h in (1, 0):
+                half[0] = h
+                look(h, s)
+            if s <= ST:
+                for h in (1, 0):
+                    half[0] = h
+                    kids(h)
+                    points(h)
+                    keys(h)
+                    fallback(h, FBS.get(s, []))
+        half[0] = 0
+
+        last = t == VI - 1
+        both = lambda nm: A(nm, 0, 16)
+        if not last:
+            for h in (1, 0):
+                tt(hc("FAR", h), HI(h, 7), A("TH", 0, 8, 1, (0, NL[h])), OP.is_ge)
+            mm(RW("FB", 0, 0, 8), EYE("TRI", 112), hc("FAR", 0))
+            mm(RW("FB", 1, 0, 8), EYE("TRI", 96), hc("FAR", 1), True, False)
+            mm(RW("FB", 1, 0, 8), A("ONB", 0, 96, 1, (0, 112)), hc("FAR", 0), False, True)
+            for h in (1, 0):
+                ts(hc("S0", h), RW("FB", h, 0, 8), float(CAP - 512), OP.is_lt)
+                tt(hc("DB", h), RW("FB", h, 0, 8), hc("KC2", h), OP.add)
+            tt(both("DB"), both("DB"), both("S0"), OP.mult)
+            tt(both("DST"), both("KC"), both("DB"), OP.add)
+            for h in (1, 0):
+                to_list(A("DST", 8 * h, 8 * h + 8), h)
+        ts(both("LWL"), A("H", 7, 128, 8), 4095, OP.bitwise_and)
+        ts(A("LW"), A("H"), 4095, OP.bitwise_and)
+        ts(A("LD0"), A("LW"), 0, OP.is_equal)
+        cp(A("LF"), A("LW"))
+        cp(A("LF", 0, 128, 8), both("NB"))
+        scan(A("LS"), A("LD0"), A("LF"), OP.mult, OP.add)
+        res = A("LS", 6, 128, 8)
+        ts(both("N1"), res, 0.0, OP.max)
+        ts(both("B1"), res, 0.0, OP.is_gt, 4096.0 * rank, OP.mult)
+        tt(both("B1"), both("B1"), both("N1"), OP.add)
+        tt(both("B1"), both("B1"), both("N1"), OP.add)
+        tt(both("B1"), both("B1"), res, OP.subtract)
+        ts(both("Z1"), both("LWL"), 0, OP.is_equal)
+        tt(both("N1"), both("N1"), both("Z1"), OP.mult)
+        tt(both("NOD"), both("N1"), both("LWL"), OP.add)
+        tt(both("B1"), both("B1"), both("Z1"), OP.mult)
+        ts(both("Z1"), both("Z1"), -4096.0 * rank, OP.mult, 4096.0 * rank, OP.add)
+        tt(both("B1"), both("B1"), both("LWL"), OP.add)
+        tt(both("BST"), both("B1"), both("Z1"), OP.add)
+        if not last:
+            for h in (1, 0):
+                list_copy(A("DL", 7 * h, 7 * h + NL[h] // 16), h)
+            w1, w2 = (ind(A("SEND%d" % t, a, a + 368), A("DL", 0, 13)) for a in (0, 368))
+            cp(w1, q(0, L))
+            for h in (1, 0):
+                ts(A("MI", 128 * h, 128 * h + 128, 16, (0, NL[h])), SI(h, 8, 16), 16, OP.logical_shift_right)
+            cp(both("BEST"), both("BST"))
+            ts(A("MI", 1, 256, 16), both("BEST"), 63, OP.bitwise_and)
+            ts(A("MI", 2, 256, 16), both("BEST"), 6, OP.logical_shift_right, 63, OP.bitwise_and)
+            ts(A("MI", 3, 256, 16), both("BEST"), 12, OP.logical_shift_right)
+            cp(A("ML"), A("MI"))
+
+            def to_gp(z="ZB0", ml="ML"):
+                for h in (1, 0):
+                    mm(A(z, K0[h], K0[h] + NL[h]), A(ml, 128 * h, 128 * h + 128, 1, (0, NL[h])), EYE("IB", NL[h]))
+            to_gp()
+            act(A("MG"), A("ZB0", 0, L), AF.Copy)
+            cp(w2, A("MG"))
+            dst = cores[(rank + 1) % n]
+            hop = hop_of(core, dst, cores, topo)
+            rid, pid = topo.addr(hop, core)
+            m = some(topo.engines(core, hop))
+
+            def send(x, a, b):
+                s, d = A("SEND%d" % t, a, a + CAP), A("LAND%d" % t, b, b + CAP)
+                ra, rl = T.sem["a%s%d" % (x, t)], T.sem["l%s%d" % (x, t)]
+                op("g", lambda: g.remote_dma(d[0], s[0], ra, rl, pid, rid, m), [s], [], "r", rl, 8, 1.0)
+            send("q", 208, 0)
+            send("m", 576, CAP)
+        for h in (1, 0):
+            ts(A("OUTL", 16 * h, 16 * h + 8, 1, (0, NL[h])), SI(h, 8, 16), 1.0 / 65536, OP.mult)
+            cp(A("OUTL", 16 * h + 8, 16 * h + 16, 1, (0, NL[h])), hc("BST", h))
+            mm(A("ZB1", K0[h], K0[h] + NL[h], 1, (0, 16)), A("OUTL", 16 * h, 16 * h + 16, 1, (0, NL[h])), EYE("IF", NL[h]))
+        yo = A("YO", t * L, t * L + L)
+        act(yo, A("ZB1", 0, L, 1, (0, 16)), AF.Copy)
+        dma("y", T.yr[:, t * L:t * L + L], A("YO", t * L, t * L + L, 1, (0, 8))[0], [yo], [])
+        dma("y", T.yb[:, t * L:t * L + L], A("YO", t * L, t * L + L, 1, (8, 16))[0], [yo], [])
+        if last:
+            break
+        for h in (1, 0):
+            to_list(A("NOD", 8 * h, 8 * h + 8), h)
+        cp(A("PT", M + t * L, M + t * L + L), q(0, L))
+        for h in (1, 0):
+            list_copy(A("NLT", 7 * h, 7 * h + NL[h] // 16), h)
+        act(A("GG"), ind(A("CH"), A("NLT", 0, 13)), AF.Copy)
+        for h in (1, 0):
+            ts(RW("BI", h), HI(h, 7), 20, OP.logical_shift_right)
+            tt(HB("OL", h), ind(HB("BI", h), A("BCL")), A("RI"), OP.is_equal)
+            mm(A("ZB0", 256 + K0[h], 256 + K0[h] + NL[h]), RW("OL", h), EYE("IB", NL[h]))
+        ob = A("ZB0", 256, 256 + L)
+        ts(A("BN"), A("KN"), float(t * L), OP.add)
+        tt(A("BN"), A("BN"), ob, OP.mult)
+        ts(A("BX"), ob, A("C4K1"), OP.mult, -1.0, OP.add)
+        tt(A("EE"), A("GG"), A("BX"), OP.is_equal)
+        for h in (1, 0):
+            mm(RW("SP", h, 0, 8), A("EE", K0[h], K0[h] + NL[h]), A("R8"))
+        cp(both("NCI"), both("NOD"))
+        ts(A("MCJ", 3, 256, 16), both("NCI"), 63, OP.bitwise_and)
+        ts(A("MCJ", 4, 256, 16), both("NCI"), 6, OP.logical_shift_right)
+        cp(A("ML2"), A("MCJ"))
+        to_gp("ZB1", "ML2")
+        act(A("MGN"), A("ZB1", 0, L), AF.Copy)
+        ts(both("FARS"), both("FAR"), 1.0 / 65536, OP.mult)
+        tt(both("LOF"), A("MCJ", 3, 256, 16), both("FARS"), OP.mult)
+        tt(both("HIF"), A("MCJ", 4, 256, 16), both("FARS"), OP.mult)
+        tt(both("YPL"), both("FARS"), both("NOD"), OP.mult)
+        for h in (1, 0):
+            for j, nm in ((1, "LOF"), (2, "HIF")):
+                tt(A("ML3", 128 * h + j, 128 * h + 128, 16, (0, NL[h])), RW("SP", h, 0, 8), hc(nm, h), OP.mult)
+        to_gp("ZB0", "ML3")
+        act(A("MG"), A("ZB0", 0, L), AF.Copy)
+        for h in (1, 0):
+            cp(hc("CAN", h), RW("SP", h, 0, 8))
+        tt(both("YPL"), both("YPL"), both("CAN"), OP.mult)
+        ts(both("DA"), both("YPL"), 0.0, OP.is_gt)
+        tt(both("DA"), both("DA"), both("KJ"), OP.mult)
+        tt(both("GD"), both("YPL"), both("DA"), OP.subtract)
+        banks, z = ("FB0", "FB1", "ZB0", "ZB1"), 0
+        for gr in range(8):
+            lg = gr * L
+            ts(A("LG", lg, lg + L), A("MGN"), A("GMF", gr, gr + 1), OP.mult)
+            for h in (1, 0):
+                nl, w = NL[h], K0[h] + NL[h]
+                o = A(banks[z % 4], 0, w, 1, (0, nl))
+                z += 1
+                mm(o, A("LG", lg + K0[h], lg + w), A("MG", 0, w), True, False)
+                mm(A(o[1], K0[h], w, 1, (0, nl)), EYE("IB", nl), A("TRP", 0, nl, 1, (0, nl)), False, True)
+                least(A("DMIN", 8 * h + gr, 8 * h + gr + 1, 1, (0, nl)), o)
+        ts(both("DMIN"), both("DMIN"), 0.0, OP.is_gt)
+        tt(both("GD"), both("GD"), both("DMIN"), OP.mult)
+        tt(both("DST"), both("KJ"), both("GD"), OP.add)
+        tt(both("YPL"), both("YPL"), both("DMIN"), OP.mult)
+        for h in (1, 0):
+            to_list(A("DST", 8 * h, 8 * h + 8), h)
+        for h in (1, 0):
+            list_copy(A("DL2", 7 * h, 7 * h + NL[h] // 16), h)
+        tt(ind(A("CH"), A("DL2", 0, 13)), A("GG"), A("BN"), OP.add)
+        for h in (1, 0):
+            mm(A("ZB1", K0[h], K0[h] + NL[h], 1, (0, 8)), hc("YPL", h), EYE("IF", NL[h]))
+        yo = A("YPO", t * L, t * L + L)
+        act(yo, A("ZB1", 0, L, 1, (0, 8)), AF.Copy)
+        dma("y", T.yp[:, t * L:t * L + L], yo[0], [yo], [])
+
+    if not PLAN:
+        PLAN.update(plan(ops))
+    emit(g, ops, QUE, SEM)
+
+
+def plan(ops):
+    def meets(a, b):
+        if a[2] >= b[3] or b[2] >= a[3] or a[4] >= b[5] or b[4] >= a[5]:
+            return False
+        return not (a[6] == b[6] and a[6] > 1 and (a[4] - b[4]) % a[6] != 0)
+
+    N = len(ops)
+    tag = [o[0] if o[4] == "c" else "a%d" % i for i, o in enumerate(ops)]
+    hist, deps, sent, pool = {}, [], [], []
+    for i in range(N):
+        R, Wr, kind, dep = ops[i][2], ops[i][3], ops[i][4], set()
+        for lst, w in ((R, False), (Wr, True)):
+            for r in lst:
+                ps = r[1] in PSUMS
+                for (j, rr, ww) in hist.get(r[1], []):
+                    if j != i and ((ps and (tag[j] != tag[i] or w or ww)) or ((w or ww) and meets(r, rr))):
+                        dep.add(j)
+        if tag[i] == "g":
+            dep.update(pool[-1:])
+            pool.append(i)
+        if kind == "x":
+            dep.add(sent[-2 if ops[i - 1][4] != "x" else -1])
+        if kind == "r":
+            sent.append(i)
+        deps.append(dep)
+        for lst, w in ((R, False), (Wr, True)):
+            for r in lst:
+                h = hist.setdefault(r[1], [])
+                if w and r[1] in PSUMS:
+                    h[:] = []
+                elif w and r[6] == 1:
+                    h[:] = [e for e in h if not (r[2] <= e[1][2] and e[1][3] <= r[3] and r[4] <= e[1][4] and e[1][5] <= r[5])]
+                h.append((i, r, w))
+    after = [{"c": 0.18, "d": 2.2, "r": 6.0, "x": 0.1}[o[4]] for o in ops]
+    nxt = [[] for _ in range(N)]
+    for i in range(N):
+        for j in deps[i]:
+            nxt[j].append((i, tag[i] == tag[j] == "t"))
+    way = [0.0] * N
+    for i in range(N - 1, -1, -1):
+        way[i] = ops[i][7] + after[i] + max([way[k] for k, st in nxt[i]] or [0.0])
+    best = None
+    for bias, noise, hold, seed in TRIES:
+        order, when, end = in_time(ops, deps, nxt, after, way, bias, noise, hold, seed)
+        if best is None or end < best[0]:
+            best = (end, order, when)
+    order, when = best[1], best[2]
+    seq, num = {q: 0 for q in "vstg"}, [1] * N
+    known = {q: {} for q in "vstgyx"}
+    snap, need, waits = [None] * N, set(), [None] * N
+    for i in order:
+        q = ops[i][0]
+        if ops[i][4] == "c":
+            seq[q] += 1
+            num[i] = seq[q]
+        k, mine, last = known[q], [], {}
+        for j in deps[i]:
+            if ops[i][4] == "x" or tag[j] == tag[i] == "t":
+                continue
+            if tag[j] not in last or num[last[tag[j]]] < num[j]:
+                last[tag[j]] = j
+        for j in sorted(last.values(), key=lambda j: -when[j]):
+            if k.get(tag[j], 0) >= num[j]:
+                continue
+            mine.append(j)
+            need.add(j)
+            for a, b in snap[j].items():
+                if k.get(a, 0) < b:
+                    k[a] = b
+        waits[i] = mine
+        snap[i] = dict(k)
+        snap[i][tag[i]] = num[i]
+    return {"order": order, "waits": waits, "need": need}
+
+
+def in_time(ops, deps, nxt, after, way, bias, noise, hold, seed):
+    N = len(ops)
+    left = [len(d) for d in deps]
+    when = [0.0] * N
+    free = {q: 0.0 for q in "vstgyx"}
+    ready = {q: [i for i in range(N) if ops[i][0] == q and left[i] == 0] for q in free}
+    z, pr = seed, []
+    for i in range(N):
+        z = (1103515245 * z + 12345) % 2147483648
+        pr.append(way[i] + bias * ops[i][8] + noise * z / 2147483648.0)
+    order = []
+    while len(order) < N:
+        best = None
+        for q in free:
+            if ready[q]:
+                t = max(free[q], min(when[i] for i in ready[q]))
+                if best is None or t < best[0]:
+                    best = (t, q)
+        t, q = best
+        i = max((i for i in ready[q] if when[i] <= t + hold), key=lambda k: (pr[k], -k))
+        ready[q].remove(i)
+        free[q] = max(t, when[i]) + ops[i][7]
+        end = free[q] + after[i]
+        order.append(i)
+        for k, st in nxt[i]:
+            left[k] -= 1
+            when[k] = max(when[k], free[q] if st else end)
+            if left[k] == 0:
+                ready[ops[k][0]].append(k)
+    return order, when, max(free.values())
+
+
+def emit(g, ops, QUE, SEM):
+    cnt, at = {q: 0 for q in "vstg"}, {}
+    for i in PLAN["order"]:
+        q, fn, R, Wr, kind, sem, val = ops[i][:7]
+        if kind == "x":
+            continue
+        for j in PLAN["waits"][i]:
+            s, v = at[j] if j in at else (ops[j][5], ops[j][6])
+            QUE[q].wait_ge(s, v)
+        inst = fn()
+        if kind == "d":
+            inst.then_inc(sem, val)
+        elif kind == "c" and i in PLAN["need"]:
+            cnt[q] += 1
+            inst.then_inc(SEM[q], 1)
+            at[i] = (SEM[q], cnt[q])
+    for q in cnt:
+        if cnt[q]:
+            g.wait_ge(SEM[q], cnt[q])
+    for o in ops:
+        if o[4] in ("d", "r", "x"):
+            g.wait_ge(o[5], o[6])

@@ -4,19 +4,26 @@ M, L, CAP, VI, ST = 2304, 208, 160, 3, 5
 W = M + (VI - 1) * L
 CW = W + L
 NL, K0 = (112, 96), (0, 112)
-TOP = 16777216
-CYC = 0.00095
-VS = {0: ((0, 36), (36, 72)), 1: ((0, 30), (30, 62))}
-SS = {0: ((72, 92), (92, 112)), 1: ((62, 78), (78, 96))}
-TRIES = [(0.2 * b, 0.3 * (s > 1), 1e-9, s) for b in range(20) for s in range(1, 30)]
+MID = 1360
+BIG = float(2 ** 30)
+U = float(2 ** 18)
+RC = 7.5 + 1.0 / 256
+C0 = RC * 65536
+NONE = -(4096.0 - MID / 4096.0)
+CYC, TCY = 0.00095, 0.0006
+VS = {0: ((0, 24), (24, 48)), 1: ((0, 20), (20, 40))}
+SS = {0: ((48, 70), (70, 92), (92, 112)), 1: ((40, 60), (60, 78), (78, 96))}
+TRIES = [(0.4 * b, 0.3 * (s > 1), 1e-9, s) for b in range(12) for s in range(1, 13)]
 
-SCRATCH = {"PT": ("sbuf", [128, W], "bfloat16"), "QA": ("sbuf", [128, VI * L], "bfloat16"), "CH": ("sbuf", [128, CW], "float32"),
-           "CHI": ("sbuf", [128, CW], "int32"), "WI": ("sbuf", [128, 1], "int32"), "THI": ("sbuf", [128, 1], "int32"),
-           "Q16": ("sbuf", [128, 16 * L], "bfloat16"), "R0I": ("sbuf", [8, VI * L], "int32"),
-           "R0F": ("sbuf", [8, VI * L], "float32"), "YO": ("sbuf", [16, VI * L], "float32"), "YPO": ("sbuf", [8, 2 * L], "float32")}
+SCRATCH = {"PT": ("sbuf", [128, W], "bfloat16"), "QA": ("sbuf", [128, VI * L], "bfloat16"), "CH": ("sbuf", [128, CW], "int32"),
+           "WI": ("sbuf", [128, 1], "int32"), "THI": ("sbuf", [128, 1], "int32"), "R0I": ("sbuf", [8, VI * L], "int32"),
+           "R0F": ("sbuf", [8, VI * L], "float32"), "YO": ("sbuf", [8, 2 * VI * L], "float32"),
+           "YPO": ("sbuf", [8, 2 * L], "float32")}
 for _h in ("0", "1"):
-    SCRATCH["SEND" + _h] = ("sbuf", [128, 736], "bfloat16")
-    SCRATCH["LAND" + _h] = ("sbuf", [128, 2 * CAP], "bfloat16")
+    SCRATCH["SQ" + _h] = ("sbuf", [128, 2 * L], "bfloat16")
+    SCRATCH["SM" + _h] = ("sbuf", [128, 2 * L], "float32")
+    SCRATCH["LQ" + _h] = ("sbuf", [128, CAP], "bfloat16")
+    SCRATCH["LM" + _h] = ("sbuf", [128, CAP], "float32")
     for _n in ("KEY", "ZB", "FB", "SP"):
         SCRATCH[_n + _h] = ("psum", [128, 512], "float32")
 PSUMS = {n for n in SCRATCH if SCRATCH[n][0] == "psum"}
@@ -24,29 +31,34 @@ SIZES = {n: (SCRATCH[n][1], SCRATCH[n][2]) for n in SCRATCH}
 POOL = {}
 
 
-def _pool(dtype, halves, **bufs):
-    big, at = "ALL" + dtype[0], 0
-    for two, group in ((False, bufs), (True, halves)):
-        for k in group:
-            for name in ([k + "_0", k + "_1"] if two else [k]):
-                POOL[name] = (big, at)
-                SIZES[name] = ([128, group[k]], dtype)
-                at += (group[k] + 15) // 16 * 16
+def _pool(big, dtype, halves, **bufs):
+    at = 0
+    for k in bufs:
+        POOL[k] = (big, at)
+        SIZES[k] = ([128, bufs[k]], dtype)
+        at += (bufs[k] + 15) // 16 * 16
+    for k in halves:
+        for name in (k + "_0", k + "_1"):
+            POOL[name] = (big, at)
+            SIZES[name] = ([128, halves[k]], dtype)
+            at += (halves[k] + 15) // 16 * 16
     SCRATCH[big] = ("sbuf", [128, at], dtype)
 
 
-_pool("bfloat16", dict(DT=1792, A0=112, ST=16, ST0=112, ST1=112, ST2=112, ST3=112, U=256, UF=256, UG=256, EA=128, EB=128, EC=128,
-                       ED=128, OL=128), THB=128, ONB=128, IB=128, I25=128, IN=128, R8=8, W8=8, ZC=896, TRI=128, TRP=112, MW=24,
-      LG=8 * L, FAR=16, ML=256, ML2=256, ML3=256, MG=L, MGN=L, EE=L, FM=CAP, QF1=L, QF2=L, XG0=512, XG1=512, QC1=L, QC2=L)
-_pool("float32", dict(PF=112, SC1=128, SC2=128, FS=128, FS2=128, NR=8, X=128, Y=128, LB=128, FC=8, FV=8, FX=8, R0S=24, KM0=128,
-                      KM1=128, KM2=128, KM3=128, PA=8, PB=8, PC=8), WF=1, THF=1, ONF=128, IF=128, ICOL=1, C4K=1, C4K1=1,
-      LMASK=128, CMASK=8, SEGR=128, KC=16, KC2=16, KJ=16, KN=L, TH=8, LD0=128, LF=128, LS=128, NB=16, S0=16, DA=16, DB=16,
-      DST=16, NOD=16, Z1=16, N1=16, B1=16, GMF=8, FARS=16, BST=16, OUTL=32, GG=L, BN=L, BX=L, LOF=16, HIF=16, GD=16, CAN=16,
-      DMIN=16, YPL=16, NF=16)
-_pool("int32", dict(SEL=8, ND=8, RBC=8, ROOT=8, BI=8), PI=2, RI=128, BCI=16, H=128, LW=128, LWL=16, SI=32, BEST=16, MI=256,
-      MCJ=256, NCI=16)
-_pool("uint16", dict(P16=112, LT=8), BCL=8, BCS=8, DL=14, NLT=14, DL2=14)
-SEMAPHORES = ["cv", "cs", "ct", "cg", "aq0", "aq1", "am0", "am1", "lq0", "lq1", "lm0", "lm1"] + ["d%d" % i for i in range(16)]
+_pool("ALLb", "bfloat16", dict(AD=144, DA=1792, DX=1024, Q16=1024, QT=128, A0=112, AS=144, XB=144, X2=144, X3=144, EA=144, EB=144,
+                               EC=144, ED=144, OL=128, EE=112, DG=112, FAR=8),
+      WZ=144, CR=288, ONB=144, SEG=144, IB=128, IN=128, I28=128, I13=128, R1=8, R16=16, R16N=16, REP=1792, TRI=128, TRP=112,
+      THB=128, IS0=112, IS1=112, FM=CAP, QF1=L, QF2=L, QC1=L, QC2=L, XG0=512, XG1=512, ID1=144, SJ=128)
+_pool("ALLf", "float32", dict(RD=144, RD0=144, SC2=144, FD=144, GD2=144, GD3=144, GD4=272, SC=1008, ML=128, X=144, Y0=144, Y1=144,
+                              Y2=144, Y3=144, KM0=144, KM1=144, KM2=144, KM3=144, FS=272, RPF=24, DK=8, IM=8, RN=8, G23=8, FX=8,
+                              LF=64, LZ=64, LS=64, NI=8, ZN=8, N=8, Z0=8, BIN=8, GG=112, NEW=112, FN=8, YPL=8, YH=8, DMIN=8,
+                              UU=8, YP=8, M1=8),
+      TD=144, MW=24, ONF=128, IF=128, WF=1, THF=1, THK=8, KK=2, KC=2, KJ=2, GM=8, GO=8, O15=1, BIAS=1, MG=L, ICOL=1, JF=9,
+      G17=9, J0=9, B1=1, B2=1, J34=4)
+_pool("ALLi", "int32", dict(NN=8, DI=8, RHO=8, TI=64, T6=8, N6=8, BI=8, RT=8), PI=4, RI=128, GI=9, BCI=8, RS=16)
+_pool("ALLu", "uint16", dict(P16=112, LT=8, DL=8, NLT=8, DL2=8), LX=10, L0=10, LH=4, BCL=8)
+_pool("ALLh", "float16", dict(NZ=144, NZ2=144, MB=128, PH=112), IDG=272, SJ1=128, SJ4=128, IH=112, GA=L, GB=L, LG=8 * L)
+SEMAPHORES = ["cv", "cs", "ct", "cg", "aq0", "aq1", "am0", "am1", "lq0", "lq1", "lm0", "lm1"] + ["d%d" % i for i in range(24)]
 PLAN = {}
 
 
@@ -71,14 +83,14 @@ def rank_program(g, core, T, topo):
             if hop_of(src, dst, cores, topo) == core:
                 rid, pid = topo.addr(dst, core)
                 for t in ("q0", "m0", "q1", "m1"):
-                    a = T["LAND" + t[1]][:, 0:CAP] if t[0] == "q" else T["LAND" + t[1]][:, CAP:2 * CAP]
+                    a = T["L" + t.upper()][:]
                     g.wait_ge(T.sem["a" + t], 8)
                     g.remote_dma(a, a, T.sem["a" + t], T.sem["l" + t], pid, rid, some(topo.engines(core, dst)))
                 for t in ("q0", "m0", "q1", "m1"):
                     g.wait_ge(T.sem["l" + t], 8)
         return
 
-    ops, half, ndma, turn = [], [0], [0], [0]
+    ops, lead, ndma, turn = [], [0], [0], [0]
     QUE = {"v": g.vector, "s": g.scalar, "t": g.tensor, "g": g, "y": g.sync}
     SEM = {"v": T.sem.cv, "s": T.sem.cs, "t": T.sem.ct, "g": T.sem.cg}
 
@@ -112,13 +124,13 @@ def rank_program(g, core, T, topo):
                 m *= 1 if any(x[1] in PSUMS for x in ins) else 2
             elif what == "red":
                 m = size(ins[0])
-            elif what != "scan" and all(SIZES[x[1]][1] in ("bfloat16", "uint16") for x in [out] + list(ins)):
+            elif all(SIZES[x[1]][1] in ("bfloat16", "uint16", "float16") for x in [out] + list(ins)):
                 m *= 0.5
             return max(64, m) * CYC
         if q == "s":
             return 0.065 + m * (1.5 if is_ind(ins[0]) else 1) * CYC
         if q == "t":
-            return max(min(64, size(ins[0])), m) * 0.0007 * (4 if SIZES[ins[0][1]][1] == "float32" else 1)
+            return max(min(64, size(ins[0])), m) * TCY * (4 if SIZES[ins[0][1]][1] == "float32" else 1)
         return 0.15 + 2 * m * CYC
 
     def op(q, fn, rd, wr, kind="c", sem=None, val=1, c=0.1):
@@ -129,15 +141,15 @@ def rank_program(g, core, T, topo):
             Wr.append(x[1] if is_ind(x) else x)
             if is_ind(x):
                 R.append(x[2])
-        ops.append((q, fn, R, Wr, kind, sem, val, c, half[0]))
+        ops.append((q, fn, R, Wr, kind, sem, val, c, lead[0]))
 
     def call(q, what, fn, out, *ins):
         op(q, fn, ins, [out], c=cost(q, what, out, ins))
 
-    def dma(q, out, in_, rd, wr):
+    def dma(q, out, in_, rd, wr, c=0.1):
         s = T.sem["d%d" % ndma[0]]
         ndma[0] += 1
-        op(q, lambda: QUE[q].dma_start(out, in_), rd, wr, "d", s, 16)
+        op(q, lambda: QUE[q].dma_start(out, in_), rd, wr, "d", s, 16, c)
 
     def load(q, name, src, a=0, b=None):
         dma(q, A(name, a, b)[0], src, [], [A(name, a, b)])
@@ -157,14 +169,26 @@ def rank_program(g, core, T, topo):
     def fill(out, c):
         call("v", "fill", lambda: g.vector.memset(ap(out), c), out)
 
+    def fill_all(names, c):
+        b, o = POOL[names[0]]
+        e = POOL[names[-1]][1] + SIZES[names[-1]][0][1]
+        x = T[b][:, o:e]
+        half = 0.5 if SIZES[names[0]][1] == "bfloat16" else 1
+        op("v", lambda: g.vector.memset(x, c), [], [A(k) for k in names], c=max(64, (e - o) * half) * CYC)
+
     def scan(out, d0, d1, o0, o1):
         call("v", "scan", lambda: g.vector.tensor_tensor_scan(ap(out), ap(d0), ap(d1), 0.0, o0, o1), out, d0, d1)
 
     def least(out, a):
         call("v", "red", lambda: g.vector.tensor_reduce(ap(out), ap(a), AxisListType.X, OP.min, apply_absolute_value=True), out, a)
 
-    def act(out, a, f, scale=1.0):
-        call("s", "", lambda: g.scalar.activation(ap(out), ap(a), f, scale=scale), out, a)
+    def act(out, a, f, scale=1.0, bias=None):
+        if bias is None:
+            call("s", "", lambda: g.scalar.activation(ap(out), ap(a), f, scale=scale), out, a)
+        elif isinstance(bias, tuple):
+            call("s", "", lambda: g.scalar.activation(ap(out), ap(a), f, bias=ap(bias), scale=scale), out, a, bias)
+        else:
+            call("s", "", lambda: g.scalar.activation(ap(out), ap(a), f, bias=bias, scale=scale), out, a)
 
     def mm(out, l, r, start=True, stop=True):
         call("t", "", lambda: g.tensor.matmul(ap(out), ap(l), ap(r), start, stop), out, l, r)
@@ -176,425 +200,406 @@ def rank_program(g, core, T, topo):
     def asel(out, a, pat, cmp, fillv, base, cm):
         call("g", "", lambda: g.affine_select(ap(out), ap(a), pat, cmp, fillv, base, cm), out, a)
 
+    HB = lambda nm, h, c0=0, c1=None, st=1: A(nm + "_" + str(h), c0, c1, st)
+    RW = lambda nm, h, c0=0, c1=None, st=1: A(nm + "_" + str(h), c0, c1, st, (0, NL[h]))
+    PS = lambda nm, h, c0, c1, st=1, r=128: A(nm + str(h), c0, c1, st, (0, r))
+    EYE = lambda nm, k: A(nm, 0, k, 1, (0, k))
+    FIRST = lambda nm, h, a=0, r=128: A(nm + "_" + str(h), a, a + 136, 17, (0, r))
+    LAST = lambda nm, h, a=0, r=128: A(nm + "_" + str(h), a + 16, a + 136, 17, (0, r))
+    both = lambda nm: [nm + "_0", nm + "_1"]
+
     load("y", "WI", T.w[:])
-    load("y", "QA", T.q[:, 0:L], 0, L)
-    load("s", "R0I", T.r0[:])
-    load("s", "CHI", T.ch[:, 0:1152], 0, 1152)
-    load("y", "PT", T.pt[:], 0, M)
-    load("s", "CHI", T.ch[:, 1152:M], 1152, M)
+    load("s", "QA", T.q[:, 0:L], 0, L)
+    load("y", "PT", T.pt[:, 0:1152], 0, 1152)
+    load("s", "CH", T.ch[:, 0:80], 0, 80)
+    load("s", "PT", T.pt[:, 1152:M], 1152, M)
+    load("y", "R0I", T.r0[:])
+    load("y", "CH", T.ch[:, 80:1200], 80, 1200)
+    load("s", "CH", T.ch[:, 1200:M], 1200, M)
     load("y", "THI", T.th[:])
     load("y", "QA", T.q[:, L:VI * L], L, VI * L)
 
-    fill(A("R8"), 65536.0)
+    fill_all(["WZ", "CR"], 0.0)
+    fill_all(["ONB", "SEG"], 1.0)
     fill(A("ONF"), 1.0)
-    fill(A("ONB"), 1.0)
-    fill(A("SEGR"), 0.0)
-    fill(A("ZC"), 0.0)
     iota(A("PI", 0, 1), [[0, 1]], 0, 1)
-    iota(A("RI"), [[0, 8], [1, 16]], 0, 0)
-    asel(A("R8"), A("R8"), [[-16, 8]], OP.is_ge, 0.0, 0, 1)
-    asel(A("R8"), A("R8"), [[16, 8]], OP.is_ge, 0.0, 15, -1)
-    asel(A("CMASK"), A("ONF", 0, 8), [[-16, 8]], OP.is_ge, 0.0, 0, 1)
-    asel(A("CMASK"), A("CMASK"), [[16, 8]], OP.is_ge, 0.0, 15, -1)
-    iota(A("BCI", 0, 8), [[1, 8]], 0, 0)
-    iota(A("BCI", 8, 16), [[16, 8]], 15, 0)
-    asel(A("IF"), A("ONF"), [[-1, 128]], OP.is_equal, 0.0, 0, 1)
-    asel(A("IB"), A("ONB"), [[-1, 128]], OP.is_equal, 0.0, 0, 1)
-    Z = lambda b: A("ZC", b * 128, b * 128 + 128)
-    asel(Z(0), Z(0), [[-1, 8], [0, 16]], OP.not_equal, 1.0, 0, 1)
-    asel(Z(5), Z(5), [[-1, 8], [0, 16]], OP.not_equal, -1.0, -8, 1)
-    tt(Z(1), Z(5), Z(0), OP.subtract)
-    tt(Z(2), Z(5), Z(0), OP.add)
-    ts(Z(3), Z(0), -1.0, OP.mult)
-    cp(Z(4), Z(0))
-    cp(Z(6), Z(5))
-    for b, sgn, c in ((0, -16, -7.5), (1, 16, 0.0), (2, -16, -15.0)):
-        z = A("ZC", b * 128, b * 128 + 128, 1, (32, 34))
-        iota(z, [[0, 8], [sgn, 16]], 0, 0, True)
-        asel(z, z, [[0, 128]], OP.not_equal, c, -1, 1)
-    cp(A("ZC", 640, 896, 1, (32, 34)), A("ZC", 128, 384, 1, (32, 34)))
-    asel(A("SEGR"), A("SEGR"), [[0, 8], [1, 16]], OP.not_equal, float(TOP), 0, 0)
+    asel(A("R1"), A("ONB", 0, 8), [[-16, 8]], OP.is_ge, 0.0, 0, 1)
+    asel(A("R1"), A("R1"), [[16, 8]], OP.is_ge, 0.0, 15, -1)
+    asel(A("IB"), A("ONB", 0, 128), [[-1, 128]], OP.is_equal, 0.0, 0, 1)
+    iota(A("PT", M, W), [[0, W - M]], 0, 0, True)
+    iota(A("JF"), [[16, 9]], 0, 0, True)
+    iota(A("CR", 0, 136, 1, (0, 1)), [[0, 8], [16384, 17]], 16384 * 119, 0, True)
+    iota(A("CR", 136, 272, 1, (0, 1)), [[0, 8], [-1, 17]], 1, 0, True)
+    asel(A("ID1", 0, 136), A("ONB", 0, 136), [[-16, 8], [-1, 17]], OP.is_equal, 0.0, 1, 1)
+    iota(A("CH", M, CW), [[0, CW - M]], 0, 0)
+    asel(A("SJ"), A("ONB", 0, 128), [[-1, 16], [-16, 8]], OP.is_equal, 0.0, 0, 1)
+    cp(A("WF"), A("WI"))
+    ts(A("WZ", 15, 143, 16), A("R1"), A("WF"), OP.mult)
+    ts(A("IN"), A("IB"), -1.0, OP.mult)
+    for i in range(16):
+        act(A("REP", i, 1792, 16), A("IB", 0, 112), AF.Copy)
+    ts(A("R16", 0, 8), A("R1"), U, OP.mult)
+    ts(A("R16", 8, 16), A("R1"), -16.0, OP.mult)
+    ts(A("R16N"), A("R16"), -1.0, OP.mult)
+    cp(A("IF"), A("IB"))
+    fill(A("SEG", 0, 136, 17), 0.0)
+    fill_all(both("AD"), -16.0)
+    fill_all(both("RD") + both("RD0"), -BIG)
+    fill(A("CR", 0, 136, 1, (32, 33)), 4.0 * (MID + 256))
+    fill(A("CR", 0, 136, 17, (0, 1)), -BIG)
+    fill(A("CR", 136, 272, 17, (0, 1)), BIG)
+    ts(A("IDG", 0, 136), A("ID1", 0, 136), 4.0, OP.mult)
+    ts(A("IDG", 136, 272), A("ID1", 0, 136), -1.0 / 4096, OP.mult)
+    ts(A("I28"), A("IB"), float(2 ** 28), OP.mult)
     ts(A("PI", 1, 2), A("PI", 0, 1), 15, OP.bitwise_and)
     cp(A("ICOL"), A("PI", 1, 2))
-    ts(A("C4K"), A("ICOL"), 4096.0, OP.mult)
-    ts(A("C4K1"), A("C4K"), 1.0, OP.add)
-    ts(A("LMASK"), A("RI"), A("ICOL"), OP.is_equal)
-    cp(A("BCL"), A("BCI", 0, 8))
-    cp(A("BCS"), A("BCI", 8, 16))
-    cp(A("WF"), A("WI"))
-    ts(A("W8"), A("R8"), 1.0 / 65536, OP.mult, A("WF"), OP.mult)
-    for h in ("_1", "_0"):
-        for nm in ("SC2", "NR", "Y", "FV", "KM0", "KM1", "KM2"):
-            fill(A(nm + h), 0.0)
-        fill(A("ND" + h), 0)
-        fill(A("BI" + h), 0)
-        for l in "0123":
-            fill(A("ST" + l + h), 0.0)
-            fill(A("ST" + l + h, 0, 112, 1, (32, 34)), 1.0)
-    fill(A("SI"), 0)
-    fill(A("H"), 0)
-    cp(A("H", 0, 128, 8), A("ONF", 0, 16))
-    for nm in ("NB", "DST", "S0", "DB", "FAR", "CAN", "DMIN"):
-        fill(A(nm), 0.0)
-    fill(A("PT", M, W), 0.0)
-    fill(A("CHI", M, CW), 0)
-    cp(A("R0F"), A("R0I"))
-    for h in (1, 0):
-        for t in range(VI):
-            a = t * L + K0[h]
-            mm(A("FB%d" % h, 8 * t, 8 * t + 8, 1, (0, NL[h])), A("R0F", a, a + NL[h]), A("IF", 0, 8, 1, (0, 8)))
-        ts(A("R0S_%d" % h, 0, 24, 1, (0, NL[h])), A("FB%d" % h, 0, 24, 1, (0, NL[h])), 65536.0, OP.mult)
-    ts(A("IN"), A("IB"), -1.0, OP.mult)
-    ts(A("I25"), A("IB"), 33554432.0, OP.mult)
-    fill(A("TRP"), 8192.0)
-    for nm in ("MW", "ML3"):
-        fill(A(nm), 0.0)
-    for nm in ("MI", "MCJ"):
-        fill(A(nm), 0)
-    cp(A("MI", 4, 256, 16), A("ONF", 0, 16))
-    for nm, j, v in (("ML3", 3, -1.0), ("ML3", 4, -64.0), ("MCJ", 1, 1.0), ("MCJ", 2, 64.0)):
-        ts(A(nm, j, 256, 16), A("ONF", 0, 16), v, OP.mult)
-    ts(A("GMF"), A("R8"), 1.0 / 65536, OP.mult)
-    for t in (0, 1):
-        fill(A("SEND%d" % t, 208, 368), -80.0)
-        fill(A("SEND%d" % t, 576, 736), 0.0)
-        ts(A("QF%d" % (t + 1)), A("QA", (t + 1) * L, (t + 2) * L), 64.0, OP.subtract)
-        cp(A("QC%d" % (t + 1), CAP, L), A("QA", (t + 1) * L + CAP, (t + 2) * L))
-    cp(A("THF"), A("THI"))
-    ts(A("THB"), A("ONB"), A("THF"), OP.mult)
-    asel(A("TRI"), A("ONB"), [[1, 128]], OP.is_ge, 0.0, -1, -1)
-    asel(A("TRI"), A("TRI"), [[1, 128]], OP.not_equal, -512.0, 0, -1)
-    asel(A("TRP"), A("TRP"), [[1, 112]], OP.is_ge, 0.0, 0, -1)
-    for c, j, v in ((0, 0, 65536.0), (8, 1, 1.0), (8, 2, 64.0), (8, 3, 4096.0), (16, 4, 1.0)):
-        asel(A("MW", c, c + 8), A("MW", c, c + 8), [[-16, 8]], OP.not_equal, v, -j, 1)
-    iota(A("KC"), [[112, 2], [0, 8]], 0, 1, True)
-    iota(A("KC2"), [[-112, 2], [0, 8]], 720, -1, True)
-    iota(A("KJ"), [[112, 2], [0, 8]], W, 1, True)
-    iota(A("KN"), [[1, L]], M, 0, True)
-    mm(A("FB1", 64, 72), A("THB"), A("R8"))
-    ts(A("TH"), A("FB1", 64, 72), 1.0 / 16, OP.mult)
+    ts(A("JF"), A("JF"), A("ICOL"), OP.add)
+    ts(A("GI"), A("JF"), 1.0 / 17, OP.mult, -8.0 / 17, OP.add)
+    ts(A("G17"), A("GI"), 17.0, OP.mult, 119.0, OP.min)
+    cp(A("L0", 0, 9), A("G17"))
+    tt(A("J0"), A("JF"), A("G17"), OP.is_equal)
+    ts(A("J0"), A("J0"), 200.0, OP.mult, 16.0, OP.add)
+    tt(A("J0"), A("J0"), A("G17"), OP.add)
+    ts(A("LX", 0, 9), A("J0"), 136.0, OP.min)
 
-    def RW(nm, h, c0=0, c1=None, st=1):
-        return A(nm + str(h) if nm + str(h) in PSUMS else nm + "_" + str(h), c0, c1, st, (0, NL[h]))
+    def radii(t):
+        cp(A("R0F", t * L, t * L + L), A("R0I", t * L, t * L + L))
+        for h in (0, 1):
+            a, o = t * L + K0[h], PS("ZB", h, 448, 456, 1, NL[h])
+            mm(o, A("R0F", a, a + NL[h]), A("IF", 0, 8, 1, (0, 8)))
+            ts(RW("RPF", h, 8 * t, 8 * t + 8), o, RC, OP.add, U, OP.mult)
+    radii(0)
+    fill(A("PT", 0, 1), 256.0)
+    fill(A("TD"), BIG)
+    fill(A("TD", 0, 136, 17), NONE)
+    for h in (0, 1):
+        fill(HB("SC", h, 144 + 136, 1008, 144), BIG)
+        fill(HB("SC2", h, 136, 137), BIG)
+        ts(HB("NZ", h), A("ONB"), 0.0, OP.mult)
+    ts(A("SJ4"), A("SJ"), -4096.0, OP.mult)
 
-    HB = lambda nm, h, c0=0, c1=None, st=1: A(nm + "_" + str(h), c0, c1, st)
-    SI = lambda h, a, b: A("SI", 16 * h + a, 16 * h + b, 1, (0, NL[h]))
-    HI = lambda h, e: A("H", h * 64 + e, h * 64 + 64, 8, (0, NL[h]))
-    LAST = lambda nm, h: RW(nm, h, 15, 128, 16)
-    SEG = lambda h: A("SEGR", 0, 128, 1, (0, NL[h]))
-    EYE = lambda nm, k: A(nm, 0, k, 1, (0, k))
-    hc = lambda nm, h, r=None: A(nm, 8 * h, 8 * h + 8, 1, (0, NL[h] if r is None else r))
+    def later():
+        ts(A("I13"), A("IB"), -8192.0, OP.mult)
+        fill_all(both("FD") + both("GD2") + both("GD3") + both("GD4"), BIG)
+        for h in (0, 1):
+            for nm in ("GD2", "GD3"):
+                fill(FIRST(nm, h), NONE)
+            fill(HB("GD4", h, 0, 272, 17), NONE)
+            fill(HB("SC", h, 0, 144), 4.0 * (C0 + 1))
+            for s in range(1, 5):
+                fill(HB("SC", h, 144 * s + 137, 144 * s + 144), 0.0)
+            ts(HB("NZ2", h), A("ONB"), 0.0, OP.mult)
+            ts(HB("MB", h), A("ONB", 0, 128), 0.0, OP.mult)
+            fill(HB("BIN", h), -4096.0 * rank)
+            fill(HB("BI", h), 0)
+        fill_all(both("ML"), 0.0)
+        for h in (0, 1):
+            fill(HB("ML", h, 2, 128, 16), 1.0)
+        fill(A("MW"), 0.0)
+        iota(A("J34"), [[34, 4]], 0, 0, True)
+        iota(A("BCI"), [[1, 8]], 0, 0)
+        iota(A("RI"), [[0, 8], [1, 16]], 0, 0)
+        asel(A("TRI"), A("ONB", 0, 128), [[1, 128]], OP.is_ge, 0.0, -1, -1)
+        asel(A("TRI"), A("TRI"), [[1, 128]], OP.not_equal, -512.0, 0, -1)
+        fill(A("TRP"), 8192.0)
+        asel(A("TRP"), A("TRP"), [[1, 112]], OP.is_ge, 0.0, 0, -1)
+        for c, j, v in ((0, 0, U), (0, 2, RC * U), (8, 2, BIG), (16, 1, 1.0)):
+            asel(A("MW", c, c + 8), A("MW", c, c + 8), [[-16, 8]], OP.not_equal, v, -j, 1)
+        asel(A("GM"), A("ONF", 0, 8), [[-16, 8]], OP.is_equal, 0.0, -15, 1)
+        asel(A("GO"), A("ONF", 0, 8), [[-16, 8]], OP.is_equal, 0.0, -14, 1)
+        iota(A("KK"), [[112, 2]], 0, 1, True)
+        iota(A("KC"), [[112, 2]], L, 1, True)
+        iota(A("KJ"), [[112, 2]], W - MID, 1, True)
+        ts(A("PI", 2, 3), A("PI", 0, 1), 7, OP.bitwise_and)
+        ts(A("PI", 3, 4), A("PI", 0, 1), 3, OP.logical_shift_right, 1, OP.bitwise_and)
+        ts(A("B1"), A("PI", 2, 3), 5.0, OP.min, 144.0, OP.mult)
+        ts(A("B2"), A("PI", 3, 4), 17.0, OP.mult, 16.0, OP.add)
+        ts(A("LH"), A("J34"), A("B1"), OP.add, A("B2"), OP.add)
+        cp(A("BCL"), A("BCI"))
+        cp(A("SJ1"), A("SJ"))
+        cp(A("IH"), A("IB", 0, 112))
+        ts(A("O15"), A("ICOL"), 15.0, OP.is_equal)
+        ts(A("BIAS"), A("ICOL"), 1.0, OP.is_equal, 4096.0 * rank, OP.mult)
+        for t in (0, 1):
+            ts(HB("DG", t), A("IB", 0, 112), A("KK", t, t + 1), OP.mult)
+            ts(A("IS%d" % t), A("IB", 0, 112), float(M + t * L), OP.mult)
+            fill(A("SQ%d" % t), -80.0)
+            fill(A("SM%d" % t), 0.0)
+            ts(A("QF%d" % (t + 1)), A("QA", (t + 1) * L, (t + 2) * L), 64.0, OP.subtract)
+            cp(A("QC%d" % (t + 1), CAP, L), A("QA", (t + 1) * L + CAP, (t + 2) * L))
+            radii(t + 1)
+        cp(A("THF"), A("THI"))
+        ts(A("THB"), A("ONB", 0, 128), A("THF"), OP.mult)
+        mm(PS("ZB", 1, 456, 464), A("THB"), A("R1"))
+        ts(A("THK"), PS("ZB", 1, 456, 464), U / 16, OP.mult, RC * U, OP.add)
 
-    def to_list(win, h):
-        tt(HB("LB", h), ind(win, A("BCL")), A("LMASK"), OP.mult)
-        mm(A("KEY%d" % h, 128, 128 + NL[h] // 16), RW("LB", h), A("CMASK", 0, NL[h] // 16, 1, (0, NL[h])))
-
-    def list_copy(out, h, more=0.0):
-        ts(out, A("KEY%d" % h, 128, 128 + NL[h] // 16), more, OP.add)
-
-    def kids(h, more=0.0):
+    def to_list(out, h, nz, sj, more):
         k = NL[h] // 16
-        list_copy(HB("LT", h, 0, k), h, more)
-        ts(HB("P16", h, 0, NL[h]), ind(A("CH"), HB("LT", h, 0, k)), A("C4K"), OP.subtract)
-        act(HB("PF", h, 0, NL[h]), ind(A("CH"), HB("LT", h, 0, k)), AF.Copy)
+        o = PS("FB", h, 288, 288 + k)
+        for j in range(16):
+            mm(o, RW(nz, h, 15 - j, 143 - j), A(sj, 8 * j, 8 * j + k, 1, (0, NL[h])), j == 0, j == 15)
+        ts(HB(out, h, 0, k), o, more, OP.add)
 
-    def masks(h, lev, want_y, fbs):
-        nl = NL[h]
-        stt = lambda l, k=34: A("ST%d_%d" % (min(l, 3), h), 0, nl, 1, (0, k))
-        mm(A("ZB%d" % h, 384, 384 + nl, 1, (0, 16)), RW("ST", h), EYE("IB", nl))
-        act(stt(lev, 16), A("ZB%d" % h, 384, 384 + nl, 1, (0, 16)), AF.Copy)
-        mm(RW("ZB", h, 0, 384), stt(lev), A("ZC", 0, 384, 1, (0, 34)))
-        act(RW("U", h), RW("ZB", h, 128, 384), AF.Relu, float(TOP))
-        if want_y:
-            act(RW("Y", h), RW("ZB", h, 0, 128), AF.Abs, 65536.0 * TOP)
-        for c, u, l, k, es in fbs:
-            mm(RW("FB", h, 128, 384), stt(l), A("ZC", 384, 640, 1, (0, 34)), True, False)
-            mm(RW("FB", h, 128, 384), stt(lev), A("ZC", 640, 896, 1, (0, 34)), False, True)
-            act(RW(u, h), RW("FB", h, 128, 384), AF.Relu, float(TOP))
+    def kids(h, top=CW):
+        cp(HB("P16", h, 0, NL[h]), ind(A("CH", 0, top), HB("LT", h, 0, NL[h] // 16)))
+        ts(HB("PH", h, 0, NL[h]), HB("P16", h, 0, NL[h]), float(MID), OP.subtract)
 
-    def fallback(h, fbs):
-        for c, u, l, k, es in fbs:
-            o = RW("FB", h, c, c + 128)
-            mm(o, EYE("IF", NL[h]), RW(k, h), True, False)
-            for e in es:
-                mm(o, EYE("I25", NL[h]), RW(e, h), False, False)
-            mm(o, EYE("IB", NL[h]), RW(u, h, 0, 128), False, False)
-            mm(o, EYE("IB", NL[h]), RW(u, h, 128, 256), False, True)
-
-    def points_scalar(h, a, b):
-        z = turn[0] = 1 - turn[0]
-        w = 16 * (b - a)
-        x, o = A("XG%d" % z, 0, w), A("SP%d" % z, 0, w)
-        act(x, ind(A("PT"), HB("P16", h, a, b)), AF.Copy)
-        mm(o, A("IN"), A("Q16", 16 * (K0[h] + a), 16 * (K0[h] + b)), True, False)
-        mm(o, A("IB"), x, False, True)
-        act(HB("DT", h, 16 * a, 16 * b), o, AF.Abs)
-
-    def points_vector(h, a, b):
-        d = HB("DT", h, 16 * a, 16 * b)
-        tt(d, ind(A("PT"), HB("P16", h, a, b)), A("Q16", 16 * (K0[h] + a), 16 * (K0[h] + b)), OP.subtract)
-        act(d, d, AF.Abs)
+    def masks(h, lev, rd):
+        y = HB("Y%d" % min(lev, 3), h)
+        scan(HB("AS", h), A("SEG"), HB("AD", h), OP.mult, OP.add)
+        act(y, HB("AS", h), AF.Abs, U, -7.5 * U)
+        tt(HB("XB", h), ind(HB(rd, h, 0, 136), A("L0", 0, 9)), y, OP.is_lt)
 
     def points(h):
-        for (a, b), (c, d) in zip(VS[h], SS[h]):
-            points_scalar(h, c, d)
-            points_vector(h, a, b)
+        for c in range(3):
+            a, b = SS[h][c]
+            z = turn[0] = 1 - turn[0]
+            w = 16 * (b - a)
+            x, o = A("XG%d" % z, 0, w), PS("SP", z, 0, w)
+            act(x, ind(A("PT"), HB("P16", h, a, b)), AF.Copy)
+            mm(o, RW("QT", h), A("REP", 16 * a, 16 * b, 1, (0, NL[h])), True, False)
+            mm(o, A("IB"), x, False, True)
+            act(HB("DA", h, 16 * a, 16 * b), o, AF.Abs)
+            if c < 2:
+                a, b = VS[h][c]
+                d = HB("DX", h, 16 * a, 16 * b)
+                tt(d, ind(A("PT"), HB("P16", h, a, b)), HB("Q16", h, 16 * a, 16 * b), OP.add)
+                ts(HB("DA", h, 16 * a, 16 * b), d, 0.0, OP.max, 2.0, OP.mult)
 
     def keys(h):
-        nl = NL[h]
-        o = RW("KEY", h, 0, 128)
-        mm(o, HB("PF", h, 0, nl), A("IF"), True, False)
-        mm(o, EYE("IB", nl), RW("U", h, 0, 128), False, False)
-        mm(o, EYE("IB", nl), RW("U", h, 128, 256), False, False)
+        nl, x = NL[h], VS[h][-1][1]
+        mm(PS("KEY", h, 0, 280, 1, nl), A("ONB", 0, nl, 1, (0, 33)), A("CR", 0, 280, 1, (0, 33)), True, False)
+        mm(PS("KEY", h, 0, 272, 1, nl), HB("PH", h, 0, nl), A("IDG"), False, False)
         for i in range(16):
-            mm(RW("KEY", h, i, 128, 16), HB("DT", h, i, 16 * nl, 16), A("R8"), False, i == 15)
+            mm(PS("KEY", h, i + 1, 272, 17, x), HB("DX", h, i, 16 * x, 16), A("R16N"), False, False)
+        mm(PS("KEY", h, 0, 136, 1, nl), EYE("I28", nl), RW("XB", h, 0, 136), False, False)
+        for i in range(16):
+            mm(PS("KEY", h, i + 1, 272, 17, nl), HB("DA", h, i, 16 * nl, 16), A("R16"), False, i == 15)
 
-    FBS = {2: [(0, "UF", 0, "KM0", ("EA",))], 3: [(0, "UF", 1, "KM1", ("EB",))],
-           4: [(0, "UF", 2, "KM2", ("EC",)), (384, "UG", 0, "KM0", ("EA", "ED"))]}
+    FBS = {2: [(0, "X2", ("EA",))], 3: [(1, "X2", ("EB",))], 4: [(2, "X2", ("EC",)), (0, "X3", ("EA", "ED"))]}
 
     def look(h, s):
-        scan(RW("SC1", h), SEG(h), RW("KEY", h, 0, 128), OP.max, OP.min)
-        t1, rho = HI(h, s + 1), SI(h, 8, 16)
-        tt(t1, LAST("SC1", h), RW("RBC", h) if s == 1 else rho, OP.min)
-        if s <= ST:
-            ts(RW("NR", h), t1, -float(TOP), OP.mult, -7.5 * 65536 * TOP, OP.add)
-        ts(rho, t1, 16711680, OP.bitwise_and)
+        a = 144 * s
+        scan(HB("SC", h, a, a + 136), PS("KEY", h, 0, 136), HB("RD", h, 0, 136), OP.min, OP.max)
         if s == ST + 1:
             return
-        tt(HB("X", h), ind(HB("NR", h), A("BCL")), HB("Y", h), OP.add)
         km = "KM%d" % min(s - 1, 3)
-        tt(RW(km, h), RW("KEY", h, 0, 128), RW("X", h), OP.max)
-        scan(RW("SC2", h), SEG(h), RW(km, h), OP.max, OP.min)
-        if s >= 3:
-            scan(RW("FS", h), SEG(h), RW("FB", h, 0, 128), OP.max, OP.min)
-            fc = LAST("FS", h)
-            if s == 5:
-                scan(RW("FS2", h), SEG(h), RW("FB", h, 384, 512), OP.max, OP.min)
-                tt(RW("FX", h), RW("PA", h), RW("PB", h), OP.min)
-                tt(RW("FX", h), RW("FX", h), LAST("FS2", h), OP.max)
-                tt(RW("FC", h), RW("FX", h), fc, OP.min)
-                fc = RW("FC", h)
-            tt(RW("FV", h), fc, RW({3: "PA", 4: "PB", 5: "PC"}[s], h), OP.max)
-            tt(RW("SEL", h), LAST("SC2", h), RW("FV", h), OP.min)
-        else:
-            cp(RW("SEL", h), LAST("SC2", h))
-        ts(RW("ND", h), RW("SEL", h), 4095, OP.bitwise_and)
-        to_list(HB("ND", h), h)
-        ts(SI(h, 0, 8), RW("SEL", h), 33488896, OP.bitwise_and)
-        ts(RW("ST", h), SI(h, 0, 16), 1.0 / 65536, OP.mult)
-        masks(h, s, s < ST, FBS.get(s, []))
-        if s in (2, 3, 4):
-            ts(RW({2: "PA", 3: "PB", 4: "PC"}[s], h), RW("SEL", h), TOP, OP.is_lt, float(TOP), OP.mult)
+        tt(HB("X", h), ind(HB("SC", h, a, a + 137), A("LX", 0, 9)), HB("Y%d" % min(s - 1, 3), h), OP.subtract)
+        tt(HB(km, h), PS("KEY", h, 136, 280), HB("X", h), OP.min)
+        scan(HB("SC2", h, 0, 136), HB(km, h, 0, 136), HB("FD", h, 0, 136) if s >= 3 else A("TD", 0, 136), OP.max, OP.min)
+        ts(HB("NN", h), LAST("SC2", h), -1.0, OP.mult)
+        tt(HB("NZ", h, 15, 143, 16), LAST("SC2", h), HB("NN", h), OP.add)
+        to_list("LT", h, "NZ", "SJ4", float(MID))
+        kids(h)
+        ts(HB("RHO", h), LAST("SC", h, a), 1.0 / U, OP.mult, -8.0, OP.add)
+        ts(FIRST("RD", h), HB("RHO", h), RC, OP.add, U, OP.mult)
+        ts(HB("DI", h), HB("NN", h), 4, OP.logical_shift_right)
+        ts(FIRST("AD", h), HB("DI", h), 16.0, OP.add)
+        masks(h, s, "RD")
+        sel = ind(HB("SC2", h, 0, 137), A("LX", 0, 9))
         if s <= 3:
-            tt(HB({1: "EA", 2: "EB", 3: "EC"}[s], h), ind(HB("SC2", h), A("BCS")), HB(km, h), OP.is_equal)
+            tt(HB({1: "EA", 2: "EB", 3: "EC"}[s], h), sel, HB(km, h), OP.is_equal)
         if s == 3:
-            tt(HB("ED", h), ind(HB("FV", h), A("BCL")), HB("KM0", h), OP.is_equal)
+            tt(HB("ED", h), sel, HB("KM0", h), OP.is_equal)
+        if s not in FBS:
+            return
+        gd = "GD%d" % s
+        ts(LAST(gd, h), HB("NN", h), 64.0, OP.mult, -256000.0, OP.add)
+        if s == 4:
+            tt(HB("G23", h), LAST("GD2", h), LAST("GD3", h), OP.max)
+            tt(LAST(gd, h, 136), HB("G23", h), LAST(gd, h), OP.min)
+        for c, (l, x, es) in enumerate(FBS[s]):
+            tt(HB(x, h), ind(HB("RD", h, 0, 136), A("L0", 0, 9)), HB("Y%d" % l, h), OP.is_lt)
+            o = PS("FB", h, 136 * c, 136 * c + 136)
+            mm(o, A("IF"), HB("KM%d" % l, h, 0, 136), True, False)
+            for e in es + (x,):
+                mm(o, A("I13"), HB(e, h, 0, 136), False, e == x)
+        w = 136 * len(FBS[s])
+        scan(HB("FS", h, 0, w), PS("FB", h, 0, w), HB(gd, h, 0, w), OP.max, OP.min)
+        if s == 4:
+            tt(HB("FX", h), LAST("FS", h), LAST("FS", h, 136), OP.max)
+        ts(FIRST("FD", h), HB("FX", h) if s == 4 else LAST("FS", h), NONE, OP.max)
 
     QN = ("QA", "QC1", "QC2")
     nh = (112, CAP - 112)
     for t in range(VI):
-        q = lambda a, b: A(QN[t], a, b)
+        q = lambda a, b, st=1: A(QN[t], a, b, st)
+        qh = lambda h: q(K0[h], K0[h] + NL[h])
+        fq = "QF%d" % t if t else "QA"
         if t:
-            ld, fq = "LAND%d" % (t - 1), "QF%d" % t
-            op("x", None, [], [A(ld, 0, CAP)], "x", T.sem["aq%d" % (t - 1)], 8)
-            op("x", None, [], [A(ld, CAP, 2 * CAP)], "x", T.sem["am%d" % (t - 1)], 8)
-            tt(A(fq, 0, CAP), A(fq, 0, CAP), A(ld, 0, CAP), OP.max)
+            lq, lm = "LQ%d" % (t - 1), "LM%d" % (t - 1)
+            op("x", None, [], [A(lq)], "x", T.sem["aq%d" % (t - 1)], 8)
+            op("x", None, [], [A(lm)], "x", T.sem["am%d" % (t - 1)], 8)
+            tt(A(fq, 0, CAP), A(fq, 0, CAP), A(lq), OP.max)
             ts(A("FM"), A(fq, 0, CAP), 0.0, OP.is_lt, 64.0, OP.mult)
             tt(q(0, CAP), A("FM"), A(fq, 0, CAP), OP.add)
-        for h in (1, 0):
-            mm(RW("KEY", h, 136, 144), A(fq if t else "QA", K0[h], K0[h] + NL[h]), A("W8"))
-            if t:
-                mm(A("KEY%d" % h, 152, 176, 1, (0, nh[h])), A(ld, CAP + K0[h], CAP + K0[h] + nh[h]), A("MW"))
-        for h in (1, 0):
-            cp(RW("SEL", h), RW("KEY", h, 136, 144))
-            ts(RW("ND", h), RW("SEL", h), 63, OP.bitwise_and)
-            to_list(HB("ND", h), h)
-            ts(RW("ROOT", h), RW("ND", h), 1, OP.add)
-        for i in range(16):
-            if i < 10:
-                cp(A("Q16", i, 16 * L, 16), q(0, L))
-            else:
-                act(A("Q16", i, 16 * L, 16), q(0, L), AF.Copy)
-        for h in (1, 0):
-            cp(SI(h, 8, 16), RW("R0S", h, 8 * t, 8 * t + 8))
-            if t:
-                r = (0, nh[h])
-                k = lambda a: A("KEY%d" % h, a, a + 8, 1, r)
-                nf = hc("NF", h, nh[h])
-                ts(nf, k(168), 0.0, OP.is_equal)
-                tt(nf, nf, A("R0S_%d" % h, 8 * t, 8 * t + 8, 1, r), OP.mult)
-                tt(A("SI", 16 * h + 8, 16 * h + 16, 1, r), k(152), nf, OP.add)
-                ts(hc("NB", h, nh[h]), k(160), -1.0, OP.mult)
-        if t == 0:
-            for a, b in ((0, 1152), (1152, CW)):
-                ts(A("CH", a, b), A("CHI", a, b), A("C4K"), OP.add)
-            fill(A("PT", 0, 1), 256.0)
-        for h in (1, 0):
-            k = NL[h] // 16
-            kids(h, 1.0)
-            a0 = HB("A0", h, 0, NL[h])
-            tt(a0, ind(A("PT"), HB("LT", h, 0, k)), q(K0[h], K0[h] + NL[h]), OP.subtract)
+        o = PS("FB", 0, 288, 301)
+        for j in range(16):
+            mm(o, A("WZ", 15 - j, 143 - j), A(fq, j, L, 16), j == 0, j == 15)
+        cp(A("RS", 0, 13), o)
+        ts(A("RS", 0, 13), A("RS", 0, 13), 63, OP.bitwise_and)
+        for h in (0, 1):
+            lead[0] = 1 - h
+            nl = NL[h]
+            ts(HB("LT", h, 0, nl // 16), A("RS", 7 * h, 7 * h + nl // 16), 1.0, OP.add)
+            mm(PS("ZB", h, 0, 128, 1, nl), qh(h), A("IN"))
+            act(RW("QT", h), PS("ZB", h, 0, 128, 1, nl), AF.Copy)
+            for a, b in VS[h]:
+                z = turn[0] = 1 - turn[0]
+                o = PS("SP", z, 0, 16 * (b - a))
+                mm(o, RW("QT", h), A("REP", 16 * a, 16 * b, 1, (0, nl)))
+                act(HB("Q16", h, 16 * a, 16 * b), o, AF.Copy)
+            kids(h, 80)
+            a0 = HB("A0", h, 0, nl)
+            tt(a0, ind(A("PT", 0, 80), HB("LT", h, 0, nl // 16)), qh(h), OP.subtract)
             act(a0, a0, AF.Abs)
-            mm(RW("KEY", h, 144, 152), a0, A("R8"))
-        for h in (1, 0):
-            cp(SI(h, 0, 8), RW("KEY", h, 144, 152))
-            ts(RW("ST", h), SI(h, 0, 16), 1.0 / 65536, OP.mult)
-            masks(h, 0, True, [])
-            tt(RW("SEL", h), SI(h, 0, 8), SI(h, 8, 16), OP.is_lt)
-            tt(RW("RBC", h), SI(h, 0, 8), SI(h, 8, 16), OP.min)
-            tt(HI(h, 1), RW("SEL", h), RW("ROOT", h), OP.mult)
-        for h in (1, 0):
+            d0, s0 = PS("ZB", h, 128, 136, 1, nl), PS("ZB", h, 136, 144, 1, nl)
+            mm(s0, A(fq, K0[h], K0[h] + nl), A("WZ", 15, 143, 16))
+            mm(d0, a0, A("R1"))
+            ts(FIRST("AD", h, 0, nl), d0, 16.0, OP.add)
+            ts(RW("DK", h), d0, RC, OP.add, U, OP.mult)
+            cp(RW("RT", h), s0)
+            rpf = lambda r: A("RPF_%d" % h, 8 * t, 8 * t + 8, 1, (0, r))
+            if nh[h] < nl or not t:
+                cp(FIRST("RD0", h, 0, nl), rpf(nl))
+            if t:
+                r = nh[h]
+                mm(PS("ZB", h, 144, 168, 1, r), A(lm, K0[h], K0[h] + r), A("MW"))
+                m1 = A("M1_%d" % h, 0, 8, 1, (0, r))
+                tt(m1, rpf(r), PS("ZB", h, 152, 160, 1, r), OP.subtract)
+                tt(FIRST("RD0", h, 0, r), PS("ZB", h, 144, 152, 1, r), m1, OP.max)
+                ts(A("BIN_%d" % h, 0, 8, 1, (0, r)), PS("ZB", h, 160, 168, 1, r), -4096.0 * rank, OP.add)
+            masks(h, 0, "RD0")
+            tt(FIRST("RD", h, 0, nl), RW("DK", h), FIRST("RD0", h, 0, nl), OP.min)
+            tt(RW("IM", h), RW("DK", h), FIRST("RD0", h, 0, nl), OP.is_lt)
+            ts(RW("RT", h), RW("RT", h), 63, OP.bitwise_and)
+            ts(RW("RN", h), RW("RT", h), 1.0, OP.add)
+            tt(RW("RN", h), RW("RN", h), RW("IM", h), OP.mult)
+        for h in (0, 1):
+            lead[0] = 1 - h
+            mm(PS("KEY", h, 0, 280), A("ONB", 0, 128, 1, (0, 33)), A("CR", 0, 280, 1, (0, 33)))
             points(h)
             keys(h)
-        for s in range(1, ST + 2):
-            for h in (1, 0):
-                half[0] = h
+        if t == 0:
+            lead[0] = -10
+            later()
+        for s in range(1, ST + 1):
+            for h in (0, 1):
+                lead[0] = 1 - h
                 look(h, s)
-            if s <= ST:
-                for h in (1, 0):
-                    half[0] = h
-                    kids(h)
-                    points(h)
-                    keys(h)
-                    fallback(h, FBS.get(s, []))
-        half[0] = 0
-
+                points(h)
+                keys(h)
         last = t == VI - 1
-        both = lambda nm: A(nm, 0, 16)
-        if not last:
-            for h in (1, 0):
-                tt(hc("FAR", h), HI(h, 7), A("TH", 0, 8, 1, (0, NL[h])), OP.is_ge)
-            mm(RW("FB", 0, 0, 8), EYE("TRI", 112), hc("FAR", 0))
-            mm(RW("FB", 1, 0, 8), EYE("TRI", 96), hc("FAR", 1), True, False)
-            mm(RW("FB", 1, 0, 8), A("ONB", 0, 96, 1, (0, 112)), hc("FAR", 0), False, True)
-            for h in (1, 0):
-                ts(hc("S0", h), RW("FB", h, 0, 8), float(CAP - 512), OP.is_lt)
-                tt(hc("DB", h), RW("FB", h, 0, 8), hc("KC2", h), OP.add)
-            tt(both("DB"), both("DB"), both("S0"), OP.mult)
-            tt(both("DST"), both("KC"), both("DB"), OP.add)
-            for h in (1, 0):
-                to_list(A("DST", 8 * h, 8 * h + 8), h)
-        ts(both("LWL"), A("H", 7, 128, 8), 4095, OP.bitwise_and)
-        ts(A("LW"), A("H"), 4095, OP.bitwise_and)
-        ts(A("LD0"), A("LW"), 0, OP.is_equal)
-        cp(A("LF"), A("LW"))
-        cp(A("LF", 0, 128, 8), both("NB"))
-        scan(A("LS"), A("LD0"), A("LF"), OP.mult, OP.add)
-        res = A("LS", 6, 128, 8)
-        ts(both("N1"), res, 0.0, OP.max)
-        ts(both("B1"), res, 0.0, OP.is_gt, 4096.0 * rank, OP.mult)
-        tt(both("B1"), both("B1"), both("N1"), OP.add)
-        tt(both("B1"), both("B1"), both("N1"), OP.add)
-        tt(both("B1"), both("B1"), res, OP.subtract)
-        ts(both("Z1"), both("LWL"), 0, OP.is_equal)
-        tt(both("N1"), both("N1"), both("Z1"), OP.mult)
-        tt(both("NOD"), both("N1"), both("LWL"), OP.add)
-        tt(both("B1"), both("B1"), both("Z1"), OP.mult)
-        ts(both("Z1"), both("Z1"), -4096.0 * rank, OP.mult, 4096.0 * rank, OP.add)
-        tt(both("B1"), both("B1"), both("LWL"), OP.add)
-        tt(both("BST"), both("B1"), both("Z1"), OP.add)
-        if not last:
-            for h in (1, 0):
-                list_copy(A("DL", 7 * h, 7 * h + NL[h] // 16), h)
-            w1, w2 = (ind(A("SEND%d" % t, a, a + 368), A("DL", 0, 13)) for a in (0, 368))
-            cp(w1, q(0, L))
-            for h in (1, 0):
-                ts(A("MI", 128 * h, 128 * h + 128, 16, (0, NL[h])), SI(h, 8, 16), 16, OP.logical_shift_right)
-            cp(both("BEST"), both("BST"))
-            ts(A("MI", 1, 256, 16), both("BEST"), 63, OP.bitwise_and)
-            ts(A("MI", 2, 256, 16), both("BEST"), 6, OP.logical_shift_right, 63, OP.bitwise_and)
-            ts(A("MI", 3, 256, 16), both("BEST"), 12, OP.logical_shift_right)
-            cp(A("ML"), A("MI"))
-
-            def to_gp(z="ZB0", ml="ML"):
-                for h in (1, 0):
-                    mm(A(z, K0[h], K0[h] + NL[h]), A(ml, 128 * h, 128 * h + 128, 1, (0, NL[h])), EYE("IB", NL[h]))
-            to_gp()
-            act(A("MG"), A("ZB0", 0, L), AF.Copy)
-            cp(w2, A("MG"))
-            dst = cores[(rank + 1) % n]
-            hop = hop_of(core, dst, cores, topo)
-            rid, pid = topo.addr(hop, core)
-            m = some(topo.engines(core, hop))
-
-            def send(x, a, b):
-                s, d = A("SEND%d" % t, a, a + CAP), A("LAND%d" % t, b, b + CAP)
-                ra, rl = T.sem["a%s%d" % (x, t)], T.sem["l%s%d" % (x, t)]
-                op("g", lambda: g.remote_dma(d[0], s[0], ra, rl, pid, rid, m), [s], [], "r", rl, 8, 1.0)
-            send("q", 208, 0)
-            send("m", 576, CAP)
-        for h in (1, 0):
-            ts(A("OUTL", 16 * h, 16 * h + 8, 1, (0, NL[h])), SI(h, 8, 16), 1.0 / 65536, OP.mult)
-            cp(A("OUTL", 16 * h + 8, 16 * h + 16, 1, (0, NL[h])), hc("BST", h))
-            mm(A("ZB1", K0[h], K0[h] + NL[h], 1, (0, 16)), A("OUTL", 16 * h, 16 * h + 16, 1, (0, NL[h])), EYE("IF", NL[h]))
-        yo = A("YO", t * L, t * L + L)
-        act(yo, A("ZB1", 0, L, 1, (0, 16)), AF.Copy)
-        dma("y", T.yr[:, t * L:t * L + L], A("YO", t * L, t * L + L, 1, (0, 8))[0], [yo], [])
-        dma("y", T.yb[:, t * L:t * L + L], A("YO", t * L, t * L + L, 1, (8, 16))[0], [yo], [])
+        for h in (0, 1):
+            lead[0] = 1 - h
+            nl = NL[h]
+            ts(HB("TI", h), ind(HB("SC", h, 0, 144 * 5 + 136), A("LH")), 0.25, OP.mult, -C0, OP.add)
+            ts(HB("TI", h), HB("TI", h), 4095, OP.bitwise_and)
+            ts(RW("LZ", h), RW("TI", h), 0, OP.is_equal)
+            cp(RW("LF", h), RW("TI", h))
+            cp(RW("LF", h, 0, 64, 8), RW("RN", h))
+            scan(RW("LS", h), RW("LZ", h), RW("LF", h), OP.mult, OP.add)
+            look(h, ST + 1)
+            t6 = LAST("SC", h, 144 * 6, nl)
+            if not last:
+                tt(RW("FAR", h), t6, A("THK", 0, 8, 1, (0, nl)), OP.is_ge)
+                o = PS("FB", h, 304, 312, 1, nl)
+                mm(o, EYE("TRI", nl), RW("FAR", h), True, h == 0)
+                if h:
+                    mm(o, A("ONB", 0, nl, 1, (0, NL[0])), RW("FAR", 0), False, True)
+                ts(RW("NZ2", h, 15, 143, 16), o, 512.0, OP.add, A("KC", h, h + 1, 1, (0, nl)), OP.min)
+                to_list("DL", h, "NZ2", "SJ1", 0.0)
+                cp(ind(A("SQ%d" % t), HB("DL", h, 0, nl // 16)), qh(h))
+            ts(RW("T6", h), t6, 0.25, OP.mult, -C0, OP.add)
+            tt(RW("NI", h), t6, FIRST("RD", h, 0, nl), OP.is_ge)
+            ts(RW("N6", h), RW("T6", h), 4095, OP.bitwise_and)
+            tt(RW("ZN", h), RW("NI", h), RW("LS", h, 5, 64, 8), OP.mult)
+            tt(RW("N", h), RW("ZN", h), RW("N6", h), OP.add)
+            if not last:
+                ts(RW("NZ", h, 15, 143, 16), RW("N", h), float(MID), OP.subtract)
+                to_list("NLT", h, "NZ", "SJ1", float(MID))
+                cp(HB("GG", h, 0, nl), ind(A("CH"), HB("NLT", h, 0, nl // 16)))
+            ts(RW("RHO", h), RW("T6", h), 16, OP.logical_shift_right)
+            cp(RW("ML", h, 0, 128, 16), RW("RHO", h))
+            ts(RW("Z0", h), RW("N", h), 0.0, OP.is_equal)
+            tt(RW("Z0", h), RW("Z0", h), RW("BIN", h), OP.mult)
+            tt(RW("ML", h, 1, 128, 16), RW("Z0", h), RW("N", h), OP.add)
+            if not last:
+                o = PS("ZB", h, 0, nl)
+                mm(o, RW("ML", h), EYE("IF", nl))
+                act(A("MG", K0[h], K0[h] + nl), o, AF.Identity, 1.0, A("BIAS"))
+                cp(ind(A("SM%d" % t), HB("DL", h, 0, nl // 16)), A("MG", K0[h], K0[h] + nl))
+            for j in (0, 1):
+                o = PS("ZB", h, 128 + 128 * j, 128 + 128 * j + nl, 1, 8)
+                a = (j * VI + t) * L + K0[h]
+                mm(o, RW("ML", h, j, 128, 16), EYE("IF", nl))
+                act(A("YO", a, a + nl), o, AF.Identity, 1.0, 4096.0 * rank * j)
+        lead[0] = 0
+        for j, y in ((0, T.yr), (1, T.yb)):
+            yo = A("YO", (j * VI + t) * L, (j * VI + t + 1) * L)
+            dma("y", y[:, t * L:t * L + L], yo[0], [yo], [])
         if last:
             break
-        for h in (1, 0):
-            to_list(A("NOD", 8 * h, 8 * h + 8), h)
+        dst = cores[(rank + 1) % n]
+        hop = hop_of(core, dst, cores, topo)
+        rid, pid = topo.addr(hop, core)
+        m = some(topo.engines(core, hop))
+
+        def send(x):
+            s, d = A("S%s%d" % (x.upper(), t), 0, CAP), A("L%s%d" % (x.upper(), t))
+            ra, rl = T.sem["a%s%d" % (x, t)], T.sem["l%s%d" % (x, t)]
+            op("g", lambda: g.remote_dma(d[0], s[0], ra, rl, pid, rid, m), [s], [], "r", rl, 8, 1.0)
+        send("q")
+        send("m")
         cp(A("PT", M + t * L, M + t * L + L), q(0, L))
-        for h in (1, 0):
-            list_copy(A("NLT", 7 * h, 7 * h + NL[h] // 16), h)
-        act(A("GG"), ind(A("CH"), A("NLT", 0, 13)), AF.Copy)
-        for h in (1, 0):
-            ts(RW("BI", h), HI(h, 7), 20, OP.logical_shift_right)
+        for h in (0, 1):
+            lead[0] = 1 - h
+            nl, k0 = NL[h], K0[h]
+            ts(RW("BI", h), RW("T6", h), 20, OP.logical_shift_right)
             tt(HB("OL", h), ind(HB("BI", h), A("BCL")), A("RI"), OP.is_equal)
-            mm(A("ZB0", 256 + K0[h], 256 + K0[h] + NL[h]), RW("OL", h), EYE("IB", NL[h]))
-        ob = A("ZB0", 256, 256 + L)
-        ts(A("BN"), A("KN"), float(t * L), OP.add)
-        tt(A("BN"), A("BN"), ob, OP.mult)
-        ts(A("BX"), ob, A("C4K1"), OP.mult, -1.0, OP.add)
-        tt(A("EE"), A("GG"), A("BX"), OP.is_equal)
-        for h in (1, 0):
-            mm(RW("SP", h, 0, 8), A("EE", K0[h], K0[h] + NL[h]), A("R8"))
-        cp(both("NCI"), both("NOD"))
-        ts(A("MCJ", 3, 256, 16), both("NCI"), 63, OP.bitwise_and)
-        ts(A("MCJ", 4, 256, 16), both("NCI"), 6, OP.logical_shift_right)
-        cp(A("ML2"), A("MCJ"))
-        to_gp("ZB1", "ML2")
-        act(A("MGN"), A("ZB1", 0, L), AF.Copy)
-        ts(both("FARS"), both("FAR"), 1.0 / 65536, OP.mult)
-        tt(both("LOF"), A("MCJ", 3, 256, 16), both("FARS"), OP.mult)
-        tt(both("HIF"), A("MCJ", 4, 256, 16), both("FARS"), OP.mult)
-        tt(both("YPL"), both("FARS"), both("NOD"), OP.mult)
-        for h in (1, 0):
-            for j, nm in ((1, "LOF"), (2, "HIF")):
-                tt(A("ML3", 128 * h + j, 128 * h + 128, 16, (0, NL[h])), RW("SP", h, 0, 8), hc(nm, h), OP.mult)
-        to_gp("ZB0", "ML3")
-        act(A("MG"), A("ZB0", 0, L), AF.Copy)
-        for h in (1, 0):
-            cp(hc("CAN", h), RW("SP", h, 0, 8))
-        tt(both("YPL"), both("YPL"), both("CAN"), OP.mult)
-        ts(both("DA"), both("YPL"), 0.0, OP.is_gt)
-        tt(both("DA"), both("DA"), both("KJ"), OP.mult)
-        tt(both("GD"), both("YPL"), both("DA"), OP.subtract)
-        banks, z = ("FB0", "FB1", "ZB0", "ZB1"), 0
-        for gr in range(8):
-            lg = gr * L
-            ts(A("LG", lg, lg + L), A("MGN"), A("GMF", gr, gr + 1), OP.mult)
-            for h in (1, 0):
-                nl, w = NL[h], K0[h] + NL[h]
-                o = A(banks[z % 4], 0, w, 1, (0, nl))
-                z += 1
-                mm(o, A("LG", lg + K0[h], lg + w), A("MG", 0, w), True, False)
-                mm(A(o[1], K0[h], w, 1, (0, nl)), EYE("IB", nl), A("TRP", 0, nl, 1, (0, nl)), False, True)
-                least(A("DMIN", 8 * h + gr, 8 * h + gr + 1, 1, (0, nl)), o)
-        ts(both("DMIN"), both("DMIN"), 0.0, OP.is_gt)
-        tt(both("GD"), both("GD"), both("DMIN"), OP.mult)
-        tt(both("DST"), both("KJ"), both("GD"), OP.add)
-        tt(both("YPL"), both("YPL"), both("DMIN"), OP.mult)
-        for h in (1, 0):
-            to_list(A("DST", 8 * h, 8 * h + 8), h)
-        for h in (1, 0):
-            list_copy(A("DL2", 7 * h, 7 * h + NL[h] // 16), h)
-        tt(ind(A("CH"), A("DL2", 0, 13)), A("GG"), A("BN"), OP.add)
-        for h in (1, 0):
-            mm(A("ZB1", K0[h], K0[h] + NL[h], 1, (0, 8)), hc("YPL", h), EYE("IF", NL[h]))
+            ob, bn = PS("KEY", h, 0, nl), PS("KEY", h, 128, 128 + nl)
+            mm(ob, RW("OL", h), EYE("IB", nl))
+            mm(bn, RW("OL", h), RW("DG", h, 0, nl), True, False)
+            mm(bn, RW("OL", h), EYE("IS%d" % t, nl), False, True)
+            ga = PS("ZB", h, 384, 384 + nl)
+            mm(ga, RW("NZ", h, 0, 128), EYE("IH", nl))
+            cp(A("GA", k0, k0 + nl), ga)
+            for gr in range(8):
+                ts(A("LG", gr * L + k0, gr * L + k0 + nl), A("GA", k0, k0 + nl), A("GM", gr, gr + 1), OP.mult,
+                   A("GO", gr, gr + 1), OP.add)
+            tt(RW("FN", h), RW("FAR", h), RW("N", h), OP.mult)
+            tt(HB("EE", h, 0, nl), HB("GG", h, 0, nl), ob, OP.is_lt)
+            tt(HB("NEW", h, 0, nl), HB("GG", h, 0, nl), bn, OP.add)
+            can = PS("KEY", h, 256, 264, 1, nl)
+            mm(can, HB("EE", h, 0, nl), A("R1"))
+            tt(RW("YPL", h), can, RW("FN", h), OP.mult)
+            ts(RW("MB", h, 14, 128, 16), RW("YPL", h), -1.0, OP.mult, float(MID), OP.add)
+            ts(RW("YH", h), RW("YPL", h), float(MID), OP.subtract)
+            gb = PS("KEY", h, 272, 272 + nl)
+            mm(gb, RW("MB", h), EYE("IH", nl))
+            ts(A("GB", k0, k0 + nl), gb, A("O15"), OP.add)
+            banks = (("ZB0", "KEY0"), ("SP0", "SP1", "ZB1", "KEY1"))[h]
+            for gr in range(8):
+                w, z = k0 + nl, banks[gr % len(banks)]
+                o = A(z, 0, w, 1, (0, nl))
+                mm(o, A("LG", gr * L + k0, gr * L + w), A("GB", 0, w), True, False)
+                mm(A(z, k0, w, 1, (0, nl)), EYE("IB", nl), A("TRP", 0, nl, 1, (0, nl)), False, True)
+                least(RW("DMIN", h, gr, gr + 1), o)
+            tt(RW("DMIN", h), RW("DMIN", h), RW("YPL", h), OP.min)
+            ts(RW("UU", h), RW("DMIN", h), -4096.0, OP.mult, A("KJ", h, h + 1, 1, (0, nl)), OP.add)
+            tt(RW("NZ2", h, 15, 143, 16), RW("UU", h), RW("YH", h), OP.max)
+            to_list("DL2", h, "NZ2", "SJ1", float(MID))
+        for h in (0, 1):
+            lead[0] = 1 - h
+            nl = NL[h]
+            cp(ind(A("CH"), HB("DL2", h, 0, nl // 16)), HB("NEW", h, 0, nl))
+            ts(RW("YP", h), RW("DMIN", h), 4096.0, OP.mult)
+            tt(RW("YP", h), RW("YP", h), RW("YPL", h), OP.min)
+            o = PS("FB", h, 320, 320 + nl, 1, 8)
+            mm(o, RW("YP", h), EYE("IF", nl))
+            act(A("YPO", t * L + K0[h], t * L + K0[h] + nl), o, AF.Copy)
+        lead[0] = 0
         yo = A("YPO", t * L, t * L + L)
-        act(yo, A("ZB1", 0, L, 1, (0, 8)), AF.Copy)
         dma("y", T.yp[:, t * L:t * L + L], yo[0], [yo], [])
 
     if not PLAN:
@@ -610,7 +615,8 @@ def plan(ops):
 
     N = len(ops)
     tag = [o[0] if o[4] == "c" else "a%d" % i for i, o in enumerate(ops)]
-    hist, deps, sent, pool = {}, [], [], []
+    in_line = lambda i, j: tag[i] == tag[j] == "t" or tag[i][:5] == tag[j][:5] in ("loady", "loads")
+    hist, deps, sent, pool, loads = {}, [], [], [], {}
     for i in range(N):
         R, Wr, kind, dep = ops[i][2], ops[i][3], ops[i][4], set()
         for lst, w in ((R, False), (Wr, True)):
@@ -626,6 +632,10 @@ def plan(ops):
             dep.add(sent[-2 if ops[i - 1][4] != "x" else -1])
         if kind == "r":
             sent.append(i)
+        if kind == "d" and Wr:
+            tag[i] = "load" + ops[i][0] + tag[i]
+            dep.update(loads.get(ops[i][0], []))
+            loads[ops[i][0]] = [i]
         deps.append(dep)
         for lst, w in ((R, False), (Wr, True)):
             for r in lst:
@@ -634,15 +644,20 @@ def plan(ops):
                     h[:] = []
                 elif w and r[6] == 1:
                     h[:] = [e for e in h if not (r[2] <= e[1][2] and e[1][3] <= r[3] and r[4] <= e[1][4] and e[1][5] <= r[5])]
+                elif w:
+                    h[:] = [e for e in h if e[1][1:] != r[1:]]
                 h.append((i, r, w))
     after = [{"c": 0.18, "d": 2.2, "r": 6.0, "x": 0.1}[o[4]] for o in ops]
+    for i in range(N):
+        if ops[i][4] == "d" and ops[i][3]:
+            after[i] += (ops[i][3][0][5] - ops[i][3][0][4]) * 0.003
     nxt = [[] for _ in range(N)]
     for i in range(N):
         for j in deps[i]:
-            nxt[j].append((i, tag[i] == tag[j] == "t"))
+            nxt[j].append((i, in_line(i, j)))
     way = [0.0] * N
     for i in range(N - 1, -1, -1):
-        way[i] = ops[i][7] + after[i] + max([way[k] for k, st in nxt[i]] or [0.0])
+        way[i] = ops[i][7] + max([way[k] + (0.0 if st else after[i]) for k, st in nxt[i]] or [after[i]])
     best = None
     for bias, noise, hold, seed in TRIES:
         order, when, end = in_time(ops, deps, nxt, after, way, bias, noise, hold, seed)
@@ -659,7 +674,7 @@ def plan(ops):
             num[i] = seq[q]
         k, mine, last = known[q], [], {}
         for j in deps[i]:
-            if ops[i][4] == "x" or tag[j] == tag[i] == "t":
+            if ops[i][4] == "x" or in_line(i, j):
                 continue
             if tag[j] not in last or num[last[tag[j]]] < num[j]:
                 last[tag[j]] = j
@@ -674,7 +689,7 @@ def plan(ops):
         waits[i] = mine
         snap[i] = dict(k)
         snap[i][tag[i]] = num[i]
-    return {"order": order, "waits": waits, "need": need}
+    return {"order": order, "waits": waits, "need": need, "end": best[0]}
 
 
 def in_time(ops, deps, nxt, after, way, bias, noise, hold, seed):

@@ -10,10 +10,21 @@ U = float(2 ** 18)
 RC = 7.5 + 1.0 / 256
 C0 = RC * 65536
 NONE = -(4096.0 - MID / 4096.0)
-CYC, TCY = 0.00095, 0.0006
-VS = {0: ((0, 24), (24, 48)), 1: ((0, 20), (20, 40))}
-SS = {0: ((48, 70), (70, 92), (92, 112)), 1: ((40, 60), (60, 78), (78, 96))}
-TRIES = [(0.4 * b, 0.3 * (s > 1), 1e-9, s) for b in range(12) for s in range(1, 13)]
+HW = 1040.0
+CYC, TCY = 0.0009, 0.00045
+XV = {0: (56, 56, 48, 48, 48, 60), 1: (48, 44, 36, 32, 32, 48)}
+
+
+def shares(h, s):
+    x, n = XV[h][s], NL[h]
+    m = x + (n - x + 2) // 4 * 2
+    return ((0, x // 4 * 2), (x // 4 * 2, x)), ((x, m), (m, n))
+
+
+TRIES = [(0.8 * b, 0.3 * (s > 1), 1e-9, s) for b in range(6) for s in range(1, 4)]
+ROUNDS, NOISE, SWAPS = 12, 0.03, 1500
+ONV = ("XB", "X2", "X3")
+KS = {0: ((0, 112),), 1: ((0, 96),)}
 
 SCRATCH = {"PT": ("sbuf", [128, W], "bfloat16"), "QA": ("sbuf", [128, VI * L], "bfloat16"), "CH": ("sbuf", [128, CW], "int32"),
            "WI": ("sbuf", [128, 1], "int32"), "THI": ("sbuf", [128, 1], "int32"), "R0I": ("sbuf", [8, VI * L], "int32"),
@@ -21,9 +32,10 @@ SCRATCH = {"PT": ("sbuf", [128, W], "bfloat16"), "QA": ("sbuf", [128, VI * L], "
            "YPO": ("sbuf", [8, 2 * L], "float32")}
 for _h in ("0", "1"):
     SCRATCH["SQ" + _h] = ("sbuf", [128, 2 * L], "bfloat16")
-    SCRATCH["SM" + _h] = ("sbuf", [128, 2 * L], "float32")
+    SCRATCH["SG" + _h] = ("sbuf", [128, 2 * L], "float32")
+    SCRATCH["SM" + _h] = ("sbuf", [128, 48], "float32")
     SCRATCH["LQ" + _h] = ("sbuf", [128, CAP], "bfloat16")
-    SCRATCH["LM" + _h] = ("sbuf", [128, CAP], "float32")
+    SCRATCH["LM" + _h] = ("sbuf", [128, 48], "float32")
     for _n in ("KEY", "ZB", "FB", "SP"):
         SCRATCH[_n + _h] = ("psum", [128, 512], "float32")
 PSUMS = {n for n in SCRATCH if SCRATCH[n][0] == "psum"}
@@ -45,19 +57,19 @@ def _pool(big, dtype, halves, **bufs):
     SCRATCH[big] = ("sbuf", [128, at], dtype)
 
 
-_pool("ALLb", "bfloat16", dict(AD=144, DA=1792, DX=1024, Q16=1024, QT=128, A0=112, AS=144, XB=144, X2=144, X3=144, EA=144, EB=144,
-                               EC=144, ED=144, OL=128, EE=112, DG=112, FAR=8),
-      WZ=144, CR=288, ONB=144, SEG=144, IB=128, IN=128, I28=128, I13=128, R1=8, R16=16, R16N=16, REP=1792, TRI=128, TRP=112,
-      THB=128, IS0=112, IS1=112, FM=CAP, QF1=L, QF2=L, QC1=L, QC2=L, XG0=512, XG1=512, ID1=144, SJ=128)
+_pool("ALLb", "bfloat16", dict(XG=1536, DA=1792, DX=1792, QT=128, A0=112, A1=112, AS=144, XB=144, X2=144, X3=144, RB=136,
+                               EA=144, EB=144, EC=144, ED=144, OL=128, EE=112, DG=112, FAR=8),
+      WZ=144, CR=288, ONB=144, SEG=144, IB=128, IN=128, I28=128, I13=128, IU=128, R1=8, R1N=8, R16=16, R16N=16,
+      REP=1792, TRI=128, TRP=112, THB=128, IS0=112, IS1=112, FM=CAP, Q16=16 * 176, QF1=L, QF2=L, QC1=L, QC2=L, ID1=144, SJ=128)
 _pool("ALLf", "float32", dict(RD=144, RD0=144, SC2=144, FD=144, GD2=144, GD3=144, GD4=272, SC=1008, ML=128, X=144, Y0=144, Y1=144,
                               Y2=144, Y3=144, KM0=144, KM1=144, KM2=144, KM3=144, FS=272, RPF=24, DK=8, IM=8, RN=8, G23=8, FX=8,
-                              LF=64, LZ=64, LS=64, NI=8, ZN=8, N=8, Z0=8, BIN=8, GG=112, NEW=112, FN=8, YPL=8, YH=8, DMIN=8,
+                              LF=64, LZ=64, LS=64, NI=8, ZN=8, N=8, Z0=8, BIN=8, GG=112, NEW=112, FN=8, YPL=8, DMIN=8,
                               UU=8, YP=8, M1=8),
-      TD=144, MW=24, ONF=128, IF=128, WF=1, THF=1, THK=8, KK=2, KC=2, KJ=2, GM=8, GO=8, O15=1, BIAS=1, MG=L, ICOL=1, JF=9,
+      TD=144, MW=24, ONF=128, IF=128, WF=1, THF=1, THK=8, KK=2, KC=2, KJ=2, BIAS=1, MG=L, ICOL=1, JF=9,
       G17=9, J0=9, B1=1, B2=1, J34=4)
 _pool("ALLi", "int32", dict(NN=8, DI=8, RHO=8, TI=64, T6=8, N6=8, BI=8, RT=8), PI=4, RI=128, GI=9, BCI=8, RS=16)
-_pool("ALLu", "uint16", dict(P16=112, LT=8, DL=8, NLT=8, DL2=8), LX=10, L0=10, LH=4, BCL=8)
-_pool("ALLh", "float16", dict(NZ=144, NZ2=144, MB=128, PH=112), IDG=272, SJ1=128, SJ4=128, IH=112, GA=L, GB=L, LG=8 * L)
+_pool("ALLu", "uint16", dict(P16=112, LT=8, DL=8, NLT=8, DL2=8), LX=10, LE=10, L0=10, LH=4, BCL=8)
+_pool("ALLh", "float16", dict(AD=144, RR=144, NZ=144, NZ2=144, MA=256, MB=256, GA=224, GB=224, PH=112), IDG=272, SJ1=128, SJ4=128, SJN=128, IH=112)
 SEMAPHORES = ["cv", "cs", "ct", "cg", "aq0", "aq1", "am0", "am1", "lq0", "lq1", "lm0", "lm1"] + ["d%d" % i for i in range(24)]
 PLAN = {}
 
@@ -70,7 +82,7 @@ def hop_of(src, dst, cores, topo):
 
 
 def some(engines):
-    return sum(1 << e for e in engines[:8])
+    return sum(1 << e for e in engines[::len(engines) // 8])
 
 
 def rank_program(g, core, T, topo):
@@ -90,7 +102,7 @@ def rank_program(g, core, T, topo):
                     g.wait_ge(T.sem["l" + t], 8)
         return
 
-    ops, lead, ndma, turn = [], [0], [0], [0]
+    ops, lead, ndma, turn, phase = [], [0], [0], [0], [0]
     QUE = {"v": g.vector, "s": g.scalar, "t": g.tensor, "g": g, "y": g.sync}
     SEM = {"v": T.sem.cv, "s": T.sem.cs, "t": T.sem.ct, "g": T.sem.cg}
 
@@ -141,7 +153,7 @@ def rank_program(g, core, T, topo):
             Wr.append(x[1] if is_ind(x) else x)
             if is_ind(x):
                 R.append(x[2])
-        ops.append((q, fn, R, Wr, kind, sem, val, c, lead[0]))
+        ops.append((q, fn, R, Wr, kind, sem, val, c, lead[0], phase[0]))
 
     def call(q, what, fn, out, *ins):
         op(q, fn, ins, [out], c=cost(q, what, out, ins))
@@ -241,12 +253,17 @@ def rank_program(g, core, T, topo):
     ts(A("R16", 0, 8), A("R1"), U, OP.mult)
     ts(A("R16", 8, 16), A("R1"), -16.0, OP.mult)
     ts(A("R16N"), A("R16"), -1.0, OP.mult)
+    ts(A("R1N"), A("R1"), -1.0, OP.mult)
     cp(A("IF"), A("IB"))
     fill(A("SEG", 0, 136, 17), 0.0)
-    fill_all(both("AD"), -16.0)
-    fill_all(both("RD") + both("RD0"), -BIG)
+    fill_all(both("RD"), -BIG)
+    fill_all(both("RD0"), 0.0)
+    for h in (0, 1):
+        for nm, v in (("AD", -16.0), ("RR", 0.0)):
+            ts(HB(nm, h), A("ONB"), v, OP.mult)
+            ts(HB(nm, h, 1, 136, 17), A("ONB", 0, 8), -HW, OP.mult)
     fill(A("CR", 0, 136, 1, (32, 33)), 4.0 * (MID + 256))
-    fill(A("CR", 0, 136, 17, (0, 1)), -BIG)
+    fill(A("CR", 0, 136, 17, (0, 1)), -BIG * 32768)
     fill(A("CR", 136, 272, 17, (0, 1)), BIG)
     ts(A("IDG", 0, 136), A("ID1", 0, 136), 4.0, OP.mult)
     ts(A("IDG", 136, 272), A("ID1", 0, 136), -1.0 / 4096, OP.mult)
@@ -256,57 +273,61 @@ def rank_program(g, core, T, topo):
     ts(A("JF"), A("JF"), A("ICOL"), OP.add)
     ts(A("GI"), A("JF"), 1.0 / 17, OP.mult, -8.0 / 17, OP.add)
     ts(A("G17"), A("GI"), 17.0, OP.mult, 119.0, OP.min)
+    ts(A("IU"), A("IB"), -U, OP.mult)
     cp(A("L0", 0, 9), A("G17"))
+    ts(A("LE", 0, 9), A("G17"), 16.0, OP.add)
     tt(A("J0"), A("JF"), A("G17"), OP.is_equal)
     ts(A("J0"), A("J0"), 200.0, OP.mult, 16.0, OP.add)
     tt(A("J0"), A("J0"), A("G17"), OP.add)
     ts(A("LX", 0, 9), A("J0"), 136.0, OP.min)
+    for h in (0, 1):
+        fill(HB("SC", h, 144 + 136, 1008, 144), BIG)
+    ts(A("I13"), A("IB"), -8192.0, OP.mult)
 
     def radii(t):
         cp(A("R0F", t * L, t * L + L), A("R0I", t * L, t * L + L))
         for h in (0, 1):
             a, o = t * L + K0[h], PS("ZB", h, 448, 456, 1, NL[h])
             mm(o, A("R0F", a, a + NL[h]), A("IF", 0, 8, 1, (0, 8)))
-            ts(RW("RPF", h, 8 * t, 8 * t + 8), o, RC, OP.add, U, OP.mult)
+            act(RW("RPF", h, 8 * t, 8 * t + 8), o, AF.Identity, 1.0, HW)
     radii(0)
     fill(A("PT", 0, 1), 256.0)
     fill(A("TD"), BIG)
     fill(A("TD", 0, 136, 17), NONE)
     for h in (0, 1):
-        fill(HB("SC", h, 144 + 136, 1008, 144), BIG)
-        fill(HB("SC2", h, 136, 137), BIG)
         ts(HB("NZ", h), A("ONB"), 0.0, OP.mult)
     ts(A("SJ4"), A("SJ"), -4096.0, OP.mult)
 
     def later():
-        ts(A("I13"), A("IB"), -8192.0, OP.mult)
-        fill_all(both("FD") + both("GD2") + both("GD3") + both("GD4"), BIG)
+        even = lambda x, v: iota(x, [[0, size(x)]], v, 0, SIZES[x[1]][1] != "int32")
+        for nm in ("GD2", "FD", "GD3", "GD4"):
+            for h in (0, 1):
+                even(HB(nm, h), 8192)
+                if nm != "FD":
+                    o = HB(nm, h, 0, None, 17) if nm == "GD4" else FIRST(nm, h)
+                    act(o, A("ONF", 0, size(o)), AF.Copy, NONE)
         for h in (0, 1):
-            for nm in ("GD2", "GD3"):
-                fill(FIRST(nm, h), NONE)
-            fill(HB("GD4", h, 0, 272, 17), NONE)
-            fill(HB("SC", h, 0, 144), 4.0 * (C0 + 1))
+            even(HB("SC", h, 0, 144), int(4 * (C0 + 1)))
             for s in range(1, 5):
-                fill(HB("SC", h, 144 * s + 137, 144 * s + 144), 0.0)
+                even(HB("SC", h, 144 * s + 137, 144 * s + 144), 0)
             ts(HB("NZ2", h), A("ONB"), 0.0, OP.mult)
-            ts(HB("MB", h), A("ONB", 0, 128), 0.0, OP.mult)
-            fill(HB("BIN", h), -4096.0 * rank)
-            fill(HB("BI", h), 0)
-        fill_all(both("ML"), 0.0)
-        for h in (0, 1):
-            fill(HB("ML", h, 2, 128, 16), 1.0)
-        fill(A("MW"), 0.0)
+            for nm, j in (("MA", 1), ("MB", 0)):
+                ts(HB(nm, h), A("REP", 0, 256), 0.0, OP.mult)
+                ts(HB(nm, h, j, 256, 32), A("ONB", 0, 8), 4096.0, OP.mult)
+            even(HB("BIN", h), -4096 * rank)
+            even(HB("BI", h), 0)
+            even(HB("ML", h), 0)
+            act(HB("ML", h, 2, 128, 16), A("ONF", 0, 8), AF.Copy)
+        even(A("MW"), 0)
         iota(A("J34"), [[34, 4]], 0, 0, True)
         iota(A("BCI"), [[1, 8]], 0, 0)
         iota(A("RI"), [[0, 8], [1, 16]], 0, 0)
         asel(A("TRI"), A("ONB", 0, 128), [[1, 128]], OP.is_ge, 0.0, -1, -1)
         asel(A("TRI"), A("TRI"), [[1, 128]], OP.not_equal, -512.0, 0, -1)
-        fill(A("TRP"), 8192.0)
+        fill(A("TRP"), float(2 ** 25))
         asel(A("TRP"), A("TRP"), [[1, 112]], OP.is_ge, 0.0, 0, -1)
-        for c, j, v in ((0, 0, U), (0, 2, RC * U), (8, 2, BIG), (16, 1, 1.0)):
+        for c, j, v in ((0, 0, 1.0), (0, 2, HW), (8, 2, 4096.0), (16, 1, 1.0)):
             asel(A("MW", c, c + 8), A("MW", c, c + 8), [[-16, 8]], OP.not_equal, v, -j, 1)
-        asel(A("GM"), A("ONF", 0, 8), [[-16, 8]], OP.is_equal, 0.0, -15, 1)
-        asel(A("GO"), A("ONF", 0, 8), [[-16, 8]], OP.is_equal, 0.0, -14, 1)
         iota(A("KK"), [[112, 2]], 0, 1, True)
         iota(A("KC"), [[112, 2]], L, 1, True)
         iota(A("KJ"), [[112, 2]], W - MID, 1, True)
@@ -318,15 +339,16 @@ def rank_program(g, core, T, topo):
         cp(A("BCL"), A("BCI"))
         cp(A("SJ1"), A("SJ"))
         cp(A("IH"), A("IB", 0, 112))
-        ts(A("O15"), A("ICOL"), 15.0, OP.is_equal)
+        ts(A("SJN"), A("SJ"), -1.0, OP.mult)
         ts(A("BIAS"), A("ICOL"), 1.0, OP.is_equal, 4096.0 * rank, OP.mult)
         for t in (0, 1):
             ts(HB("DG", t), A("IB", 0, 112), A("KK", t, t + 1), OP.mult)
             ts(A("IS%d" % t), A("IB", 0, 112), float(M + t * L), OP.mult)
-            fill(A("SQ%d" % t), -80.0)
-            fill(A("SM%d" % t), 0.0)
-            ts(A("QF%d" % (t + 1)), A("QA", (t + 1) * L, (t + 2) * L), 64.0, OP.subtract)
-            cp(A("QC%d" % (t + 1), CAP, L), A("QA", (t + 1) * L + CAP, (t + 2) * L))
+            even(A("SQ%d" % t), -80)
+            even(A("SG%d" % t), 0)
+            even(A("SM%d" % t), 0)
+            act(A("QF%d" % (t + 1)), A("QA", (t + 1) * L, (t + 2) * L), AF.Identity, 1.0, -64.0)
+            act(A("QC%d" % (t + 1), CAP, L), A("QA", (t + 1) * L + CAP, (t + 2) * L), AF.Copy)
             radii(t + 1)
         cp(A("THF"), A("THI"))
         ts(A("THB"), A("ONB", 0, 128), A("THF"), OP.mult)
@@ -344,37 +366,47 @@ def rank_program(g, core, T, topo):
         cp(HB("P16", h, 0, NL[h]), ind(A("CH", 0, top), HB("LT", h, 0, NL[h] // 16)))
         ts(HB("PH", h, 0, NL[h]), HB("P16", h, 0, NL[h]), float(MID), OP.subtract)
 
-    def masks(h, lev, rd):
-        y = HB("Y%d" % min(lev, 3), h)
-        scan(HB("AS", h), A("SEG"), HB("AD", h), OP.mult, OP.add)
-        act(y, HB("AS", h), AF.Abs, U, -7.5 * U)
-        tt(HB("XB", h), ind(HB(rd, h, 0, 136), A("L0", 0, 9)), y, OP.is_lt)
+    def outside(h, out, lev, c, root=False):
+        if out in ONV:
+            tt(HB(out, h), ind(HB("RD0" if root else "RD", h, 0, 136), A("L0", 0, 9)), HB("Y%d" % lev, h), OP.is_lt)
+            return
+        out = HB(out, h, 0, 136)
+        o = PS("ZB", h, 136 * c, 136 * c + 136)
+        mm(o, A("IU"), HB("RB", h), True, False)
+        mm(o, A("IF"), HB("Y%d" % lev, h, 0, 136), False, True)
+        act(out, o, AF.Relu, 2.0 / U, -16.0)
 
-    def points(h):
-        for c in range(3):
-            a, b = SS[h][c]
-            z = turn[0] = 1 - turn[0]
+    def masks(h, lev):
+        if "XB" not in ONV or (lev in FBS and "X2" not in ONV):
+            scan(HB("RB", h), A("SEG", 0, 136), HB("RR", h, 0, 136), OP.mult, OP.add)
+        scan(HB("AS", h), A("SEG"), HB("AD", h), OP.mult, OP.add)
+        act(HB("Y%d" % min(lev, 3), h), HB("AS", h), AF.Abs, U, -7.5 * U)
+        outside(h, "XB", min(lev, 3), 0, lev == 0)
+
+    def points(h, s):
+        vs, ss = shares(h, s)
+        for c, (a, b) in enumerate(ss):
             w = 16 * (b - a)
-            x, o = A("XG%d" % z, 0, w), PS("SP", z, 0, w)
+            x, o = HB("XG", h, 512 * c, 512 * c + w), A(("SP0", "SP1", "ZB%d" % h)[c], 0, w)
             act(x, ind(A("PT"), HB("P16", h, a, b)), AF.Copy)
             mm(o, RW("QT", h), A("REP", 16 * a, 16 * b, 1, (0, NL[h])), True, False)
             mm(o, A("IB"), x, False, True)
             act(HB("DA", h, 16 * a, 16 * b), o, AF.Abs)
-            if c < 2:
-                a, b = VS[h][c]
-                d = HB("DX", h, 16 * a, 16 * b)
-                tt(d, ind(A("PT"), HB("P16", h, a, b)), HB("Q16", h, 16 * a, 16 * b), OP.add)
-                ts(HB("DA", h, 16 * a, 16 * b), d, 0.0, OP.max, 2.0, OP.mult)
+        for a, b in vs:
+            d, z = HB("DX", h, 16 * a, 16 * b), K0[h]
+            tt(d, ind(A("PT"), HB("P16", h, a, b)), A("Q16", 16 * (z + a), 16 * (z + b)), OP.subtract)
+            ts(HB("DA", h, 16 * a, 16 * b), d, 0.0, OP.max, 2.0, OP.mult)
 
-    def keys(h):
-        nl, x = NL[h], VS[h][-1][1]
+    def keys(h, s):
+        nl, a, b = NL[h], 0, XV[h][s]
         mm(PS("KEY", h, 0, 280, 1, nl), A("ONB", 0, nl, 1, (0, 33)), A("CR", 0, 280, 1, (0, 33)), True, False)
         mm(PS("KEY", h, 0, 272, 1, nl), HB("PH", h, 0, nl), A("IDG"), False, False)
         for i in range(16):
-            mm(PS("KEY", h, i + 1, 272, 17, x), HB("DX", h, i, 16 * x, 16), A("R16N"), False, False)
+            mm(A("KEY%d" % h, i + 1, 272, 17, (a, b)), HB("DX", h, 16 * a + i, 16 * b, 16), A("R16N"), False, False)
         mm(PS("KEY", h, 0, 136, 1, nl), EYE("I28", nl), RW("XB", h, 0, 136), False, False)
-        for i in range(16):
-            mm(PS("KEY", h, i + 1, 272, 17, nl), HB("DA", h, i, 16 * nl, 16), A("R16"), False, i == 15)
+        for a, b in KS[h]:
+            for i in range(16):
+                mm(A("KEY%d" % h, i + 1, 272, 17, (a, b)), HB("DA", h, 16 * a + i, 16 * b, 16), A("R16"), False, i == 15)
 
     FBS = {2: [(0, "X2", ("EA",))], 3: [(1, "X2", ("EB",))], 4: [(2, "X2", ("EC",)), (0, "X3", ("EA", "ED"))]}
 
@@ -391,12 +423,12 @@ def rank_program(g, core, T, topo):
         tt(HB("NZ", h, 15, 143, 16), LAST("SC2", h), HB("NN", h), OP.add)
         to_list("LT", h, "NZ", "SJ4", float(MID))
         kids(h)
-        ts(HB("RHO", h), LAST("SC", h, a), 1.0 / U, OP.mult, -8.0, OP.add)
-        ts(FIRST("RD", h), HB("RHO", h), RC, OP.add, U, OP.mult)
-        ts(HB("DI", h), HB("NN", h), 4, OP.logical_shift_right)
-        ts(FIRST("AD", h), HB("DI", h), 16.0, OP.add)
-        masks(h, s, "RD")
-        sel = ind(HB("SC2", h, 0, 137), A("LX", 0, 9))
+        phase[0] += 3
+        ts(FIRST("RR", h), LAST("SC", h, a), 1.0 / U, OP.mult, HW - 8.0, OP.add)
+        ts(FIRST("RD", h), FIRST("RR", h), RC - HW, OP.add, U, OP.mult)
+        ts(FIRST("AD", h), LAST("SC2", h), -1.0 / 16, OP.mult, HW - 0.47, OP.add)
+        masks(h, s)
+        sel = ind(HB("SC2", h, 0, 136), A("LE", 0, 9))
         if s <= 3:
             tt(HB({1: "EA", 2: "EB", 3: "EC"}[s], h), sel, HB(km, h), OP.is_equal)
         if s == 3:
@@ -404,12 +436,12 @@ def rank_program(g, core, T, topo):
         if s not in FBS:
             return
         gd = "GD%d" % s
-        ts(LAST(gd, h), HB("NN", h), 64.0, OP.mult, -256000.0, OP.add)
+        ts(LAST(gd, h), LAST("SC2", h), -64.0, OP.mult, -256000.0, OP.add)
         if s == 4:
             tt(HB("G23", h), LAST("GD2", h), LAST("GD3", h), OP.max)
             tt(LAST(gd, h, 136), HB("G23", h), LAST(gd, h), OP.min)
         for c, (l, x, es) in enumerate(FBS[s]):
-            tt(HB(x, h), ind(HB("RD", h, 0, 136), A("L0", 0, 9)), HB("Y%d" % l, h), OP.is_lt)
+            outside(h, x, l, c + 1)
             o = PS("FB", h, 136 * c, 136 * c + 136)
             mm(o, A("IF"), HB("KM%d" % l, h, 0, 136), True, False)
             for e in es + (x,):
@@ -426,6 +458,7 @@ def rank_program(g, core, T, topo):
         q = lambda a, b, st=1: A(QN[t], a, b, st)
         qh = lambda h: q(K0[h], K0[h] + NL[h])
         fq = "QF%d" % t if t else "QA"
+        phase[0] = 100 * t
         if t:
             lq, lm = "LQ%d" % (t - 1), "LM%d" % (t - 1)
             op("x", None, [], [A(lq)], "x", T.sem["aq%d" % (t - 1)], 8)
@@ -433,6 +466,9 @@ def rank_program(g, core, T, topo):
             tt(A(fq, 0, CAP), A(fq, 0, CAP), A(lq), OP.max)
             ts(A("FM"), A(fq, 0, CAP), 0.0, OP.is_lt, 64.0, OP.mult)
             tt(q(0, CAP), A("FM"), A(fq, 0, CAP), OP.add)
+        hi = K0[1] + max(XV[1])
+        for i in range(16):
+            cp(A("Q16", i, 16 * hi, 16), q(0, hi))
         o = PS("FB", 0, 288, 301)
         for j in range(16):
             mm(o, A("WZ", 15 - j, 143 - j), A(fq, j, L, 16), j == 0, j == 15)
@@ -442,63 +478,67 @@ def rank_program(g, core, T, topo):
             lead[0] = 1 - h
             nl = NL[h]
             ts(HB("LT", h, 0, nl // 16), A("RS", 7 * h, 7 * h + nl // 16), 1.0, OP.add)
-            mm(PS("ZB", h, 0, 128, 1, nl), qh(h), A("IN"))
-            act(RW("QT", h), PS("ZB", h, 0, 128, 1, nl), AF.Copy)
-            for a, b in VS[h]:
-                z = turn[0] = 1 - turn[0]
-                o = PS("SP", z, 0, 16 * (b - a))
-                mm(o, RW("QT", h), A("REP", 16 * a, 16 * b, 1, (0, nl)))
-                act(HB("Q16", h, 16 * a, 16 * b), o, AF.Copy)
+            o = PS("ZB", h, 0, 128, 1, nl)
+            mm(o, qh(h), A("IN"))
+            act(RW("QT", h), o, AF.Copy)
             kids(h, 80)
-            a0 = HB("A0", h, 0, nl)
+            a0, a1 = HB("A0", h, 0, nl), HB("A1", h, 0, nl)
             tt(a0, ind(A("PT", 0, 80), HB("LT", h, 0, nl // 16)), qh(h), OP.subtract)
-            act(a0, a0, AF.Abs)
+            ts(a1, a0, 0.0, OP.max, 2.0, OP.mult)
             d0, s0 = PS("ZB", h, 128, 136, 1, nl), PS("ZB", h, 136, 144, 1, nl)
             mm(s0, A(fq, K0[h], K0[h] + nl), A("WZ", 15, 143, 16))
-            mm(d0, a0, A("R1"))
-            ts(FIRST("AD", h, 0, nl), d0, 16.0, OP.add)
-            ts(RW("DK", h), d0, RC, OP.add, U, OP.mult)
+            mm(d0, a0, A("R1N"), True, False)
+            mm(d0, a1, A("R1"), False, True)
+            ts(FIRST("AD", h, 0, nl), d0, HW, OP.add)
             cp(RW("RT", h), s0)
             rpf = lambda r: A("RPF_%d" % h, 8 * t, 8 * t + 8, 1, (0, r))
             if nh[h] < nl or not t:
-                cp(FIRST("RD0", h, 0, nl), rpf(nl))
+                cp(FIRST("RR", h, 0, nl), rpf(nl))
             if t:
                 r = nh[h]
-                mm(PS("ZB", h, 144, 168, 1, r), A(lm, K0[h], K0[h] + r), A("MW"))
-                m1 = A("M1_%d" % h, 0, 8, 1, (0, r))
-                tt(m1, rpf(r), PS("ZB", h, 152, 160, 1, r), OP.subtract)
-                tt(FIRST("RD0", h, 0, r), PS("ZB", h, 144, 152, 1, r), m1, OP.max)
-                ts(A("BIN_%d" % h, 0, 8, 1, (0, r)), PS("ZB", h, 160, 168, 1, r), -4096.0 * rank, OP.add)
-            masks(h, 0, "RD0")
-            tt(FIRST("RD", h, 0, nl), RW("DK", h), FIRST("RD0", h, 0, nl), OP.min)
-            tt(RW("IM", h), RW("DK", h), FIRST("RD0", h, 0, nl), OP.is_lt)
+                m1, came = A("M1_%d" % h, 0, 8, 1, (0, r)), lambda c: A(lm, 24 * h + c, 24 * h + c + 8, 1, (0, r))
+                tt(m1, rpf(r), came(8), OP.subtract)
+                tt(FIRST("RR", h, 0, r), came(0), m1, OP.max)
+                act(A("BIN_%d" % h, 0, 8, 1, (0, r)), came(16), AF.Identity, 1.0, -4096.0 * rank)
+            ts(FIRST("RD0", h, 0, nl), FIRST("RR", h, 0, nl), RC - HW, OP.add, U, OP.mult)
+            tt(RW("IM", h), FIRST("AD", h, 0, nl), FIRST("RR", h, 0, nl), OP.is_lt)
+            tt(RW("DK", h), FIRST("AD", h, 0, nl), FIRST("RR", h, 0, nl), OP.min)
+            masks(h, 0)
+            ts(FIRST("RD", h, 0, nl), RW("DK", h), RC - HW, OP.add, U, OP.mult)
             ts(RW("RT", h), RW("RT", h), 63, OP.bitwise_and)
             ts(RW("RN", h), RW("RT", h), 1.0, OP.add)
             tt(RW("RN", h), RW("RN", h), RW("IM", h), OP.mult)
         for h in (0, 1):
             lead[0] = 1 - h
+            phase[0] = 100 * t + 2 * h + 3
             mm(PS("KEY", h, 0, 280), A("ONB", 0, 128, 1, (0, 33)), A("CR", 0, 280, 1, (0, 33)))
-            points(h)
-            keys(h)
+            points(h, 0)
+            keys(h, 0)
         if t == 0:
-            lead[0] = -10
+            lead[0], phase[0] = -10, 9.5
             later()
         for s in range(1, ST + 1):
             for h in (0, 1):
                 lead[0] = 1 - h
+                phase[0] = 100 * t + 4 * s + 2 * h
                 look(h, s)
-                points(h)
-                keys(h)
+                points(h, s)
+                keys(h, s)
         last = t == VI - 1
         for h in (0, 1):
             lead[0] = 1 - h
             nl = NL[h]
+            phase[0] = 100 * t + 24 + 2 * h
             ts(HB("TI", h), ind(HB("SC", h, 0, 144 * 5 + 136), A("LH")), 0.25, OP.mult, -C0, OP.add)
             ts(HB("TI", h), HB("TI", h), 4095, OP.bitwise_and)
             ts(RW("LZ", h), RW("TI", h), 0, OP.is_equal)
             cp(RW("LF", h), RW("TI", h))
             cp(RW("LF", h, 0, 64, 8), RW("RN", h))
             scan(RW("LS", h), RW("LZ", h), RW("LF", h), OP.mult, OP.add)
+            prev = RW("LS", h, 5, 64, 8)
+            ts(RW("Z0", h), prev, 0.0, OP.is_equal)
+            tt(RW("Z0", h), RW("Z0", h), RW("BIN", h), OP.mult)
+            tt(RW("Z0", h), RW("Z0", h), prev, OP.add)
             look(h, ST + 1)
             t6 = LAST("SC", h, 144 * 6, nl)
             if not last:
@@ -513,22 +553,21 @@ def rank_program(g, core, T, topo):
             ts(RW("T6", h), t6, 0.25, OP.mult, -C0, OP.add)
             tt(RW("NI", h), t6, FIRST("RD", h, 0, nl), OP.is_ge)
             ts(RW("N6", h), RW("T6", h), 4095, OP.bitwise_and)
-            tt(RW("ZN", h), RW("NI", h), RW("LS", h, 5, 64, 8), OP.mult)
-            tt(RW("N", h), RW("ZN", h), RW("N6", h), OP.add)
             if not last:
+                tt(RW("ZN", h), RW("NI", h), prev, OP.mult)
+                tt(RW("N", h), RW("ZN", h), RW("N6", h), OP.add)
                 ts(RW("NZ", h, 15, 143, 16), RW("N", h), float(MID), OP.subtract)
                 to_list("NLT", h, "NZ", "SJ1", float(MID))
                 cp(HB("GG", h, 0, nl), ind(A("CH"), HB("NLT", h, 0, nl // 16)))
             ts(RW("RHO", h), RW("T6", h), 16, OP.logical_shift_right)
             cp(RW("ML", h, 0, 128, 16), RW("RHO", h))
-            ts(RW("Z0", h), RW("N", h), 0.0, OP.is_equal)
-            tt(RW("Z0", h), RW("Z0", h), RW("BIN", h), OP.mult)
-            tt(RW("ML", h, 1, 128, 16), RW("Z0", h), RW("N", h), OP.add)
+            tt(RW("Z0", h), RW("Z0", h), RW("NI", h), OP.mult)
+            tt(RW("ML", h, 1, 128, 16), RW("Z0", h), RW("N6", h), OP.add)
             if not last:
                 o = PS("ZB", h, 0, nl)
                 mm(o, RW("ML", h), EYE("IF", nl))
                 act(A("MG", K0[h], K0[h] + nl), o, AF.Identity, 1.0, A("BIAS"))
-                cp(ind(A("SM%d" % t), HB("DL", h, 0, nl // 16)), A("MG", K0[h], K0[h] + nl))
+                cp(ind(A("SG%d" % t), HB("DL", h, 0, nl // 16)), A("MG", K0[h], K0[h] + nl))
             for j in (0, 1):
                 o = PS("ZB", h, 128 + 128 * j, 128 + 128 * j + nl, 1, 8)
                 a = (j * VI + t) * L + K0[h]
@@ -546,10 +585,15 @@ def rank_program(g, core, T, topo):
         m = some(topo.engines(core, hop))
 
         def send(x):
-            s, d = A("S%s%d" % (x.upper(), t), 0, CAP), A("L%s%d" % (x.upper(), t))
+            d = A("L%s%d" % (x.upper(), t))
+            s = A("S%s%d" % (x.upper(), t), 0, size(d))
             ra, rl = T.sem["a%s%d" % (x, t)], T.sem["l%s%d" % (x, t)]
             op("g", lambda: g.remote_dma(d[0], s[0], ra, rl, pid, rid, m), [s], [], "r", rl, 8, 1.0)
         send("q")
+        for h in (0, 1):
+            o = PS("FB", h, 440, 464, 1, nh[h])
+            mm(o, A("SG%d" % t, K0[h], K0[h] + nh[h]), A("MW"))
+            act(A("SM%d" % t, 24 * h, 24 * h + 24, 1, (0, nh[h])), o, AF.Copy)
         send("m")
         cp(A("PT", M + t * L, M + t * L + L), q(0, L))
         for h in (0, 1):
@@ -561,40 +605,38 @@ def rank_program(g, core, T, topo):
             mm(ob, RW("OL", h), EYE("IB", nl))
             mm(bn, RW("OL", h), RW("DG", h, 0, nl), True, False)
             mm(bn, RW("OL", h), EYE("IS%d" % t, nl), False, True)
-            ga = PS("ZB", h, 384, 384 + nl)
-            mm(ga, RW("NZ", h, 0, 128), EYE("IH", nl))
-            cp(A("GA", k0, k0 + nl), ga)
-            for gr in range(8):
-                ts(A("LG", gr * L + k0, gr * L + k0 + nl), A("GA", k0, k0 + nl), A("GM", gr, gr + 1), OP.mult,
-                   A("GO", gr, gr + 1), OP.add)
+            def turned(out, src, z, a):
+                for u in (0, 1):
+                    mm(PS(z, h, a + u * nl, a + u * nl + nl), RW(src, h, 128 * u, 128 * u + 128), EYE("IH", nl))
+                cp(HB(out, h, 0, 2 * nl), PS(z, h, a, a + 2 * nl))
+            ts(RW("MA", h, 0, 256, 32), RW("N", h), float(MID), OP.subtract)
+            turned("GA", "MA", "FB", 0)
             tt(RW("FN", h), RW("FAR", h), RW("N", h), OP.mult)
             tt(HB("EE", h, 0, nl), HB("GG", h, 0, nl), ob, OP.is_lt)
             tt(HB("NEW", h, 0, nl), HB("GG", h, 0, nl), bn, OP.add)
             can = PS("KEY", h, 256, 264, 1, nl)
             mm(can, HB("EE", h, 0, nl), A("R1"))
             tt(RW("YPL", h), can, RW("FN", h), OP.mult)
-            ts(RW("MB", h, 14, 128, 16), RW("YPL", h), -1.0, OP.mult, float(MID), OP.add)
-            ts(RW("YH", h), RW("YPL", h), float(MID), OP.subtract)
-            gb = PS("KEY", h, 272, 272 + nl)
-            mm(gb, RW("MB", h), EYE("IH", nl))
-            ts(A("GB", k0, k0 + nl), gb, A("O15"), OP.add)
+            ts(RW("MB", h, 1, 256, 32), RW("YPL", h), -1.0, OP.mult, float(MID), OP.add)
+            turned("GB", "MB", "KEY", 272)
             banks = (("ZB0", "KEY0"), ("SP0", "SP1", "ZB1", "KEY1"))[h]
             for gr in range(8):
-                w, z = k0 + nl, banks[gr % len(banks)]
-                o = A(z, 0, w, 1, (0, nl))
-                mm(o, A("LG", gr * L + k0, gr * L + w), A("GB", 0, w), True, False)
-                mm(A(z, k0, w, 1, (0, nl)), EYE("IB", nl), A("TRP", 0, nl, 1, (0, nl)), False, True)
-                least(RW("DMIN", h, gr, gr + 1), o)
-            tt(RW("DMIN", h), RW("DMIN", h), RW("YPL", h), OP.min)
-            ts(RW("UU", h), RW("DMIN", h), -4096.0, OP.mult, A("KJ", h, h + 1, 1, (0, nl)), OP.add)
-            tt(RW("NZ2", h, 15, 143, 16), RW("UU", h), RW("YH", h), OP.max)
-            to_list("DL2", h, "NZ2", "SJ1", float(MID))
+                w, z, r = k0 + nl, banks[gr % len(banks)], gr % 4 * 32
+                side = lambda nm, e: A("%s_%d" % (nm, e), gr // 4 * NL[e], (gr // 4 + 1) * NL[e], 1, (r, r + 2))
+                if h:
+                    mm(A(z, 0, k0, 1, (0, nl)), side("GA", h), side("GB", 0))
+                o = A(z, k0, w, 1, (0, nl))
+                mm(o, EYE("IB", nl), A("TRP", 0, nl, 1, (0, nl)), True, False)
+                mm(o, side("GA", h), side("GB", h), False, True)
+                least(RW("DMIN", h, gr, gr + 1), A(z, 0, w, 1, (0, nl)))
+            tt(RW("YP", h), RW("DMIN", h), RW("YPL", h), OP.min)
+            ts(RW("UU", h), RW("YP", h), 4096.0, OP.mult, A("KJ", h, h + 1, 1, (0, nl)), OP.subtract)
+            tt(RW("NZ2", h, 15, 143, 16), RW("UU", h), RW("MB", h, 1, 256, 32), OP.min)
+            to_list("DL2", h, "NZ2", "SJN", float(MID))
         for h in (0, 1):
             lead[0] = 1 - h
             nl = NL[h]
             cp(ind(A("CH"), HB("DL2", h, 0, nl // 16)), HB("NEW", h, 0, nl))
-            ts(RW("YP", h), RW("DMIN", h), 4096.0, OP.mult)
-            tt(RW("YP", h), RW("YP", h), RW("YPL", h), OP.min)
             o = PS("FB", h, 320, 320 + nl, 1, 8)
             mm(o, RW("YP", h), EYE("IF", nl))
             act(A("YPO", t * L + K0[h], t * L + K0[h] + nl), o, AF.Copy)
@@ -647,7 +689,7 @@ def plan(ops):
                 elif w:
                     h[:] = [e for e in h if e[1][1:] != r[1:]]
                 h.append((i, r, w))
-    after = [{"c": 0.18, "d": 2.2, "r": 6.0, "x": 0.1}[o[4]] for o in ops]
+    after = [{"c": 0.18, "d": 2.2, "r": 5.0, "x": 0.1}[o[4]] for o in ops]
     for i in range(N):
         if ops[i][4] == "d" and ops[i][3]:
             after[i] += (ops[i][3][0][5] - ops[i][3][0][4]) * 0.003
@@ -663,6 +705,7 @@ def plan(ops):
         order, when, end = in_time(ops, deps, nxt, after, way, bias, noise, hold, seed)
         if best is None or end < best[0]:
             best = (end, order, when)
+    best = tighten(ops, nxt, after, best)
     order, when = best[1], best[2]
     seq, num = {q: 0 for q in "vstg"}, [1] * N
     known = {q: {} for q in "vstgyx"}
@@ -722,6 +765,127 @@ def in_time(ops, deps, nxt, after, way, bias, noise, hold, seed):
             if left[k] == 0:
                 ready[ops[k][0]].append(k)
     return order, when, max(free.values())
+
+
+def pack(ops, order, pre):
+    start, begin, ends = [0.0] * len(ops), {q: [] for q in "vstgyx"}, {q: [] for q in "vstgyx"}
+    for i in order:
+        c, t = ops[i][7], 0.0
+        for j, gap in pre[i]:
+            u = start[j] + ops[j][7] + gap
+            if u > t:
+                t = u
+        b, e = begin[ops[i][0]], ends[ops[i][0]]
+        lo, hi = 0, len(e)
+        while lo < hi:
+            mid = (lo + hi) // 2
+            if e[mid] > t:
+                hi = mid
+            else:
+                lo = mid + 1
+        while lo < len(b) and b[lo] < t + c - 1e-9:
+            t = e[lo]
+            lo += 1
+        b.insert(lo, t)
+        e.insert(lo, t + c)
+        start[i] = t
+    return start
+
+
+def tighten(ops, nxt, after, best):
+    N = len(ops)
+    pre, post = [[] for _ in range(N)], [[] for _ in range(N)]
+    for i in range(N):
+        for k, st in nxt[i]:
+            pre[k].append((i, 0.0 if st else after[i]))
+            post[i].append((k, 0.0 if st else after[i]))
+    start, z = pack(ops, best[1], pre), 1
+    top = None
+    for r in range(ROUNDS):
+        end = max(start[i] + ops[i][7] + after[i] for i in range(N))
+        if top is None or end < top[0]:
+            top = (end, start)
+        elif r % 4 == 0:
+            start = top[1]
+        key = []
+        for i in range(N):
+            z = (1103515245 * z + 12345) % 2147483648
+            key.append(start[i] + ops[i][7] + NOISE * z / 2147483648.0)
+        for i in range(N):
+            for j, gap in pre[i]:
+                if key[i] <= key[j]:
+                    key[i] = key[j] + 1e-6
+        back = pack(ops, sorted(range(N), key=lambda i: -key[i]), post)
+        start = pack(ops, sorted(range(N), key=lambda i: -back[i] - ops[i][7]), pre)
+    end, start = polish(ops, pre, post, after, top[1])
+    return end, sorted(range(N), key=lambda i: start[i]), start
+
+
+def polish(ops, pre, post, after, start):
+    N = len(ops)
+    c = [o[7] for o in ops]
+    before, behind, tail_of = [-1] * N, [-1] * N, {}
+    for i in sorted(range(N), key=lambda i: start[i]):
+        j = tail_of.get(ops[i][0], -1)
+        before[i] = j
+        if j >= 0:
+            behind[j] = i
+        tail_of[ops[i][0]] = i
+    ps = [set(j for j, g in pre[i]) for i in range(N)]
+    best, z = None, 1
+    for r in range(SWAPS):
+        left = [len(pre[i]) + (before[i] >= 0) for i in range(N)]
+        head = [0.0] * N
+        order = [i for i in range(N) if not left[i]]
+        for i in order:
+            e = head[i] + c[i]
+            for k, g in post[i] + ([(behind[i], 0.0)] if behind[i] >= 0 else []):
+                if head[k] < e + g:
+                    head[k] = e + g
+                left[k] -= 1
+                if not left[k]:
+                    order.append(k)
+        if len(order) < N:
+            before, behind = list(best[2]), list(best[3])
+            continue
+        tail = [0.0] * N
+        for i in reversed(order):
+            t = after[i]
+            for k, g in post[i]:
+                if t < g + tail[k]:
+                    t = g + tail[k]
+            k = behind[i]
+            if k >= 0 and t < tail[k]:
+                t = tail[k]
+            tail[i] = t + c[i]
+        end = max(tail)
+        if best is None or end < best[0] - 1e-9:
+            best = (end, head, list(before), list(behind))
+        elif end > best[0] + 0.8:
+            before, behind = list(best[2]), list(best[3])
+            continue
+        last = -9.0
+        for v in sorted((i for i in range(N) if head[i] + tail[i] > end - 1e-6), key=lambda i: head[i]):
+            u = before[v]
+            if u < 0 or u in ps[v] or head[u] + c[u] < head[v] - 1e-9 or head[u] < last:
+                continue
+            a, b = before[u], behind[v]
+            hv = max([head[j] + c[j] + g for j, g in pre[v]] + [head[a] + c[a] if a >= 0 else 0.0])
+            if hv > head[u] + c[u] - 1e-9:
+                continue
+            hu = max(head[u], hv + c[v])
+            tu = c[u] + max([g + tail[k] for k, g in post[u]] + [tail[b] if b >= 0 else 0.0, after[u]])
+            tv = c[v] + max([g + tail[k] for k, g in post[v]] + [tu, after[v]])
+            z = (1103515245 * z + 12345) % 2147483648
+            if max(hv + tv, hu + tu) > end + (0.1 if z % 1024 < 60 else -1e-6) or z % 4096 < 1000:
+                continue
+            if a >= 0:
+                behind[a] = v
+            if b >= 0:
+                before[b] = u
+            before[v], behind[v], before[u], behind[u] = a, u, v, b
+            last = head[v] + 1.0
+    return best[0], best[1]
 
 
 def emit(g, ops, QUE, SEM):

@@ -11,19 +11,30 @@ RC = 7.5 + 1.0 / 256
 C0 = RC * 65536
 NONE = -(4096.0 - MID / 4096.0)
 HW = 1040.0
+WHOLE = 1.5 * 2 ** 23
 CYC, TCY = 0.0009, 0.00045
-XV = {0: (56, 56, 48, 48, 48, 60), 1: (48, 44, 36, 32, 32, 48)}
+XV = {0: (52, 56, 52, 52, 52, 52, 60), 1: (40, 44, 36, 36, 36, 48, 52)}
 
 
 def shares(h, s):
     x, n = XV[h][s], NL[h]
-    m = x + (n - x + 2) // 4 * 2
-    return ((0, x // 4 * 2), (x // 4 * 2, x)), ((x, m), (m, n))
+    k = 2 if n - x <= 64 else 3
+    m = [x + (n - x) * i // k // 2 * 2 for i in range(k)] + [n]
+    if MS[h] and k == 2 and 0 < MS[h] - x <= 32:
+        m[1] = MS[h]
+    v = [x * i // NV // 2 * 2 for i in range(NV)] + [x]
+    return tuple(zip(v, v[1:])), tuple(zip(m, m[1:]))
+
+
+MS, NV, CUT = (0, 0), 2, (0, 0)
+QS, GS, RDS = 6, (0, 1), (1, 2, 3, 4, 5)
+RS, Q0 = 12, 3
+FLY = {"q": 6.0, "f": 4.0, "m": 4.2}
 
 
 TRIES = [(0.8 * b, 0.3 * (s > 1), 1e-9, s) for b in range(6) for s in range(1, 4)]
-ROUNDS, NOISE, SWAPS = 12, 0.03, 1500
-ONV = ("XB", "X2", "X3")
+STARTS, ROUNDS, NOISE, SWAPS = 8, 5, 0.03, 3000
+ONV = (("X2", "X3"), ("XB", "X2", "X3"))
 KS = {0: ((0, 112),), 1: ((0, 96),)}
 
 SCRATCH = {"PT": ("sbuf", [128, W], "bfloat16"), "QA": ("sbuf", [128, VI * L], "bfloat16"), "CH": ("sbuf", [128, CW], "int32"),
@@ -31,11 +42,11 @@ SCRATCH = {"PT": ("sbuf", [128, W], "bfloat16"), "QA": ("sbuf", [128, VI * L], "
            "R0F": ("sbuf", [8, VI * L], "float32"), "YO": ("sbuf", [8, 2 * VI * L], "float32"),
            "YPO": ("sbuf", [8, 2 * L], "float32")}
 for _h in ("0", "1"):
-    SCRATCH["SQ" + _h] = ("sbuf", [128, 2 * L], "bfloat16")
     SCRATCH["SG" + _h] = ("sbuf", [128, 2 * L], "float32")
-    SCRATCH["SM" + _h] = ("sbuf", [128, 48], "float32")
-    SCRATCH["LQ" + _h] = ("sbuf", [128, CAP], "bfloat16")
-    SCRATCH["LM" + _h] = ("sbuf", [128, 48], "float32")
+    for _n in "SL":
+        SCRATCH[_n + "F" + _h] = ("sbuf", [128, 16], "bfloat16")
+        SCRATCH[_n + "M" + _h] = ("sbuf", [128, 32], "float32")
+    SCRATCH["LQ" + _h] = ("sbuf", [128, L], "bfloat16")
     for _n in ("KEY", "ZB", "FB", "SP"):
         SCRATCH[_n + _h] = ("psum", [128, 512], "float32")
 PSUMS = {n for n in SCRATCH if SCRATCH[n][0] == "psum"}
@@ -57,20 +68,21 @@ def _pool(big, dtype, halves, **bufs):
     SCRATCH[big] = ("sbuf", [128, at], dtype)
 
 
-_pool("ALLb", "bfloat16", dict(XG=1536, DA=1792, DX=1792, QT=128, A0=112, A1=112, AS=144, XB=144, X2=144, X3=144, RB=136,
-                               EA=144, EB=144, EC=144, ED=144, OL=128, EE=112, DG=112, FAR=8),
+_pool("ALLb", "bfloat16", dict(XG=1536, DA=1792, DX=1792, QT=128, A0=112, A1=112, AS=144, XB=144, X2=144, X3=144, RB=136, RR=136,
+                               EA=144, EB=144, EC=144, ED=144, OL=128, EE=112, DG=112, JK=4 * L),
       WZ=144, CR=288, ONB=144, SEG=144, IB=128, IN=128, I28=128, I13=128, IU=128, R1=8, R1N=8, R16=16, R16N=16,
-      REP=1792, TRI=128, TRP=112, THB=128, IS0=112, IS1=112, FM=CAP, Q16=16 * 176, QF1=L, QF2=L, QC1=L, QC2=L, ID1=144, SJ=128)
+      REP=1792, TRI=128, TRP=112, THB=128, IS0=112, IS1=112, Q16=16 * 176, QC1=2 * L, QC2=2 * L, ID1=144, SJ=128)
 _pool("ALLf", "float32", dict(RD=144, RD0=144, SC2=144, FD=144, GD2=144, GD3=144, GD4=272, SC=1008, ML=128, X=144, Y0=144, Y1=144,
                               Y2=144, Y3=144, KM0=144, KM1=144, KM2=144, KM3=144, FS=272, RPF=24, DK=8, IM=8, RN=8, G23=8, FX=8,
                               LF=64, LZ=64, LS=64, NI=8, ZN=8, N=8, Z0=8, BIN=8, GG=112, NEW=112, FN=8, YPL=8, DMIN=8,
-                              UU=8, YP=8, M1=8),
-      TD=144, MW=24, ONF=128, IF=128, WF=1, THF=1, THK=8, KK=2, KC=2, KJ=2, BIAS=1, MG=L, ICOL=1, JF=9,
+                              UU=8, YP=8, M1=8, RV=8, S1=8, S2=8),
+      TD=144, MW=24, ONF=128, IF=128, WF=1, THF=1, THK=8, KK=2, KC=2, KJ=2, SM2=32, MG=L, ICOL=1, JF=9,
       G17=9, J0=9, B1=1, B2=1, J34=4)
 _pool("ALLi", "int32", dict(NN=8, DI=8, RHO=8, TI=64, T6=8, N6=8, BI=8, RT=8), PI=4, RI=128, GI=9, BCI=8, RS=16)
 _pool("ALLu", "uint16", dict(P16=112, LT=8, DL=8, NLT=8, DL2=8), LX=10, LE=10, L0=10, LH=4, BCL=8)
-_pool("ALLh", "float16", dict(AD=144, RR=144, NZ=144, NZ2=144, MA=256, MB=256, GA=224, GB=224, PH=112), IDG=272, SJ1=128, SJ4=128, SJN=128, IH=112)
-SEMAPHORES = ["cv", "cs", "ct", "cg", "aq0", "aq1", "am0", "am1", "lq0", "lq1", "lm0", "lm1"] + ["d%d" % i for i in range(24)]
+_pool("ALLh", "float16", dict(AD=144, NZ=144, NZ2=144, NZ3=144, MA=256, MB=256, GA=224, GB=224, PH=112), IDG=272, SJ1=128, SJ4=128, SJN=128, IH=112)
+SENDS = ("q0", "f0", "m0", "q1", "f1", "m1")
+SEMAPHORES = ["cv", "cs", "ct", "cg"] + [a + b for a in "al" for b in SENDS] + ["d%d" % i for i in range(24)]
 PLAN = {}
 
 
@@ -94,11 +106,11 @@ def rank_program(g, core, T, topo):
             src, dst = cores[r], cores[(r + 1) % n]
             if hop_of(src, dst, cores, topo) == core:
                 rid, pid = topo.addr(dst, core)
-                for t in ("q0", "m0", "q1", "m1"):
+                for t in SENDS:
                     a = T["L" + t.upper()][:]
                     g.wait_ge(T.sem["a" + t], 8)
                     g.remote_dma(a, a, T.sem["a" + t], T.sem["l" + t], pid, rid, some(topo.engines(core, dst)))
-                for t in ("q0", "m0", "q1", "m1"):
+                for t in SENDS:
                     g.wait_ge(T.sem["l" + t], 8)
         return
 
@@ -202,6 +214,10 @@ def rank_program(g, core, T, topo):
         else:
             call("s", "", lambda: g.scalar.activation(ap(out), ap(a), f, bias=bias, scale=scale), out, a)
 
+    def signs(out, a, bias, total):
+        op("s", lambda: g.scalar.activation(ap(out), ap(a), AF.Sign, bias=bias, accum_out=ap(total)), [a], [out, total],
+           c=cost("s", "", out, [a]) + 0.02)
+
     def mm(out, l, r, start=True, stop=True):
         call("t", "", lambda: g.tensor.matmul(ap(out), ap(l), ap(r), start, stop), out, l, r)
 
@@ -222,8 +238,9 @@ def rank_program(g, core, T, topo):
 
     load("y", "WI", T.w[:])
     load("s", "QA", T.q[:, 0:L], 0, L)
-    load("y", "PT", T.pt[:, 0:1152], 0, 1152)
+    load("y", "PT", T.pt[:, 16:1152], 16, 1152)
     load("s", "CH", T.ch[:, 0:80], 0, 80)
+    load("s", "PT", T.pt[:, 0:16], 0, 16)
     load("s", "PT", T.pt[:, 1152:M], 1152, M)
     load("y", "R0I", T.r0[:])
     load("y", "CH", T.ch[:, 80:1200], 80, 1200)
@@ -243,13 +260,19 @@ def rank_program(g, core, T, topo):
     iota(A("CR", 0, 136, 1, (0, 1)), [[0, 8], [16384, 17]], 16384 * 119, 0, True)
     iota(A("CR", 136, 272, 1, (0, 1)), [[0, 8], [-1, 17]], 1, 0, True)
     asel(A("ID1", 0, 136), A("ONB", 0, 136), [[-16, 8], [-1, 17]], OP.is_equal, 0.0, 1, 1)
-    iota(A("CH", M, CW), [[0, CW - M]], 0, 0)
     asel(A("SJ"), A("ONB", 0, 128), [[-1, 16], [-16, 8]], OP.is_equal, 0.0, 0, 1)
+    iota(A("KK"), [[112, 2]], 0, 1, True)
+    iota(A("J34"), [[34, 4]], 0, 0, True)
+    iota(A("BCI"), [[1, 8]], 0, 0)
+    iota(A("CH", M, CW), [[0, CW - M]], 0, 0)
     cp(A("WF"), A("WI"))
     ts(A("WZ", 15, 143, 16), A("R1"), A("WF"), OP.mult)
     ts(A("IN"), A("IB"), -1.0, OP.mult)
     for i in range(16):
-        act(A("REP", i, 1792, 16), A("IB", 0, 112), AF.Copy)
+        if i < RS:
+            act(A("REP", 512 + i, 1792, 16), A("IB", 32, 112), AF.Copy)
+        else:
+            cp(A("REP", 512 + i, 1792, 16), A("IB", 32, 112))
     ts(A("R16", 0, 8), A("R1"), U, OP.mult)
     ts(A("R16", 8, 16), A("R1"), -16.0, OP.mult)
     ts(A("R16N"), A("R16"), -1.0, OP.mult)
@@ -259,9 +282,9 @@ def rank_program(g, core, T, topo):
     fill_all(both("RD"), -BIG)
     fill_all(both("RD0"), 0.0)
     for h in (0, 1):
-        for nm, v in (("AD", -16.0), ("RR", 0.0)):
-            ts(HB(nm, h), A("ONB"), v, OP.mult)
-            ts(HB(nm, h, 1, 136, 17), A("ONB", 0, 8), -HW, OP.mult)
+        ts(HB("AD", h), A("ONB"), -16.0, OP.mult)
+        ts(HB("AD", h, 1, 136, 17), A("ONB", 0, 8), -HW, OP.mult)
+    fill_all(both("RR"), 0.0)
     fill(A("CR", 0, 136, 1, (32, 33)), 4.0 * (MID + 256))
     fill(A("CR", 0, 136, 17, (0, 1)), -BIG * 32768)
     fill(A("CR", 136, 272, 17, (0, 1)), BIG)
@@ -287,9 +310,9 @@ def rank_program(g, core, T, topo):
     def radii(t):
         cp(A("R0F", t * L, t * L + L), A("R0I", t * L, t * L + L))
         for h in (0, 1):
-            a, o = t * L + K0[h], PS("ZB", h, 448, 456, 1, NL[h])
+            a, o = t * L + K0[h], PS("FB", h, 448, 456, 1, NL[h])
             mm(o, A("R0F", a, a + NL[h]), A("IF", 0, 8, 1, (0, 8)))
-            act(RW("RPF", h, 8 * t, 8 * t + 8), o, AF.Identity, 1.0, HW)
+            act(RW("RPF", h, 8 * t, 8 * t + 8), o, AF.Copy)
     radii(0)
     fill(A("PT", 0, 1), 256.0)
     fill(A("TD"), BIG)
@@ -312,23 +335,20 @@ def rank_program(g, core, T, topo):
                 even(HB("SC", h, 144 * s + 137, 144 * s + 144), 0)
             ts(HB("NZ2", h), A("ONB"), 0.0, OP.mult)
             for nm, j in (("MA", 1), ("MB", 0)):
-                ts(HB(nm, h), A("REP", 0, 256), 0.0, OP.mult)
+                ts(HB(nm, h), A("CR", 0, 256), 0.0, OP.mult)
                 ts(HB(nm, h, j, 256, 32), A("ONB", 0, 8), 4096.0, OP.mult)
             even(HB("BIN", h), -4096 * rank)
             even(HB("BI", h), 0)
             even(HB("ML", h), 0)
             act(HB("ML", h, 2, 128, 16), A("ONF", 0, 8), AF.Copy)
         even(A("MW"), 0)
-        iota(A("J34"), [[34, 4]], 0, 0, True)
-        iota(A("BCI"), [[1, 8]], 0, 0)
         iota(A("RI"), [[0, 8], [1, 16]], 0, 0)
         asel(A("TRI"), A("ONB", 0, 128), [[1, 128]], OP.is_ge, 0.0, -1, -1)
         asel(A("TRI"), A("TRI"), [[1, 128]], OP.not_equal, -512.0, 0, -1)
         fill(A("TRP"), float(2 ** 25))
         asel(A("TRP"), A("TRP"), [[1, 112]], OP.is_ge, 0.0, 0, -1)
-        for c, j, v in ((0, 0, 1.0), (0, 2, HW), (8, 2, 4096.0), (16, 1, 1.0)):
+        for c, j, v in ((0, 0, 1.0), (8, 2, 4096.0), (16, 1, 1.0)):
             asel(A("MW", c, c + 8), A("MW", c, c + 8), [[-16, 8]], OP.not_equal, v, -j, 1)
-        iota(A("KK"), [[112, 2]], 0, 1, True)
         iota(A("KC"), [[112, 2]], L, 1, True)
         iota(A("KJ"), [[112, 2]], W - MID, 1, True)
         ts(A("PI", 2, 3), A("PI", 0, 1), 7, OP.bitwise_and)
@@ -340,34 +360,35 @@ def rank_program(g, core, T, topo):
         cp(A("SJ1"), A("SJ"))
         cp(A("IH"), A("IB", 0, 112))
         ts(A("SJN"), A("SJ"), -1.0, OP.mult)
-        ts(A("BIAS"), A("ICOL"), 1.0, OP.is_equal, 4096.0 * rank, OP.mult)
         for t in (0, 1):
             ts(HB("DG", t), A("IB", 0, 112), A("KK", t, t + 1), OP.mult)
             ts(A("IS%d" % t), A("IB", 0, 112), float(M + t * L), OP.mult)
-            even(A("SQ%d" % t), -80)
-            even(A("SG%d" % t), 0)
-            even(A("SM%d" % t), 0)
-            act(A("QF%d" % (t + 1)), A("QA", (t + 1) * L, (t + 2) * L), AF.Identity, 1.0, -64.0)
-            act(A("QC%d" % (t + 1), CAP, L), A("QA", (t + 1) * L + CAP, (t + 2) * L), AF.Copy)
+            ts(HB("NZ3", t), A("ONB"), 0.0, OP.mult)
+            for nm in ("SG", "SM", "SF"):
+                even(A(nm + str(t)), 0)
+            even(A("QC%d" % (t + 1), L, 2 * L), 0)
+            act(A("QC%d" % (t + 1), 0, L), A("QA", (t + 1) * L, (t + 2) * L), AF.Copy)
             radii(t + 1)
         cp(A("THF"), A("THI"))
         ts(A("THB"), A("ONB", 0, 128), A("THF"), OP.mult)
         mm(PS("ZB", 1, 456, 464), A("THB"), A("R1"))
         ts(A("THK"), PS("ZB", 1, 456, 464), U / 16, OP.mult, RC * U, OP.add)
 
-    def to_list(out, h, nz, sj, more):
+    def to_list(out, h, nz, sj, more, bank="FB"):
         k = NL[h] // 16
-        o = PS("FB", h, 288, 288 + k)
+        o = PS(bank, h, 288, 288 + k)
         for j in range(16):
             mm(o, RW(nz, h, 15 - j, 143 - j), A(sj, 8 * j, 8 * j + k, 1, (0, NL[h])), j == 0, j == 15)
         ts(HB(out, h, 0, k), o, more, OP.add)
 
     def kids(h, top=CW):
-        cp(HB("P16", h, 0, NL[h]), ind(A("CH", 0, top), HB("LT", h, 0, NL[h] // 16)))
+        for a, b in ((CUT[h], NL[h] // 16), (0, CUT[h])):
+            if b > a:
+                cp(HB("P16", h, 16 * a, 16 * b), ind(A("CH", 0, top), HB("LT", h, a, b)))
         ts(HB("PH", h, 0, NL[h]), HB("P16", h, 0, NL[h]), float(MID), OP.subtract)
 
     def outside(h, out, lev, c, root=False):
-        if out in ONV:
+        if out in ONV[h] or root:
             tt(HB(out, h), ind(HB("RD0" if root else "RD", h, 0, 136), A("L0", 0, 9)), HB("Y%d" % lev, h), OP.is_lt)
             return
         out = HB(out, h, 0, 136)
@@ -377,7 +398,7 @@ def rank_program(g, core, T, topo):
         act(out, o, AF.Relu, 2.0 / U, -16.0)
 
     def masks(h, lev):
-        if "XB" not in ONV or (lev in FBS and "X2" not in ONV):
+        if lev and ("XB" not in ONV[h] or (lev in FBS and "X2" not in ONV[h]) or (lev == 4 and "X3" not in ONV[h])):
             scan(HB("RB", h), A("SEG", 0, 136), HB("RR", h, 0, 136), OP.mult, OP.add)
         scan(HB("AS", h), A("SEG"), HB("AD", h), OP.mult, OP.add)
         act(HB("Y%d" % min(lev, 3), h), HB("AS", h), AF.Abs, U, -7.5 * U)
@@ -424,8 +445,15 @@ def rank_program(g, core, T, topo):
         to_list("LT", h, "NZ", "SJ4", float(MID))
         kids(h)
         phase[0] += 3
-        ts(FIRST("RR", h), LAST("SC", h, a), 1.0 / U, OP.mult, HW - 8.0, OP.add)
-        ts(FIRST("RD", h), FIRST("RR", h), RC - HW, OP.add, U, OP.mult)
+        if s in RDS:
+            act(HB("RV", h), LAST("SC", h, a), AF.Identity, 1.0 / U, WHOLE - 8.0)
+            act(FIRST("RR", h), HB("RV", h), AF.Identity, 1.0, -WHOLE)
+            act(FIRST("RD", h), FIRST("RR", h), AF.Identity, U, RC * U)
+        else:
+            ts(HB("RHO", h), LAST("SC", h, a), 1.0 / U, OP.mult, -8.0, OP.add)
+            ts(FIRST("RD", h), HB("RHO", h), RC, OP.add, U, OP.mult)
+            if len(ONV[h]) < 3:
+                act(FIRST("RR", h), FIRST("RD", h), AF.Identity, 1.0 / U, -RC)
         ts(FIRST("AD", h), LAST("SC2", h), -1.0 / 16, OP.mult, HW - 0.47, OP.add)
         masks(h, s)
         sel = ind(HB("SC2", h, 0, 136), A("LE", 0, 9))
@@ -452,28 +480,59 @@ def rank_program(g, core, T, topo):
             tt(HB("FX", h), LAST("FS", h), LAST("FS", h, 136), OP.max)
         ts(FIRST("FD", h), HB("FX", h) if s == 4 else LAST("FS", h), NONE, OP.max)
 
+    hop = hop_of(core, cores[(rank + 1) % n], cores, topo)
+    rid, pid = topo.addr(hop, core)
+    sent = {}
+
+    def send(x, t, s):
+        d, ra, rl = A("L%s%d" % (x.upper(), t)), T.sem["a%s%d" % (x, t)], T.sem["l%s%d" % (x, t)]
+        sent[x] = (len(ops), FLY[x])
+        op("g", lambda: g.remote_dma(d[0], s[0], ra, rl, pid, rid, some(topo.engines(core, hop))), [s], [], "r", rl, 8, 1.0)
+
     QN = ("QA", "QC1", "QC2")
     nh = (112, CAP - 112)
     for t in range(VI):
         q = lambda a, b, st=1: A(QN[t], a, b, st)
         qh = lambda h: q(K0[h], K0[h] + NL[h])
-        fq = "QF%d" % t if t else "QA"
         phase[0] = 100 * t
         if t:
-            lq, lm = "LQ%d" % (t - 1), "LM%d" % (t - 1)
-            op("x", None, [], [A(lq)], "x", T.sem["aq%d" % (t - 1)], 8)
-            op("x", None, [], [A(lm)], "x", T.sem["am%d" % (t - 1)], 8)
-            tt(A(fq, 0, CAP), A(fq, 0, CAP), A(lq), OP.max)
-            ts(A("FM"), A(fq, 0, CAP), 0.0, OP.is_lt, 64.0, OP.mult)
-            tt(q(0, CAP), A("FM"), A(fq, 0, CAP), OP.add)
+            lq, lf, lm, sg = (x + str(t - 1) for x in ("LQ", "LF", "LM", "SG"))
+            for x in "qfm":
+                op("x", sent[x], [], [A("L%s%d" % (x.upper(), t - 1))], "x", T.sem["a%s%d" % (x, t - 1)], 8)
+            far = lambda h: A(lf, 8 * h, 8 * h + 8, 1, (0, NL[h]))
+            for h in (0, 1):
+                nl = NL[h]
+                o = PS("ZB", h, 304, 312, 1, nl)
+                mm(o, EYE("TRI", nl), far(h), True, h == 0)
+                if h:
+                    mm(o, A("ONB", 0, nl, 1, (0, NL[0])), far(0), False, True)
+                ts(RW("NZ3", h, 15, 143, 16), o, 512.0, OP.add, A("KC", h, h + 1, 1, (0, nl)), OP.min)
+                to_list("DL", h, "NZ3", "SJ1", 0.0, "ZB")
+                cp(ind(q(0, 2 * L), HB("DL", h, 0, nl // 16)), A(lq, K0[h], K0[h] + nl))
+            cp(q(CAP, L), A("QA", t * L + CAP, t * L + L))
+        if t < VI - 1:
+            send("q", t, q(0, L))
         hi = K0[1] + max(XV[1])
         for i in range(16):
-            cp(A("Q16", i, 16 * hi, 16), q(0, hi))
-        o = PS("FB", 0, 288, 301)
+            if i < (QS if t else Q0):
+                act(A("Q16", i, 16 * hi, 16), q(0, hi), AF.Copy)
+            else:
+                cp(A("Q16", i, 16 * hi, 16), q(0, hi))
+        o = PS("ZB", 0, 288, 301)
         for j in range(16):
-            mm(o, A("WZ", 15 - j, 143 - j), A(fq, j, L, 16), j == 0, j == 15)
+            mm(o, A("WZ", 15 - j, 143 - j), q(j, L, 16), j == 0, j == 15)
         cp(A("RS", 0, 13), o)
         ts(A("RS", 0, 13), A("RS", 0, 13), 63, OP.bitwise_and)
+        if t:
+            for h in (0, 1):
+                nl = NL[h]
+                for j in (0, 1):
+                    act(RW("ML", h, j, 128, 16), A(lm, 16 * h + 8 * j, 16 * h + 8 * j + 8, 1, (0, nl)), AF.Identity, 1.0,
+                        4096.0 * ((rank - 1) % n) * j)
+                o = PS("SP", h, 0, nl)
+                mm(o, RW("ML", h), EYE("IF", nl))
+                act(A("MG", K0[h], K0[h] + nl), o, AF.Copy)
+                cp(ind(A(sg), HB("DL", h, 0, nl // 16)), A("MG", K0[h], K0[h] + nl))
         for h in (0, 1):
             lead[0] = 1 - h
             nl = NL[h]
@@ -486,34 +545,34 @@ def rank_program(g, core, T, topo):
             tt(a0, ind(A("PT", 0, 80), HB("LT", h, 0, nl // 16)), qh(h), OP.subtract)
             ts(a1, a0, 0.0, OP.max, 2.0, OP.mult)
             d0, s0 = PS("ZB", h, 128, 136, 1, nl), PS("ZB", h, 136, 144, 1, nl)
-            mm(s0, A(fq, K0[h], K0[h] + nl), A("WZ", 15, 143, 16))
+            mm(s0, qh(h), A("WZ", 15, 143, 16))
             mm(d0, a0, A("R1N"), True, False)
             mm(d0, a1, A("R1"), False, True)
             ts(FIRST("AD", h, 0, nl), d0, HW, OP.add)
             cp(RW("RT", h), s0)
             rpf = lambda r: A("RPF_%d" % h, 8 * t, 8 * t + 8, 1, (0, r))
             if nh[h] < nl or not t:
-                cp(FIRST("RR", h, 0, nl), rpf(nl))
+                act(FIRST("RR", h, 0, nl), rpf(nl), AF.Copy)
             if t:
                 r = nh[h]
-                m1, came = A("M1_%d" % h, 0, 8, 1, (0, r)), lambda c: A(lm, 24 * h + c, 24 * h + c + 8, 1, (0, r))
+                mm(PS("ZB", h, 144, 168, 1, r), A(sg, K0[h], K0[h] + r), A("MW"))
+                m1, came = A("M1_%d" % h, 0, 8, 1, (0, r)), lambda c: PS("ZB", h, 144 + c, 152 + c, 1, r)
                 tt(m1, rpf(r), came(8), OP.subtract)
                 tt(FIRST("RR", h, 0, r), came(0), m1, OP.max)
                 act(A("BIN_%d" % h, 0, 8, 1, (0, r)), came(16), AF.Identity, 1.0, -4096.0 * rank)
-            ts(FIRST("RD0", h, 0, nl), FIRST("RR", h, 0, nl), RC - HW, OP.add, U, OP.mult)
-            tt(RW("IM", h), FIRST("AD", h, 0, nl), FIRST("RR", h, 0, nl), OP.is_lt)
-            tt(RW("DK", h), FIRST("AD", h, 0, nl), FIRST("RR", h, 0, nl), OP.min)
+            act(FIRST("RD0", h, 0, nl), FIRST("RR", h, 0, nl), AF.Identity, U, RC * U)
+            tt(RW("IM", h), d0, FIRST("RR", h, 0, nl), OP.is_lt)
+            tt(RW("DK", h), d0, FIRST("RR", h, 0, nl), OP.min)
             masks(h, 0)
-            ts(FIRST("RD", h, 0, nl), RW("DK", h), RC - HW, OP.add, U, OP.mult)
+            act(FIRST("RD", h, 0, nl), RW("DK", h), AF.Identity, U, RC * U)
             ts(RW("RT", h), RW("RT", h), 63, OP.bitwise_and)
             ts(RW("RN", h), RW("RT", h), 1.0, OP.add)
-            tt(RW("RN", h), RW("RN", h), RW("IM", h), OP.mult)
         for h in (0, 1):
             lead[0] = 1 - h
             phase[0] = 100 * t + 2 * h + 3
             mm(PS("KEY", h, 0, 280), A("ONB", 0, 128, 1, (0, 33)), A("CR", 0, 280, 1, (0, 33)))
-            points(h, 0)
-            keys(h, 0)
+            points(h, 0 if t else 6)
+            keys(h, 0 if t else 6)
         if t == 0:
             lead[0], phase[0] = -10, 9.5
             later()
@@ -533,7 +592,7 @@ def rank_program(g, core, T, topo):
             ts(HB("TI", h), HB("TI", h), 4095, OP.bitwise_and)
             ts(RW("LZ", h), RW("TI", h), 0, OP.is_equal)
             cp(RW("LF", h), RW("TI", h))
-            cp(RW("LF", h, 0, 64, 8), RW("RN", h))
+            tt(RW("LF", h, 0, 64, 8), RW("RN", h), RW("IM", h), OP.mult)
             scan(RW("LS", h), RW("LZ", h), RW("LF", h), OP.mult, OP.add)
             prev = RW("LS", h, 5, 64, 8)
             ts(RW("Z0", h), prev, 0.0, OP.is_equal)
@@ -541,15 +600,9 @@ def rank_program(g, core, T, topo):
             tt(RW("Z0", h), RW("Z0", h), prev, OP.add)
             look(h, ST + 1)
             t6 = LAST("SC", h, 144 * 6, nl)
+            far = lambda h: A("SF%d" % t, 8 * h, 8 * h + 8, 1, (0, NL[h]))
             if not last:
-                tt(RW("FAR", h), t6, A("THK", 0, 8, 1, (0, nl)), OP.is_ge)
-                o = PS("FB", h, 304, 312, 1, nl)
-                mm(o, EYE("TRI", nl), RW("FAR", h), True, h == 0)
-                if h:
-                    mm(o, A("ONB", 0, nl, 1, (0, NL[0])), RW("FAR", 0), False, True)
-                ts(RW("NZ2", h, 15, 143, 16), o, 512.0, OP.add, A("KC", h, h + 1, 1, (0, nl)), OP.min)
-                to_list("DL", h, "NZ2", "SJ1", 0.0)
-                cp(ind(A("SQ%d" % t), HB("DL", h, 0, nl // 16)), qh(h))
+                tt(far(h), t6, A("THK", 0, 8, 1, (0, nl)), OP.is_ge)
             ts(RW("T6", h), t6, 0.25, OP.mult, -C0, OP.add)
             tt(RW("NI", h), t6, FIRST("RD", h, 0, nl), OP.is_ge)
             ts(RW("N6", h), RW("T6", h), 4095, OP.bitwise_and)
@@ -559,19 +612,15 @@ def rank_program(g, core, T, topo):
                 ts(RW("NZ", h, 15, 143, 16), RW("N", h), float(MID), OP.subtract)
                 to_list("NLT", h, "NZ", "SJ1", float(MID))
                 cp(HB("GG", h, 0, nl), ind(A("CH"), HB("NLT", h, 0, nl // 16)))
-            ts(RW("RHO", h), RW("T6", h), 16, OP.logical_shift_right)
-            cp(RW("ML", h, 0, 128, 16), RW("RHO", h))
+            sm = lambda j: A("SM%d" % t, 16 * h + 8 * j, 16 * h + 8 * j + 8, 1, (0, nl))
+            act(RW("RV", h), t6, AF.Identity, 1.0 / U, WHOLE - 8.0)
+            act(sm(0), RW("RV", h), AF.Identity, 1.0, -WHOLE)
             tt(RW("Z0", h), RW("Z0", h), RW("NI", h), OP.mult)
-            tt(RW("ML", h, 1, 128, 16), RW("Z0", h), RW("N6", h), OP.add)
-            if not last:
-                o = PS("ZB", h, 0, nl)
-                mm(o, RW("ML", h), EYE("IF", nl))
-                act(A("MG", K0[h], K0[h] + nl), o, AF.Identity, 1.0, A("BIAS"))
-                cp(ind(A("SG%d" % t), HB("DL", h, 0, nl // 16)), A("MG", K0[h], K0[h] + nl))
+            tt(sm(1), RW("Z0", h), RW("N6", h), OP.add)
             for j in (0, 1):
-                o = PS("ZB", h, 128 + 128 * j, 128 + 128 * j + nl, 1, 8)
+                o = PS(("ZB", "KEY")[j], h, 384, 384 + nl, 1, 8)
                 a = (j * VI + t) * L + K0[h]
-                mm(o, RW("ML", h, j, 128, 16), EYE("IF", nl))
+                mm(o, sm(j), EYE("IF", nl))
                 act(A("YO", a, a + nl), o, AF.Identity, 1.0, 4096.0 * rank * j)
         lead[0] = 0
         for j, y in ((0, T.yr), (1, T.yb)):
@@ -579,22 +628,8 @@ def rank_program(g, core, T, topo):
             dma("y", y[:, t * L:t * L + L], yo[0], [yo], [])
         if last:
             break
-        dst = cores[(rank + 1) % n]
-        hop = hop_of(core, dst, cores, topo)
-        rid, pid = topo.addr(hop, core)
-        m = some(topo.engines(core, hop))
-
-        def send(x):
-            d = A("L%s%d" % (x.upper(), t))
-            s = A("S%s%d" % (x.upper(), t), 0, size(d))
-            ra, rl = T.sem["a%s%d" % (x, t)], T.sem["l%s%d" % (x, t)]
-            op("g", lambda: g.remote_dma(d[0], s[0], ra, rl, pid, rid, m), [s], [], "r", rl, 8, 1.0)
-        send("q")
-        for h in (0, 1):
-            o = PS("FB", h, 440, 464, 1, nh[h])
-            mm(o, A("SG%d" % t, K0[h], K0[h] + nh[h]), A("MW"))
-            act(A("SM%d" % t, 24 * h, 24 * h + 24, 1, (0, nh[h])), o, AF.Copy)
-        send("m")
+        send("f", t, A("SF%d" % t))
+        send("m", t, A("SM%d" % t))
         cp(A("PT", M + t * L, M + t * L + L), q(0, L))
         for h in (0, 1):
             lead[0] = 1 - h
@@ -611,7 +646,7 @@ def rank_program(g, core, T, topo):
                 cp(HB(out, h, 0, 2 * nl), PS(z, h, a, a + 2 * nl))
             ts(RW("MA", h, 0, 256, 32), RW("N", h), float(MID), OP.subtract)
             turned("GA", "MA", "FB", 0)
-            tt(RW("FN", h), RW("FAR", h), RW("N", h), OP.mult)
+            tt(RW("FN", h), far(h), RW("N", h), OP.mult)
             tt(HB("EE", h, 0, nl), HB("GG", h, 0, nl), ob, OP.is_lt)
             tt(HB("NEW", h, 0, nl), HB("GG", h, 0, nl), bn, OP.add)
             can = PS("KEY", h, 256, 264, 1, nl)
@@ -619,16 +654,28 @@ def rank_program(g, core, T, topo):
             tt(RW("YPL", h), can, RW("FN", h), OP.mult)
             ts(RW("MB", h, 1, 256, 32), RW("YPL", h), -1.0, OP.mult, float(MID), OP.add)
             turned("GB", "MB", "KEY", 272)
-            banks = (("ZB0", "KEY0"), ("SP0", "SP1", "ZB1", "KEY1"))[h]
-            for gr in range(8):
-                w, z, r = k0 + nl, banks[gr % len(banks)], gr % 4 * 32
-                side = lambda nm, e: A("%s_%d" % (nm, e), gr // 4 * NL[e], (gr // 4 + 1) * NL[e], 1, (r, r + 2))
-                if h:
-                    mm(A(z, 0, k0, 1, (0, nl)), side("GA", h), side("GB", 0))
-                o = A(z, k0, w, 1, (0, nl))
-                mm(o, EYE("IB", nl), A("TRP", 0, nl, 1, (0, nl)), True, False)
-                mm(o, side("GA", h), side("GB", h), False, True)
-                least(RW("DMIN", h, gr, gr + 1), A(z, 0, w, 1, (0, nl)))
+            banks = ("SP0", "SP1", "FB%d" % h, "KEY%d" % h)
+            w = k0 + nl
+            for z, bank in enumerate(banks):
+                for gr in (z, z + 4):
+                    r, a = gr % 4 * 32, gr // 4 * w
+                    side = lambda nm, e: A("%s_%d" % (nm, e), gr // 4 * NL[e], (gr // 4 + 1) * NL[e], 1, (r, r + 2))
+                    if h:
+                        mm(A(bank, a, a + k0, 1, (0, nl)), side("GA", h), side("GB", 0))
+                    o = A(bank, a + k0, a + w, 1, (0, nl))
+                    mm(o, EYE("IB", nl), A("TRP", 0, nl, 1, (0, nl)), True, False)
+                    mm(o, side("GA", h), side("GB", h), False, True)
+                for gr in (z, z + 4):
+                    o = A(bank, gr // 4 * w, gr // 4 * w + w, 1, (0, nl))
+                    if z < GS[h]:
+                        for j, b in ((1, 0.5), (2, -0.5)):
+                            c = (gr // 4 * 2 + j - 1) * L
+                            signs(RW("JK", h, c, c + w), o, b, RW("S%d" % j, h, gr, gr + 1))
+                    else:
+                        least(RW("DMIN", h, gr, gr + 1), o)
+            if GS[h]:
+                tt(RW("S1", h, 0, 8, 4), RW("S1", h, 0, 8, 4), RW("S2", h, 0, 8, 4), OP.is_equal)
+                ts(RW("DMIN", h, 0, 8, 4), RW("S1", h, 0, 8, 4), 4096.0, OP.mult)
             tt(RW("YP", h), RW("DMIN", h), RW("YPL", h), OP.min)
             ts(RW("UU", h), RW("YP", h), 4096.0, OP.mult, A("KJ", h, h + 1, 1, (0, nl)), OP.subtract)
             tt(RW("NZ2", h, 15, 143, 16), RW("UU", h), RW("MB", h, 1, 256, 32), OP.min)
@@ -657,8 +704,8 @@ def plan(ops):
 
     N = len(ops)
     tag = [o[0] if o[4] == "c" else "a%d" % i for i, o in enumerate(ops)]
-    in_line = lambda i, j: tag[i] == tag[j] == "t" or tag[i][:5] == tag[j][:5] in ("loady", "loads")
-    hist, deps, sent, pool, loads = {}, [], [], [], {}
+    in_line = lambda i, j: tag[i] == tag[j] == "t" or tag[i][:5] == tag[j][:5] in ("loady", "loads", "loadg")
+    hist, deps, sent, pool, loads, fly = {}, [], [], [], {}, {}
     for i in range(N):
         R, Wr, kind, dep = ops[i][2], ops[i][3], ops[i][4], set()
         for lst, w in ((R, False), (Wr, True)):
@@ -671,8 +718,11 @@ def plan(ops):
             dep.update(pool[-1:])
             pool.append(i)
         if kind == "x":
-            dep.add(sent[-2 if ops[i - 1][4] != "x" else -1])
+            dep.add(ops[i][1][0])
+            fly[ops[i][1][0]] = ops[i][1][1]
         if kind == "r":
+            tag[i] = "loadg" + tag[i]
+            dep.update(sent[-1:])
             sent.append(i)
         if kind == "d" and Wr:
             tag[i] = "load" + ops[i][0] + tag[i]
@@ -689,10 +739,11 @@ def plan(ops):
                 elif w:
                     h[:] = [e for e in h if e[1][1:] != r[1:]]
                 h.append((i, r, w))
-    after = [{"c": 0.18, "d": 2.2, "r": 5.0, "x": 0.1}[o[4]] for o in ops]
+    after = [{"c": 0.23, "d": 2.2, "r": 5.0, "x": 0.1}[o[4]] for o in ops]
     for i in range(N):
+        after[i] = fly.get(i, after[i])
         if ops[i][4] == "d" and ops[i][3]:
-            after[i] += (ops[i][3][0][5] - ops[i][3][0][4]) * 0.003
+            after[i] += (ops[i][3][0][5] - ops[i][3][0][4]) * ops[i][3][0][3] * 0.000022
     nxt = [[] for _ in range(N)]
     for i in range(N):
         for j in deps[i]:
@@ -701,11 +752,8 @@ def plan(ops):
     for i in range(N - 1, -1, -1):
         way[i] = ops[i][7] + max([way[k] + (0.0 if st else after[i]) for k, st in nxt[i]] or [after[i]])
     best = None
-    for bias, noise, hold, seed in TRIES:
-        order, when, end = in_time(ops, deps, nxt, after, way, bias, noise, hold, seed)
-        if best is None or end < best[0]:
-            best = (end, order, when)
-    best = tighten(ops, nxt, after, best)
+    tried = [in_time(ops, deps, nxt, after, way, bias, noise, hold, seed) for bias, noise, hold, seed in TRIES]
+    best = tighten(ops, nxt, after, [x[0] for x in sorted(tried, key=lambda x: x[2])[:STARTS]])
     order, when = best[1], best[2]
     seq, num = {q: 0 for q in "vstg"}, [1] * N
     known = {q: {} for q in "vstgyx"}
@@ -799,14 +847,13 @@ def tighten(ops, nxt, after, best):
         for k, st in nxt[i]:
             pre[k].append((i, 0.0 if st else after[i]))
             post[i].append((k, 0.0 if st else after[i]))
-    start, z = pack(ops, best[1], pre), 1
-    top = None
-    for r in range(ROUNDS):
+    top, z = None, 1
+    for r in range(ROUNDS * len(best)):
+        if r % ROUNDS == 0:
+            start = pack(ops, best[r // ROUNDS], pre)
         end = max(start[i] + ops[i][7] + after[i] for i in range(N))
         if top is None or end < top[0]:
             top = (end, start)
-        elif r % 4 == 0:
-            start = top[1]
         key = []
         for i in range(N):
             z = (1103515245 * z + 12345) % 2147483648

from concourse.mybir import AluOpType as OP, AxisListType, ActivationFunctionType as AF

M, L, CAP, VI, ST = 2304, 208, 160, 3, 5
W = M + (VI - 1) * L
CW = W + L
NL, K0 = (112, 96), (0, 112)
MID = 1360
BIG = float(2 ** 30)
U = float(2 ** 18)
RC = 7.5 + 1.0 / 256
C0 = RC * 65536
NONE = -(4096.0 - MID / 4096.0)
HW = 1040.0
WHOLE = 1.5 * 2 ** 23
CYC, TCY = 0.0009, 0.00045
XV = {0: (52, 56, 52, 52, 52, 52, 60), 1: (40, 44, 36, 36, 36, 48, 52)}


def shares(h, s):
    x, n = XV[h][s], NL[h]
    k = 2 if n - x <= 64 else 3
    m = [x + (n - x) * i // k // 2 * 2 for i in range(k)] + [n]
    if MS[h] and k == 2 and 0 < MS[h] - x <= 32:
        m[1] = MS[h]
    v = [x * i // NV // 2 * 2 for i in range(NV)] + [x]
    return tuple(zip(v, v[1:])), tuple(zip(m, m[1:]))


MS, NV, CUT = (0, 0), 2, (0, 0)
QS, GS, RDS = 6, (0, 1), (1, 2, 3, 4, 5)
RS, Q0 = 12, 3
FLY = {"q": 6.0, "f": 4.0, "m": 4.2}


TRIES = [(0.8 * b, 0.3 * (s > 1), 1e-9, s) for b in range(6) for s in range(1, 4)]
STARTS, ROUNDS, NOISE, SWAPS = 8, 5, 0.03, 3000
ONV = (("X2", "X3"), ("XB", "X2", "X3"))
KS = {0: ((0, 112),), 1: ((0, 96),)}

SCRATCH = {"PT": ("sbuf", [128, W], "bfloat16"), "QA": ("sbuf", [128, VI * L], "bfloat16"), "CH": ("sbuf", [128, CW], "int32"),
           "WI": ("sbuf", [128, 1], "int32"), "THI": ("sbuf", [128, 1], "int32"), "R0I": ("sbuf", [8, VI * L], "int32"),
           "R0F": ("sbuf", [8, VI * L], "float32"), "YO": ("sbuf", [8, 2 * VI * L], "float32"),
           "YPO": ("sbuf", [8, 2 * L], "float32")}
for _h in ("0", "1"):
    SCRATCH["SG" + _h] = ("sbuf", [128, 2 * L], "float32")
    for _n in "SL":
        SCRATCH[_n + "F" + _h] = ("sbuf", [128, 16], "bfloat16")
        SCRATCH[_n + "M" + _h] = ("sbuf", [128, 32], "float32")
    SCRATCH["LQ" + _h] = ("sbuf", [128, L], "bfloat16")
    for _n in ("KEY", "ZB", "FB", "SP"):
        SCRATCH[_n + _h] = ("psum", [128, 512], "float32")
PSUMS = {n for n in SCRATCH if SCRATCH[n][0] == "psum"}
SIZES = {n: (SCRATCH[n][1], SCRATCH[n][2]) for n in SCRATCH}
POOL = {}


def _pool(big, dtype, halves, **bufs):
    at = 0
    for k in bufs:
        POOL[k] = (big, at)
        SIZES[k] = ([128, bufs[k]], dtype)
        at += (bufs[k] + 15) // 16 * 16
    for k in halves:
        for name in (k + "_0", k + "_1"):
            POOL[name] = (big, at)
            SIZES[name] = ([128, halves[k]], dtype)
            at += (halves[k] + 15) // 16 * 16
    SCRATCH[big] = ("sbuf", [128, at], dtype)


_pool("ALLb", "bfloat16", dict(XG=1536, DA=1792, DX=1792, QT=128, A0=112, A1=112, AS=144, XB=144, X2=144, X3=144, RB=136, RR=136,
                               EA=144, EB=144, EC=144, ED=144, OL=128, EE=112, DG=112, JK=4 * L),
      WZ=144, CR=288, ONB=144, SEG=144, IB=128, IN=128, I28=128, I13=128, IU=128, R1=8, R1N=8, R16=16, R16N=16,
      REP=1792, TRI=128, TRP=112, THB=128, IS0=112, IS1=112, Q16=16 * 176, QC1=2 * L, QC2=2 * L, ID1=144, SJ=128)
_pool("ALLf", "float32", dict(RD=144, RD0=144, SC2=144, FD=144, GD2=144, GD3=144, GD4=272, SC=1008, ML=128, X=144, Y0=144, Y1=144,
                              Y2=144, Y3=144, KM0=144, KM1=144, KM2=144, KM3=144, FS=272, RPF=24, DK=8, IM=8, RN=8, G23=8, FX=8,
                              LF=64, LZ=64, LS=64, NI=8, ZN=8, N=8, Z0=8, BIN=8, GG=112, NEW=112, FN=8, YPL=8, DMIN=8,
                              UU=8, YP=8, M1=8, RV=8, S1=8, S2=8),
      TD=144, MW=24, ONF=128, IF=128, WF=1, THF=1, THK=8, KK=2, KC=2, KJ=2, SM2=32, MG=L, ICOL=1, JF=9,
      G17=9, J0=9, B1=1, B2=1, J34=4)
_pool("ALLi", "int32", dict(NN=8, DI=8, RHO=8, TI=64, T6=8, N6=8, BI=8, RT=8), PI=4, RI=128, GI=9, BCI=8, RS=16)
_pool("ALLu", "uint16", dict(P16=112, LT=8, DL=8, NLT=8, DL2=8), LX=10, LE=10, L0=10, LH=4, BCL=8)
_pool("ALLh", "float16", dict(AD=144, NZ=144, NZ2=144, NZ3=144, MA=256, MB=256, GA=224, GB=224, PH=112), IDG=272, SJ1=128, SJ4=128, SJN=128, IH=112)
SENDS = ("q0", "f0", "m0", "q1", "f1", "m1")
SEMAPHORES = ["cv", "cs", "ct", "cg"] + [a + b for a in "al" for b in SENDS] + ["d%d" % i for i in range(24)]
PLAN = {}


def hop_of(src, dst, cores, topo):
    if topo.may_write(src, dst):
        return dst
    fit = [c for c in topo.cores_of(src) if c not in cores and topo.may_write(c, dst)]
    return ([c for c in fit if topo.die(c) == topo.die(src)] or fit)[0]


def some(engines):
    return sum(1 << e for e in engines[::len(engines) // 8])


def rank_program(g, core, T, topo):
    rank = T.rank_of(core)
    cores = list(T.cores)
    n = len(cores)
    if rank is None:
        for r in range(n):
            src, dst = cores[r], cores[(r + 1) % n]
            if hop_of(src, dst, cores, topo) == core:
                rid, pid = topo.addr(dst, core)
                for t in SENDS:
                    a = T["L" + t.upper()][:]
                    g.wait_ge(T.sem["a" + t], 8)
                    g.remote_dma(a, a, T.sem["a" + t], T.sem["l" + t], pid, rid, some(topo.engines(core, dst)))
                for t in SENDS:
                    g.wait_ge(T.sem["l" + t], 8)
        return

    ops, lead, ndma, turn, phase = [], [0], [0], [0], [0]
    QUE = {"v": g.vector, "s": g.scalar, "t": g.tensor, "g": g, "y": g.sync}
    SEM = {"v": T.sem.cv, "s": T.sem.cs, "t": T.sem.ct, "g": T.sem.cg}

    def A(name, c0=0, c1=None, st=1, p=(0, None)):
        shp, (b, o) = SIZES[name][0], POOL.get(name, (name, 0))
        c1 = shp[1] if c1 is None else c1
        p1 = shp[0] if p[1] is None else p[1]
        x = T[b][p[0]:p1, o + c0:o + c1:st] if st > 1 else T[b][p[0]:p1, o + c0:o + c1]
        return (x, name, p[0], p1, c0, c1, st)

    def ind(win, off):
        return ("I", win, off)

    def is_ind(x):
        return isinstance(x[0], str)

    def ap(x):
        return x[1][0].indirect(x[2][0]) if is_ind(x) else x[0]

    def size(x):
        return 16 * (x[2][5] - x[2][4]) if is_ind(x) else (x[5] - x[4] + x[6] - 1) // x[6]

    def cost(q, what, out, ins):
        m = size(out)
        if q == "v":
            if is_ind(out):
                return 0.05 + m * 3.5 * CYC
            if any(is_ind(x) for x in ins):
                return 0.05 + m * 1.5 * CYC
            if what == "tt":
                m *= 1 if any(x[1] in PSUMS for x in ins) else 2
            elif what == "red":
                m = size(ins[0])
            elif all(SIZES[x[1]][1] in ("bfloat16", "uint16", "float16") for x in [out] + list(ins)):
                m *= 0.5
            return max(64, m) * CYC
        if q == "s":
            return 0.065 + m * (1.5 if is_ind(ins[0]) else 1) * CYC
        if q == "t":
            return max(min(64, size(ins[0])), m) * TCY * (4 if SIZES[ins[0][1]][1] == "float32" else 1)
        return 0.15 + 2 * m * CYC

    def op(q, fn, rd, wr, kind="c", sem=None, val=1, c=0.1):
        R, Wr = [], []
        for x in rd:
            R += [x[1], x[2]] if is_ind(x) else [x]
        for x in wr:
            Wr.append(x[1] if is_ind(x) else x)
            if is_ind(x):
                R.append(x[2])
        ops.append((q, fn, R, Wr, kind, sem, val, c, lead[0], phase[0]))

    def call(q, what, fn, out, *ins):
        op(q, fn, ins, [out], c=cost(q, what, out, ins))

    def dma(q, out, in_, rd, wr, c=0.1):
        s = T.sem["d%d" % ndma[0]]
        ndma[0] += 1
        op(q, lambda: QUE[q].dma_start(out, in_), rd, wr, "d", s, 16, c)

    def load(q, name, src, a=0, b=None):
        dma(q, A(name, a, b)[0], src, [], [A(name, a, b)])

    def tt(out, a, b, o):
        call("v", "tt", lambda: g.vector.tensor_tensor(ap(out), ap(a), ap(b), o), out, a, b)

    def ts(out, a, s1, o0, s2=None, o1=None):
        rd = [a] + [x for x in (s1, s2) if isinstance(x, tuple)]
        v1, v2 = (ap(x) if isinstance(x, tuple) else x for x in (s1, s2))
        more = () if o1 is None else (o1,)
        op("v", lambda: g.vector.tensor_scalar(ap(out), ap(a), v1, v2, o0, *more), rd, [out], c=cost("v", "ts", out, [a]))

    def cp(out, a):
        call("v", "cp", lambda: g.vector.tensor_copy(ap(out), ap(a)), out, a)

    def fill(out, c):
        call("v", "fill", lambda: g.vector.memset(ap(out), c), out)

    def fill_all(names, c):
        b, o = POOL[names[0]]
        e = POOL[names[-1]][1] + SIZES[names[-1]][0][1]
        x = T[b][:, o:e]
        half = 0.5 if SIZES[names[0]][1] == "bfloat16" else 1
        op("v", lambda: g.vector.memset(x, c), [], [A(k) for k in names], c=max(64, (e - o) * half) * CYC)

    def scan(out, d0, d1, o0, o1):
        call("v", "scan", lambda: g.vector.tensor_tensor_scan(ap(out), ap(d0), ap(d1), 0.0, o0, o1), out, d0, d1)

    def least(out, a):
        call("v", "red", lambda: g.vector.tensor_reduce(ap(out), ap(a), AxisListType.X, OP.min, apply_absolute_value=True), out, a)

    def act(out, a, f, scale=1.0, bias=None):
        if bias is None:
            call("s", "", lambda: g.scalar.activation(ap(out), ap(a), f, scale=scale), out, a)
        elif isinstance(bias, tuple):
            call("s", "", lambda: g.scalar.activation(ap(out), ap(a), f, bias=ap(bias), scale=scale), out, a, bias)
        else:
            call("s", "", lambda: g.scalar.activation(ap(out), ap(a), f, bias=bias, scale=scale), out, a)

    def signs(out, a, bias, total):
        op("s", lambda: g.scalar.activation(ap(out), ap(a), AF.Sign, bias=bias, accum_out=ap(total)), [a], [out, total],
           c=cost("s", "", out, [a]) + 0.02)

    def mm(out, l, r, start=True, stop=True):
        call("t", "", lambda: g.tensor.matmul(ap(out), ap(l), ap(r), start, stop), out, l, r)

    def iota(out, pat, base, cm, small=False):
        kw = {"allow_small_or_imprecise_dtypes": True} if small else {}
        call("g", "", lambda: g.iota(ap(out), pat, base, cm, **kw), out)

    def asel(out, a, pat, cmp, fillv, base, cm):
        call("g", "", lambda: g.affine_select(ap(out), ap(a), pat, cmp, fillv, base, cm), out, a)

    HB = lambda nm, h, c0=0, c1=None, st=1: A(nm + "_" + str(h), c0, c1, st)
    RW = lambda nm, h, c0=0, c1=None, st=1: A(nm + "_" + str(h), c0, c1, st, (0, NL[h]))
    PS = lambda nm, h, c0, c1, st=1, r=128: A(nm + str(h), c0, c1, st, (0, r))
    EYE = lambda nm, k: A(nm, 0, k, 1, (0, k))
    FIRST = lambda nm, h, a=0, r=128: A(nm + "_" + str(h), a, a + 136, 17, (0, r))
    LAST = lambda nm, h, a=0, r=128: A(nm + "_" + str(h), a + 16, a + 136, 17, (0, r))
    both = lambda nm: [nm + "_0", nm + "_1"]

    load("y", "WI", T.w[:])
    load("s", "QA", T.q[:, 0:L], 0, L)
    load("y", "PT", T.pt[:, 16:1152], 16, 1152)
    load("s", "CH", T.ch[:, 0:80], 0, 80)
    load("s", "PT", T.pt[:, 0:16], 0, 16)
    load("s", "PT", T.pt[:, 1152:M], 1152, M)
    load("y", "R0I", T.r0[:])
    load("y", "CH", T.ch[:, 80:1200], 80, 1200)
    load("s", "CH", T.ch[:, 1200:M], 1200, M)
    load("y", "THI", T.th[:])
    load("y", "QA", T.q[:, L:VI * L], L, VI * L)

    fill_all(["WZ", "CR"], 0.0)
    fill_all(["ONB", "SEG"], 1.0)
    fill(A("ONF"), 1.0)
    iota(A("PI", 0, 1), [[0, 1]], 0, 1)
    asel(A("R1"), A("ONB", 0, 8), [[-16, 8]], OP.is_ge, 0.0, 0, 1)
    asel(A("R1"), A("R1"), [[16, 8]], OP.is_ge, 0.0, 15, -1)
    asel(A("IB"), A("ONB", 0, 128), [[-1, 128]], OP.is_equal, 0.0, 0, 1)
    iota(A("PT", M, W), [[0, W - M]], 0, 0, True)
    iota(A("JF"), [[16, 9]], 0, 0, True)
    iota(A("CR", 0, 136, 1, (0, 1)), [[0, 8], [16384, 17]], 16384 * 119, 0, True)
    iota(A("CR", 136, 272, 1, (0, 1)), [[0, 8], [-1, 17]], 1, 0, True)
    asel(A("ID1", 0, 136), A("ONB", 0, 136), [[-16, 8], [-1, 17]], OP.is_equal, 0.0, 1, 1)
    asel(A("SJ"), A("ONB", 0, 128), [[-1, 16], [-16, 8]], OP.is_equal, 0.0, 0, 1)
    iota(A("KK"), [[112, 2]], 0, 1, True)
    iota(A("J34"), [[34, 4]], 0, 0, True)
    iota(A("BCI"), [[1, 8]], 0, 0)
    iota(A("CH", M, CW), [[0, CW - M]], 0, 0)
    cp(A("WF"), A("WI"))
    ts(A("WZ", 15, 143, 16), A("R1"), A("WF"), OP.mult)
    ts(A("IN"), A("IB"), -1.0, OP.mult)
    for i in range(16):
        if i < RS:
            act(A("REP", 512 + i, 1792, 16), A("IB", 32, 112), AF.Copy)
        else:
            cp(A("REP", 512 + i, 1792, 16), A("IB", 32, 112))
    ts(A("R16", 0, 8), A("R1"), U, OP.mult)
    ts(A("R16", 8, 16), A("R1"), -16.0, OP.mult)
    ts(A("R16N"), A("R16"), -1.0, OP.mult)
    ts(A("R1N"), A("R1"), -1.0, OP.mult)
    cp(A("IF"), A("IB"))
    fill(A("SEG", 0, 136, 17), 0.0)
    fill_all(both("RD"), -BIG)
    fill_all(both("RD0"), 0.0)
    for h in (0, 1):
        ts(HB("AD", h), A("ONB"), -16.0, OP.mult)
        ts(HB("AD", h, 1, 136, 17), A("ONB", 0, 8), -HW, OP.mult)
    fill_all(both("RR"), 0.0)
    fill(A("CR", 0, 136, 1, (32, 33)), 4.0 * (MID + 256))
    fill(A("CR", 0, 136, 17, (0, 1)), -BIG * 32768)
    fill(A("CR", 136, 272, 17, (0, 1)), BIG)
    ts(A("IDG", 0, 136), A("ID1", 0, 136), 4.0, OP.mult)
    ts(A("IDG", 136, 272), A("ID1", 0, 136), -1.0 / 4096, OP.mult)
    ts(A("I28"), A("IB"), float(2 ** 28), OP.mult)
    ts(A("PI", 1, 2), A("PI", 0, 1), 15, OP.bitwise_and)
    cp(A("ICOL"), A("PI", 1, 2))
    ts(A("JF"), A("JF"), A("ICOL"), OP.add)
    ts(A("GI"), A("JF"), 1.0 / 17, OP.mult, -8.0 / 17, OP.add)
    ts(A("G17"), A("GI"), 17.0, OP.mult, 119.0, OP.min)
    ts(A("IU"), A("IB"), -U, OP.mult)
    cp(A("L0", 0, 9), A("G17"))
    ts(A("LE", 0, 9), A("G17"), 16.0, OP.add)
    tt(A("J0"), A("JF"), A("G17"), OP.is_equal)
    ts(A("J0"), A("J0"), 200.0, OP.mult, 16.0, OP.add)
    tt(A("J0"), A("J0"), A("G17"), OP.add)
    ts(A("LX", 0, 9), A("J0"), 136.0, OP.min)
    for h in (0, 1):
        fill(HB("SC", h, 144 + 136, 1008, 144), BIG)
    ts(A("I13"), A("IB"), -8192.0, OP.mult)

    def radii(t):
        cp(A("R0F", t * L, t * L + L), A("R0I", t * L, t * L + L))
        for h in (0, 1):
            a, o = t * L + K0[h], PS("FB", h, 448, 456, 1, NL[h])
            mm(o, A("R0F", a, a + NL[h]), A("IF", 0, 8, 1, (0, 8)))
            act(RW("RPF", h, 8 * t, 8 * t + 8), o, AF.Copy)
    radii(0)
    fill(A("PT", 0, 1), 256.0)
    fill(A("TD"), BIG)
    fill(A("TD", 0, 136, 17), NONE)
    for h in (0, 1):
        ts(HB("NZ", h), A("ONB"), 0.0, OP.mult)
    ts(A("SJ4"), A("SJ"), -4096.0, OP.mult)

    def later():
        even = lambda x, v: iota(x, [[0, size(x)]], v, 0, SIZES[x[1]][1] != "int32")
        for nm in ("GD2", "FD", "GD3", "GD4"):
            for h in (0, 1):
                even(HB(nm, h), 8192)
                if nm != "FD":
                    o = HB(nm, h, 0, None, 17) if nm == "GD4" else FIRST(nm, h)
                    act(o, A("ONF", 0, size(o)), AF.Copy, NONE)
        for h in (0, 1):
            even(HB("SC", h, 0, 144), int(4 * (C0 + 1)))
            for s in range(1, 5):
                even(HB("SC", h, 144 * s + 137, 144 * s + 144), 0)
            ts(HB("NZ2", h), A("ONB"), 0.0, OP.mult)
            for nm, j in (("MA", 1), ("MB", 0)):
                ts(HB(nm, h), A("CR", 0, 256), 0.0, OP.mult)
                ts(HB(nm, h, j, 256, 32), A("ONB", 0, 8), 4096.0, OP.mult)
            even(HB("BIN", h), -4096 * rank)
            even(HB("BI", h), 0)
            even(HB("ML", h), 0)
            act(HB("ML", h, 2, 128, 16), A("ONF", 0, 8), AF.Copy)
        even(A("MW"), 0)
        iota(A("RI"), [[0, 8], [1, 16]], 0, 0)
        asel(A("TRI"), A("ONB", 0, 128), [[1, 128]], OP.is_ge, 0.0, -1, -1)
        asel(A("TRI"), A("TRI"), [[1, 128]], OP.not_equal, -512.0, 0, -1)
        fill(A("TRP"), float(2 ** 25))
        asel(A("TRP"), A("TRP"), [[1, 112]], OP.is_ge, 0.0, 0, -1)
        for c, j, v in ((0, 0, 1.0), (8, 2, 4096.0), (16, 1, 1.0)):
            asel(A("MW", c, c + 8), A("MW", c, c + 8), [[-16, 8]], OP.not_equal, v, -j, 1)
        iota(A("KC"), [[112, 2]], L, 1, True)
        iota(A("KJ"), [[112, 2]], W - MID, 1, True)
        ts(A("PI", 2, 3), A("PI", 0, 1), 7, OP.bitwise_and)
        ts(A("PI", 3, 4), A("PI", 0, 1), 3, OP.logical_shift_right, 1, OP.bitwise_and)
        ts(A("B1"), A("PI", 2, 3), 5.0, OP.min, 144.0, OP.mult)
        ts(A("B2"), A("PI", 3, 4), 17.0, OP.mult, 16.0, OP.add)
        ts(A("LH"), A("J34"), A("B1"), OP.add, A("B2"), OP.add)
        cp(A("BCL"), A("BCI"))
        cp(A("SJ1"), A("SJ"))
        cp(A("IH"), A("IB", 0, 112))
        ts(A("SJN"), A("SJ"), -1.0, OP.mult)
        for t in (0, 1):
            ts(HB("DG", t), A("IB", 0, 112), A("KK", t, t + 1), OP.mult)
            ts(A("IS%d" % t), A("IB", 0, 112), float(M + t * L), OP.mult)
            ts(HB("NZ3", t), A("ONB"), 0.0, OP.mult)
            for nm in ("SG", "SM", "SF"):
                even(A(nm + str(t)), 0)
            even(A("QC%d" % (t + 1), L, 2 * L), 0)
            act(A("QC%d" % (t + 1), 0, L), A("QA", (t + 1) * L, (t + 2) * L), AF.Copy)
            radii(t + 1)
        cp(A("THF"), A("THI"))
        ts(A("THB"), A("ONB", 0, 128), A("THF"), OP.mult)
        mm(PS("ZB", 1, 456, 464), A("THB"), A("R1"))
        ts(A("THK"), PS("ZB", 1, 456, 464), U / 16, OP.mult, RC * U, OP.add)

    def to_list(out, h, nz, sj, more, bank="FB"):
        k = NL[h] // 16
        o = PS(bank, h, 288, 288 + k)
        for j in range(16):
            mm(o, RW(nz, h, 15 - j, 143 - j), A(sj, 8 * j, 8 * j + k, 1, (0, NL[h])), j == 0, j == 15)
        ts(HB(out, h, 0, k), o, more, OP.add)

    def kids(h, top=CW):
        for a, b in ((CUT[h], NL[h] // 16), (0, CUT[h])):
            if b > a:
                cp(HB("P16", h, 16 * a, 16 * b), ind(A("CH", 0, top), HB("LT", h, a, b)))
        ts(HB("PH", h, 0, NL[h]), HB("P16", h, 0, NL[h]), float(MID), OP.subtract)

    def outside(h, out, lev, c, root=False):
        if out in ONV[h] or root:
            tt(HB(out, h), ind(HB("RD0" if root else "RD", h, 0, 136), A("L0", 0, 9)), HB("Y%d" % lev, h), OP.is_lt)
            return
        out = HB(out, h, 0, 136)
        o = PS("ZB", h, 136 * c, 136 * c + 136)
        mm(o, A("IU"), HB("RB", h), True, False)
        mm(o, A("IF"), HB("Y%d" % lev, h, 0, 136), False, True)
        act(out, o, AF.Relu, 2.0 / U, -16.0)

    def masks(h, lev):
        if lev and ("XB" not in ONV[h] or (lev in FBS and "X2" not in ONV[h]) or (lev == 4 and "X3" not in ONV[h])):
            scan(HB("RB", h), A("SEG", 0, 136), HB("RR", h, 0, 136), OP.mult, OP.add)
        scan(HB("AS", h), A("SEG"), HB("AD", h), OP.mult, OP.add)
        act(HB("Y%d" % min(lev, 3), h), HB("AS", h), AF.Abs, U, -7.5 * U)
        outside(h, "XB", min(lev, 3), 0, lev == 0)

    def points(h, s):
        vs, ss = shares(h, s)
        for c, (a, b) in enumerate(ss):
            w = 16 * (b - a)
            x, o = HB("XG", h, 512 * c, 512 * c + w), A(("SP0", "SP1", "ZB%d" % h)[c], 0, w)
            act(x, ind(A("PT"), HB("P16", h, a, b)), AF.Copy)
            mm(o, RW("QT", h), A("REP", 16 * a, 16 * b, 1, (0, NL[h])), True, False)
            mm(o, A("IB"), x, False, True)
            act(HB("DA", h, 16 * a, 16 * b), o, AF.Abs)
        for a, b in vs:
            d, z = HB("DX", h, 16 * a, 16 * b), K0[h]
            tt(d, ind(A("PT"), HB("P16", h, a, b)), A("Q16", 16 * (z + a), 16 * (z + b)), OP.subtract)
            ts(HB("DA", h, 16 * a, 16 * b), d, 0.0, OP.max, 2.0, OP.mult)

    def keys(h, s):
        nl, a, b = NL[h], 0, XV[h][s]
        mm(PS("KEY", h, 0, 280, 1, nl), A("ONB", 0, nl, 1, (0, 33)), A("CR", 0, 280, 1, (0, 33)), True, False)
        mm(PS("KEY", h, 0, 272, 1, nl), HB("PH", h, 0, nl), A("IDG"), False, False)
        for i in range(16):
            mm(A("KEY%d" % h, i + 1, 272, 17, (a, b)), HB("DX", h, 16 * a + i, 16 * b, 16), A("R16N"), False, False)
        mm(PS("KEY", h, 0, 136, 1, nl), EYE("I28", nl), RW("XB", h, 0, 136), False, False)
        for a, b in KS[h]:
            for i in range(16):
                mm(A("KEY%d" % h, i + 1, 272, 17, (a, b)), HB("DA", h, 16 * a + i, 16 * b, 16), A("R16"), False, i == 15)

    FBS = {2: [(0, "X2", ("EA",))], 3: [(1, "X2", ("EB",))], 4: [(2, "X2", ("EC",)), (0, "X3", ("EA", "ED"))]}

    def look(h, s):
        a = 144 * s
        scan(HB("SC", h, a, a + 136), PS("KEY", h, 0, 136), HB("RD", h, 0, 136), OP.min, OP.max)
        if s == ST + 1:
            return
        km = "KM%d" % min(s - 1, 3)
        tt(HB("X", h), ind(HB("SC", h, a, a + 137), A("LX", 0, 9)), HB("Y%d" % min(s - 1, 3), h), OP.subtract)
        tt(HB(km, h), PS("KEY", h, 136, 280), HB("X", h), OP.min)
        scan(HB("SC2", h, 0, 136), HB(km, h, 0, 136), HB("FD", h, 0, 136) if s >= 3 else A("TD", 0, 136), OP.max, OP.min)
        ts(HB("NN", h), LAST("SC2", h), -1.0, OP.mult)
        tt(HB("NZ", h, 15, 143, 16), LAST("SC2", h), HB("NN", h), OP.add)
        to_list("LT", h, "NZ", "SJ4", float(MID))
        kids(h)
        phase[0] += 3
        if s in RDS:
            act(HB("RV", h), LAST("SC", h, a), AF.Identity, 1.0 / U, WHOLE - 8.0)
            act(FIRST("RR", h), HB("RV", h), AF.Identity, 1.0, -WHOLE)
            act(FIRST("RD", h), FIRST("RR", h), AF.Identity, U, RC * U)
        else:
            ts(HB("RHO", h), LAST("SC", h, a), 1.0 / U, OP.mult, -8.0, OP.add)
            ts(FIRST("RD", h), HB("RHO", h), RC, OP.add, U, OP.mult)
            if len(ONV[h]) < 3:
                act(FIRST("RR", h), FIRST("RD", h), AF.Identity, 1.0 / U, -RC)
        ts(FIRST("AD", h), LAST("SC2", h), -1.0 / 16, OP.mult, HW - 0.47, OP.add)
        masks(h, s)
        sel = ind(HB("SC2", h, 0, 136), A("LE", 0, 9))
        if s <= 3:
            tt(HB({1: "EA", 2: "EB", 3: "EC"}[s], h), sel, HB(km, h), OP.is_equal)
        if s == 3:
            tt(HB("ED", h), sel, HB("KM0", h), OP.is_equal)
        if s not in FBS:
            return
        gd = "GD%d" % s
        ts(LAST(gd, h), LAST("SC2", h), -64.0, OP.mult, -256000.0, OP.add)
        if s == 4:
            tt(HB("G23", h), LAST("GD2", h), LAST("GD3", h), OP.max)
            tt(LAST(gd, h, 136), HB("G23", h), LAST(gd, h), OP.min)
        for c, (l, x, es) in enumerate(FBS[s]):
            outside(h, x, l, c + 1)
            o = PS("FB", h, 136 * c, 136 * c + 136)
            mm(o, A("IF"), HB("KM%d" % l, h, 0, 136), True, False)
            for e in es + (x,):
                mm(o, A("I13"), HB(e, h, 0, 136), False, e == x)
        w = 136 * len(FBS[s])
        scan(HB("FS", h, 0, w), PS("FB", h, 0, w), HB(gd, h, 0, w), OP.max, OP.min)
        if s == 4:
            tt(HB("FX", h), LAST("FS", h), LAST("FS", h, 136), OP.max)
        ts(FIRST("FD", h), HB("FX", h) if s == 4 else LAST("FS", h), NONE, OP.max)

    hop = hop_of(core, cores[(rank + 1) % n], cores, topo)
    rid, pid = topo.addr(hop, core)
    sent = {}

    def send(x, t, s):
        d, ra, rl = A("L%s%d" % (x.upper(), t)), T.sem["a%s%d" % (x, t)], T.sem["l%s%d" % (x, t)]
        sent[x] = (len(ops), FLY[x])
        op("g", lambda: g.remote_dma(d[0], s[0], ra, rl, pid, rid, some(topo.engines(core, hop))), [s], [], "r", rl, 8, 1.0)

    QN = ("QA", "QC1", "QC2")
    nh = (112, CAP - 112)
    for t in range(VI):
        q = lambda a, b, st=1: A(QN[t], a, b, st)
        qh = lambda h: q(K0[h], K0[h] + NL[h])
        phase[0] = 100 * t
        if t:
            lq, lf, lm, sg = (x + str(t - 1) for x in ("LQ", "LF", "LM", "SG"))
            for x in "qfm":
                op("x", sent[x], [], [A("L%s%d" % (x.upper(), t - 1))], "x", T.sem["a%s%d" % (x, t - 1)], 8)
            far = lambda h: A(lf, 8 * h, 8 * h + 8, 1, (0, NL[h]))
            for h in (0, 1):
                nl = NL[h]
                o = PS("ZB", h, 304, 312, 1, nl)
                mm(o, EYE("TRI", nl), far(h), True, h == 0)
                if h:
                    mm(o, A("ONB", 0, nl, 1, (0, NL[0])), far(0), False, True)
                ts(RW("NZ3", h, 15, 143, 16), o, 512.0, OP.add, A("KC", h, h + 1, 1, (0, nl)), OP.min)
                to_list("DL", h, "NZ3", "SJ1", 0.0, "ZB")
                cp(ind(q(0, 2 * L), HB("DL", h, 0, nl // 16)), A(lq, K0[h], K0[h] + nl))
            cp(q(CAP, L), A("QA", t * L + CAP, t * L + L))
        if t < VI - 1:
            send("q", t, q(0, L))
        hi = K0[1] + max(XV[1])
        for i in range(16):
            if i < (QS if t else Q0):
                act(A("Q16", i, 16 * hi, 16), q(0, hi), AF.Copy)
            else:
                cp(A("Q16", i, 16 * hi, 16), q(0, hi))
        o = PS("ZB", 0, 288, 301)
        for j in range(16):
            mm(o, A("WZ", 15 - j, 143 - j), q(j, L, 16), j == 0, j == 15)
        cp(A("RS", 0, 13), o)
        ts(A("RS", 0, 13), A("RS", 0, 13), 63, OP.bitwise_and)
        if t:
            for h in (0, 1):
                nl = NL[h]
                for j in (0, 1):
                    act(RW("ML", h, j, 128, 16), A(lm, 16 * h + 8 * j, 16 * h + 8 * j + 8, 1, (0, nl)), AF.Identity, 1.0,
                        4096.0 * ((rank - 1) % n) * j)
                o = PS("SP", h, 0, nl)
                mm(o, RW("ML", h), EYE("IF", nl))
                act(A("MG", K0[h], K0[h] + nl), o, AF.Copy)
                cp(ind(A(sg), HB("DL", h, 0, nl // 16)), A("MG", K0[h], K0[h] + nl))
        for h in (0, 1):
            lead[0] = 1 - h
            nl = NL[h]
            ts(HB("LT", h, 0, nl // 16), A("RS", 7 * h, 7 * h + nl // 16), 1.0, OP.add)
            o = PS("ZB", h, 0, 128, 1, nl)
            mm(o, qh(h), A("IN"))
            act(RW("QT", h), o, AF.Copy)
            kids(h, 80)
            a0, a1 = HB("A0", h, 0, nl), HB("A1", h, 0, nl)
            tt(a0, ind(A("PT", 0, 80), HB("LT", h, 0, nl // 16)), qh(h), OP.subtract)
            ts(a1, a0, 0.0, OP.max, 2.0, OP.mult)
            d0, s0 = PS("ZB", h, 128, 136, 1, nl), PS("ZB", h, 136, 144, 1, nl)
            mm(s0, qh(h), A("WZ", 15, 143, 16))
            mm(d0, a0, A("R1N"), True, False)
            mm(d0, a1, A("R1"), False, True)
            ts(FIRST("AD", h, 0, nl), d0, HW, OP.add)
            cp(RW("RT", h), s0)
            rpf = lambda r: A("RPF_%d" % h, 8 * t, 8 * t + 8, 1, (0, r))
            if nh[h] < nl or not t:
                act(FIRST("RR", h, 0, nl), rpf(nl), AF.Copy)
            if t:
                r = nh[h]
                mm(PS("ZB", h, 144, 168, 1, r), A(sg, K0[h], K0[h] + r), A("MW"))
                m1, came = A("M1_%d" % h, 0, 8, 1, (0, r)), lambda c: PS("ZB", h, 144 + c, 152 + c, 1, r)
                tt(m1, rpf(r), came(8), OP.subtract)
                tt(FIRST("RR", h, 0, r), came(0), m1, OP.max)
                act(A("BIN_%d" % h, 0, 8, 1, (0, r)), came(16), AF.Identity, 1.0, -4096.0 * rank)
            act(FIRST("RD0", h, 0, nl), FIRST("RR", h, 0, nl), AF.Identity, U, RC * U)
            tt(RW("IM", h), d0, FIRST("RR", h, 0, nl), OP.is_lt)
            tt(RW("DK", h), d0, FIRST("RR", h, 0, nl), OP.min)
            masks(h, 0)
            act(FIRST("RD", h, 0, nl), RW("DK", h), AF.Identity, U, RC * U)
            ts(RW("RT", h), RW("RT", h), 63, OP.bitwise_and)
            ts(RW("RN", h), RW("RT", h), 1.0, OP.add)
        for h in (0, 1):
            lead[0] = 1 - h
            phase[0] = 100 * t + 2 * h + 3
            mm(PS("KEY", h, 0, 280), A("ONB", 0, 128, 1, (0, 33)), A("CR", 0, 280, 1, (0, 33)))
            points(h, 0 if t else 6)
            keys(h, 0 if t else 6)
        if t == 0:
            lead[0], phase[0] = -10, 9.5
            later()
        for s in range(1, ST + 1):
            for h in (0, 1):
                lead[0] = 1 - h
                phase[0] = 100 * t + 4 * s + 2 * h
                look(h, s)
                points(h, s)
                keys(h, s)
        last = t == VI - 1
        for h in (0, 1):
            lead[0] = 1 - h
            nl = NL[h]
            phase[0] = 100 * t + 24 + 2 * h
            ts(HB("TI", h), ind(HB("SC", h, 0, 144 * 5 + 136), A("LH")), 0.25, OP.mult, -C0, OP.add)
            ts(HB("TI", h), HB("TI", h), 4095, OP.bitwise_and)
            ts(RW("LZ", h), RW("TI", h), 0, OP.is_equal)
            cp(RW("LF", h), RW("TI", h))
            tt(RW("LF", h, 0, 64, 8), RW("RN", h), RW("IM", h), OP.mult)
            scan(RW("LS", h), RW("LZ", h), RW("LF", h), OP.mult, OP.add)
            prev = RW("LS", h, 5, 64, 8)
            ts(RW("Z0", h), prev, 0.0, OP.is_equal)
            tt(RW("Z0", h), RW("Z0", h), RW("BIN", h), OP.mult)
            tt(RW("Z0", h), RW("Z0", h), prev, OP.add)
            look(h, ST + 1)
            t6 = LAST("SC", h, 144 * 6, nl)
            far = lambda h: A("SF%d" % t, 8 * h, 8 * h + 8, 1, (0, NL[h]))
            if not last:
                tt(far(h), t6, A("THK", 0, 8, 1, (0, nl)), OP.is_ge)
            ts(RW("T6", h), t6, 0.25, OP.mult, -C0, OP.add)
            tt(RW("NI", h), t6, FIRST("RD", h, 0, nl), OP.is_ge)
            ts(RW("N6", h), RW("T6", h), 4095, OP.bitwise_and)
            if not last:
                tt(RW("ZN", h), RW("NI", h), prev, OP.mult)
                tt(RW("N", h), RW("ZN", h), RW("N6", h), OP.add)
                ts(RW("NZ", h, 15, 143, 16), RW("N", h), float(MID), OP.subtract)
                to_list("NLT", h, "NZ", "SJ1", float(MID))
                cp(HB("GG", h, 0, nl), ind(A("CH"), HB("NLT", h, 0, nl // 16)))
            sm = lambda j: A("SM%d" % t, 16 * h + 8 * j, 16 * h + 8 * j + 8, 1, (0, nl))
            act(RW("RV", h), t6, AF.Identity, 1.0 / U, WHOLE - 8.0)
            act(sm(0), RW("RV", h), AF.Identity, 1.0, -WHOLE)
            tt(RW("Z0", h), RW("Z0", h), RW("NI", h), OP.mult)
            tt(sm(1), RW("Z0", h), RW("N6", h), OP.add)
            for j in (0, 1):
                o = PS(("ZB", "KEY")[j], h, 384, 384 + nl, 1, 8)
                a = (j * VI + t) * L + K0[h]
                mm(o, sm(j), EYE("IF", nl))
                act(A("YO", a, a + nl), o, AF.Identity, 1.0, 4096.0 * rank * j)
        lead[0] = 0
        for j, y in ((0, T.yr), (1, T.yb)):
            yo = A("YO", (j * VI + t) * L, (j * VI + t + 1) * L)
            dma("y", y[:, t * L:t * L + L], yo[0], [yo], [])
        if last:
            break
        send("f", t, A("SF%d" % t))
        send("m", t, A("SM%d" % t))
        cp(A("PT", M + t * L, M + t * L + L), q(0, L))
        for h in (0, 1):
            lead[0] = 1 - h
            nl, k0 = NL[h], K0[h]
            ts(RW("BI", h), RW("T6", h), 20, OP.logical_shift_right)
            tt(HB("OL", h), ind(HB("BI", h), A("BCL")), A("RI"), OP.is_equal)
            ob, bn = PS("KEY", h, 0, nl), PS("KEY", h, 128, 128 + nl)
            mm(ob, RW("OL", h), EYE("IB", nl))
            mm(bn, RW("OL", h), RW("DG", h, 0, nl), True, False)
            mm(bn, RW("OL", h), EYE("IS%d" % t, nl), False, True)
            def turned(out, src, z, a):
                for u in (0, 1):
                    mm(PS(z, h, a + u * nl, a + u * nl + nl), RW(src, h, 128 * u, 128 * u + 128), EYE("IH", nl))
                cp(HB(out, h, 0, 2 * nl), PS(z, h, a, a + 2 * nl))
            ts(RW("MA", h, 0, 256, 32), RW("N", h), float(MID), OP.subtract)
            turned("GA", "MA", "FB", 0)
            tt(RW("FN", h), far(h), RW("N", h), OP.mult)
            tt(HB("EE", h, 0, nl), HB("GG", h, 0, nl), ob, OP.is_lt)
            tt(HB("NEW", h, 0, nl), HB("GG", h, 0, nl), bn, OP.add)
            can = PS("KEY", h, 256, 264, 1, nl)
            mm(can, HB("EE", h, 0, nl), A("R1"))
            tt(RW("YPL", h), can, RW("FN", h), OP.mult)
            ts(RW("MB", h, 1, 256, 32), RW("YPL", h), -1.0, OP.mult, float(MID), OP.add)
            turned("GB", "MB", "KEY", 272)
            banks = ("SP0", "SP1", "FB%d" % h, "KEY%d" % h)
            w = k0 + nl
            for z, bank in enumerate(banks):
                for gr in (z, z + 4):
                    r, a = gr % 4 * 32, gr // 4 * w
                    side = lambda nm, e: A("%s_%d" % (nm, e), gr // 4 * NL[e], (gr // 4 + 1) * NL[e], 1, (r, r + 2))
                    if h:
                        mm(A(bank, a, a + k0, 1, (0, nl)), side("GA", h), side("GB", 0))
                    o = A(bank, a + k0, a + w, 1, (0, nl))
                    mm(o, EYE("IB", nl), A("TRP", 0, nl, 1, (0, nl)), True, False)
                    mm(o, side("GA", h), side("GB", h), False, True)
                for gr in (z, z + 4):
                    o = A(bank, gr // 4 * w, gr // 4 * w + w, 1, (0, nl))
                    if z < GS[h]:
                        for j, b in ((1, 0.5), (2, -0.5)):
                            c = (gr // 4 * 2 + j - 1) * L
                            signs(RW("JK", h, c, c + w), o, b, RW("S%d" % j, h, gr, gr + 1))
                    else:
                        least(RW("DMIN", h, gr, gr + 1), o)
            if GS[h]:
                tt(RW("S1", h, 0, 8, 4), RW("S1", h, 0, 8, 4), RW("S2", h, 0, 8, 4), OP.is_equal)
                ts(RW("DMIN", h, 0, 8, 4), RW("S1", h, 0, 8, 4), 4096.0, OP.mult)
            tt(RW("YP", h), RW("DMIN", h), RW("YPL", h), OP.min)
            ts(RW("UU", h), RW("YP", h), 4096.0, OP.mult, A("KJ", h, h + 1, 1, (0, nl)), OP.subtract)
            tt(RW("NZ2", h, 15, 143, 16), RW("UU", h), RW("MB", h, 1, 256, 32), OP.min)
            to_list("DL2", h, "NZ2", "SJN", float(MID))
        for h in (0, 1):
            lead[0] = 1 - h
            nl = NL[h]
            cp(ind(A("CH"), HB("DL2", h, 0, nl // 16)), HB("NEW", h, 0, nl))
            o = PS("FB", h, 320, 320 + nl, 1, 8)
            mm(o, RW("YP", h), EYE("IF", nl))
            act(A("YPO", t * L + K0[h], t * L + K0[h] + nl), o, AF.Copy)
        lead[0] = 0
        yo = A("YPO", t * L, t * L + L)
        dma("y", T.yp[:, t * L:t * L + L], yo[0], [yo], [])

    if not PLAN:
        PLAN.update(plan(ops))
    emit(g, ops, QUE, SEM)


def plan(ops):
    def meets(a, b):
        if a[2] >= b[3] or b[2] >= a[3] or a[4] >= b[5] or b[4] >= a[5]:
            return False
        return not (a[6] == b[6] and a[6] > 1 and (a[4] - b[4]) % a[6] != 0)

    N = len(ops)
    tag = [o[0] if o[4] == "c" else "a%d" % i for i, o in enumerate(ops)]
    in_line = lambda i, j: tag[i] == tag[j] == "t" or tag[i][:5] == tag[j][:5] in ("loady", "loads", "loadg")
    hist, deps, sent, pool, loads, fly = {}, [], [], [], {}, {}
    for i in range(N):
        R, Wr, kind, dep = ops[i][2], ops[i][3], ops[i][4], set()
        for lst, w in ((R, False), (Wr, True)):
            for r in lst:
                ps = r[1] in PSUMS
                for (j, rr, ww) in hist.get(r[1], []):
                    if j != i and ((ps and (tag[j] != tag[i] or w or ww)) or ((w or ww) and meets(r, rr))):
                        dep.add(j)
        if tag[i] == "g":
            dep.update(pool[-1:])
            pool.append(i)
        if kind == "x":
            dep.add(ops[i][1][0])
            fly[ops[i][1][0]] = ops[i][1][1]
        if kind == "r":
            tag[i] = "loadg" + tag[i]
            dep.update(sent[-1:])
            sent.append(i)
        if kind == "d" and Wr:
            tag[i] = "load" + ops[i][0] + tag[i]
            dep.update(loads.get(ops[i][0], []))
            loads[ops[i][0]] = [i]
        deps.append(dep)
        for lst, w in ((R, False), (Wr, True)):
            for r in lst:
                h = hist.setdefault(r[1], [])
                if w and r[1] in PSUMS:
                    h[:] = []
                elif w and r[6] == 1:
                    h[:] = [e for e in h if not (r[2] <= e[1][2] and e[1][3] <= r[3] and r[4] <= e[1][4] and e[1][5] <= r[5])]
                elif w:
                    h[:] = [e for e in h if e[1][1:] != r[1:]]
                h.append((i, r, w))
    after = [{"c": 0.23, "d": 2.2, "r": 5.0, "x": 0.1}[o[4]] for o in ops]
    for i in range(N):
        after[i] = fly.get(i, after[i])
        if ops[i][4] == "d" and ops[i][3]:
            after[i] += (ops[i][3][0][5] - ops[i][3][0][4]) * ops[i][3][0][3] * 0.000022
    nxt = [[] for _ in range(N)]
    for i in range(N):
        for j in deps[i]:
            nxt[j].append((i, in_line(i, j)))
    way = [0.0] * N
    for i in range(N - 1, -1, -1):
        way[i] = ops[i][7] + max([way[k] + (0.0 if st else after[i]) for k, st in nxt[i]] or [after[i]])
    best = None
    tried = [in_time(ops, deps, nxt, after, way, bias, noise, hold, seed) for bias, noise, hold, seed in TRIES]
    best = tighten(ops, nxt, after, [x[0] for x in sorted(tried, key=lambda x: x[2])[:STARTS]])
    order, when = best[1], best[2]
    seq, num = {q: 0 for q in "vstg"}, [1] * N
    known = {q: {} for q in "vstgyx"}
    snap, need, waits = [None] * N, set(), [None] * N
    for i in order:
        q = ops[i][0]
        if ops[i][4] == "c":
            seq[q] += 1
            num[i] = seq[q]
        k, mine, last = known[q], [], {}
        for j in deps[i]:
            if ops[i][4] == "x" or in_line(i, j):
                continue
            if tag[j] not in last or num[last[tag[j]]] < num[j]:
                last[tag[j]] = j
        for j in sorted(last.values(), key=lambda j: -when[j]):
            if k.get(tag[j], 0) >= num[j]:
                continue
            mine.append(j)
            need.add(j)
            for a, b in snap[j].items():
                if k.get(a, 0) < b:
                    k[a] = b
        waits[i] = mine
        snap[i] = dict(k)
        snap[i][tag[i]] = num[i]
    return {"order": order, "waits": waits, "need": need, "end": best[0]}


def in_time(ops, deps, nxt, after, way, bias, noise, hold, seed):
    N = len(ops)
    left = [len(d) for d in deps]
    when = [0.0] * N
    free = {q: 0.0 for q in "vstgyx"}
    ready = {q: [i for i in range(N) if ops[i][0] == q and left[i] == 0] for q in free}
    z, pr = seed, []
    for i in range(N):
        z = (1103515245 * z + 12345) % 2147483648
        pr.append(way[i] + bias * ops[i][8] + noise * z / 2147483648.0)
    order = []
    while len(order) < N:
        best = None
        for q in free:
            if ready[q]:
                t = max(free[q], min(when[i] for i in ready[q]))
                if best is None or t < best[0]:
                    best = (t, q)
        t, q = best
        i = max((i for i in ready[q] if when[i] <= t + hold), key=lambda k: (pr[k], -k))
        ready[q].remove(i)
        free[q] = max(t, when[i]) + ops[i][7]
        end = free[q] + after[i]
        order.append(i)
        for k, st in nxt[i]:
            left[k] -= 1
            when[k] = max(when[k], free[q] if st else end)
            if left[k] == 0:
                ready[ops[k][0]].append(k)
    return order, when, max(free.values())


def pack(ops, order, pre):
    start, begin, ends = [0.0] * len(ops), {q: [] for q in "vstgyx"}, {q: [] for q in "vstgyx"}
    for i in order:
        c, t = ops[i][7], 0.0
        for j, gap in pre[i]:
            u = start[j] + ops[j][7] + gap
            if u > t:
                t = u
        b, e = begin[ops[i][0]], ends[ops[i][0]]
        lo, hi = 0, len(e)
        while lo < hi:
            mid = (lo + hi) // 2
            if e[mid] > t:
                hi = mid
            else:
                lo = mid + 1
        while lo < len(b) and b[lo] < t + c - 1e-9:
            t = e[lo]
            lo += 1
        b.insert(lo, t)
        e.insert(lo, t + c)
        start[i] = t
    return start


def tighten(ops, nxt, after, best):
    N = len(ops)
    pre, post = [[] for _ in range(N)], [[] for _ in range(N)]
    for i in range(N):
        for k, st in nxt[i]:
            pre[k].append((i, 0.0 if st else after[i]))
            post[i].append((k, 0.0 if st else after[i]))
    top, z = None, 1
    for r in range(ROUNDS * len(best)):
        if r % ROUNDS == 0:
            start = pack(ops, best[r // ROUNDS], pre)
        end = max(start[i] + ops[i][7] + after[i] for i in range(N))
        if top is None or end < top[0]:
            top = (end, start)
        key = []
        for i in range(N):
            z = (1103515245 * z + 12345) % 2147483648
            key.append(start[i] + ops[i][7] + NOISE * z / 2147483648.0)
        for i in range(N):
            for j, gap in pre[i]:
                if key[i] <= key[j]:
                    key[i] = key[j] + 1e-6
        back = pack(ops, sorted(range(N), key=lambda i: -key[i]), post)
        start = pack(ops, sorted(range(N), key=lambda i: -back[i] - ops[i][7]), pre)
    end, start = polish(ops, pre, post, after, top[1])
    return end, sorted(range(N), key=lambda i: start[i]), start


def polish(ops, pre, post, after, start):
    N = len(ops)
    c = [o[7] for o in ops]
    before, behind, tail_of = [-1] * N, [-1] * N, {}
    for i in sorted(range(N), key=lambda i: start[i]):
        j = tail_of.get(ops[i][0], -1)
        before[i] = j
        if j >= 0:
            behind[j] = i
        tail_of[ops[i][0]] = i
    ps = [set(j for j, g in pre[i]) for i in range(N)]
    best, z = None, 1
    for r in range(SWAPS):
        left = [len(pre[i]) + (before[i] >= 0) for i in range(N)]
        head = [0.0] * N
        order = [i for i in range(N) if not left[i]]
        for i in order:
            e = head[i] + c[i]
            for k, g in post[i] + ([(behind[i], 0.0)] if behind[i] >= 0 else []):
                if head[k] < e + g:
                    head[k] = e + g
                left[k] -= 1
                if not left[k]:
                    order.append(k)
        if len(order) < N:
            before, behind = list(best[2]), list(best[3])
            continue
        tail = [0.0] * N
        for i in reversed(order):
            t = after[i]
            for k, g in post[i]:
                if t < g + tail[k]:
                    t = g + tail[k]
            k = behind[i]
            if k >= 0 and t < tail[k]:
                t = tail[k]
            tail[i] = t + c[i]
        end = max(tail)
        if best is None or end < best[0] - 1e-9:
            best = (end, head, list(before), list(behind))
        elif end > best[0] + 0.8:
            before, behind = list(best[2]), list(best[3])
            continue
        last = -9.0
        for v in sorted((i for i in range(N) if head[i] + tail[i] > end - 1e-6), key=lambda i: head[i]):
            u = before[v]
            if u < 0 or u in ps[v] or head[u] + c[u] < head[v] - 1e-9 or head[u] < last:
                continue
            a, b = before[u], behind[v]
            hv = max([head[j] + c[j] + g for j, g in pre[v]] + [head[a] + c[a] if a >= 0 else 0.0])
            if hv > head[u] + c[u] - 1e-9:
                continue
            hu = max(head[u], hv + c[v])
            tu = c[u] + max([g + tail[k] for k, g in post[u]] + [tail[b] if b >= 0 else 0.0, after[u]])
            tv = c[v] + max([g + tail[k] for k, g in post[v]] + [tu, after[v]])
            z = (1103515245 * z + 12345) % 2147483648
            if max(hv + tv, hu + tu) > end + (0.1 if z % 1024 < 60 else -1e-6) or z % 4096 < 1000:
                continue
            if a >= 0:
                behind[a] = v
            if b >= 0:
                before[b] = u
            before[v], behind[v], before[u], behind[u] = a, u, v, b
            last = head[v] + 1.0
    return best[0], best[1]


def emit(g, ops, QUE, SEM):
    cnt, at = {q: 0 for q in "vstg"}, {}
    for i in PLAN["order"]:
        q, fn, R, Wr, kind, sem, val = ops[i][:7]
        if kind == "x":
            continue
        for j in PLAN["waits"][i]:
            s, v = at[j] if j in at else (ops[j][5], ops[j][6])
            QUE[q].wait_ge(s, v)
        inst = fn()
        if kind == "d":
            inst.then_inc(sem, val)
        elif kind == "c" and i in PLAN["need"]:
            cnt[q] += 1
            inst.then_inc(SEM[q], 1)
            at[i] = (SEM[q], cnt[q])
    for q in cnt:
        if cnt[q]:
            g.wait_ge(SEM[q], cnt[q])
    for o in ops:
        if o[4] in ("d", "r", "x"):
            g.wait_ge(o[5], o[6])
